import numpy as np
import ml_dtypes


def mxq(x, axis, fmt="e4m3"):
    dtype, down = {"e4m3": (ml_dtypes.float8_e4m3fn, 7), "e5m2": (ml_dtypes.float8_e5m2, 14)}[fmt]
    v = np.moveaxis(np.asarray(x, np.float32).astype(ml_dtypes.bfloat16).astype(np.float64), axis, -1)
    blocks = v.reshape(v.shape[:-1] + (-1, 32))
    amax = np.abs(blocks).max(-1, keepdims=True)
    byte = np.maximum(np.where(amax > 0, np.frexp(amax)[1] - 1 + 127, 0) - down, 1)
    scale = np.exp2(byte - 127.0)
    codes = (blocks / scale).astype(np.float32).astype(dtype).astype(np.float64)
    return np.moveaxis((codes * scale).reshape(v.shape), -1, axis)


WIDE = False


def mx_kscale(k):
    if not WIDE:
        return np.ones(k)
    levels = np.array([10, -10, 5, -5, 0])
    if k % 512:
        return np.exp2(np.random.permutation(np.resize(levels, k // 32))).repeat(32)
    a = np.empty((k // 512, 16))
    for p in range(k // 512):
        a[p, :8] = np.random.permutation(np.resize(levels, 8))
        for g in range(8):
            far = levels[np.abs(levels - a[p, g]) >= 10]
            a[p, g + 8] = far[np.random.randint(len(far))]
    return np.exp2(a.ravel()).repeat(32)


def f64(x):
    return np.asarray(x).astype(np.float64)


def striped(idx):
    return np.tile(idx.reshape(-1, 16).T, (8, 1)).astype(np.uint16)


def unstriped(offs):
    return offs[:16].T.reshape(-1).astype(np.int64)


def pack_weight(w):
    k, n = w.shape
    w = f64(np.asarray(w, np.float32).astype(ml_dtypes.bfloat16)).reshape(k // 32, 32, n)
    amax = np.abs(w).max(1)
    byte = np.clip(np.where(amax > 0, np.frexp(amax)[1] - 1 + 127 - 7, 1), 1, 254)
    scaled = (w * np.exp2(127.0 - byte)[:, None, :]).reshape(k, n).astype(np.float32)
    words = np.ascontiguousarray(scaled.reshape(k // 512, 128, 4, n).transpose(0, 1, 3, 2)).astype(ml_dtypes.float8_e4m3fn).view(np.uint8)
    return words, np.ascontiguousarray(byte.astype(np.uint8).reshape(k // 512, 16, n))


def unpack_weight(words, scales):
    g, p, n, _ = words.shape
    vals = np.ascontiguousarray(words).view(ml_dtypes.float8_e4m3fn).astype(np.float64) * np.repeat(np.exp2(scales.astype(np.float64) - 127.0), 8, axis=1)[..., None]
    return vals.transpose(0, 1, 3, 2).reshape(g * 512, n)


def planes(y):
    n, m = y.shape
    v = y.astype(np.float32).astype(ml_dtypes.bfloat16).astype(np.float64).reshape(n // 32, 32, m)
    top = np.abs(v).max(1)
    byte = np.clip(np.where(top > 0, np.frexp(top)[1] - 1 + 127 - 7, 1), 1, 254)
    codes = (v * np.exp2(127.0 - byte)[:, None, :]).reshape(n, m).astype(np.float32).astype(ml_dtypes.float8_e4m3fn).view(np.uint8)
    words = codes.reshape(n // 512, 128, 4, m).transpose(0, 1, 3, 2)
    return np.ascontiguousarray(words), np.ascontiguousarray(byte.astype(np.uint8).reshape(n // 512, 16, m))


K, T, S, N, V, W = 512, 2048, 512, 512, 512, 2048
P = 2 ** 7


def setup_inputs():
    n = np.random.standard_normal
    s = mx_kscale(K)[:, None]
    c = mx_kscale(S)
    packed_xT = pack_weight(n((K, T)) * s)
    packed_eT = pack_weight(n((K, W)) / np.sqrt(K) / s)
    return {
        "x_words": packed_xT[0],
        "x_scales": packed_xT[1],
        "e_words": packed_eT[0],
        "e_scales": packed_eT[1],
        "half": (np.tile(np.random.uniform(0.3, 1.0, W), (P, 1))).astype(np.float32),
        "own": (-np.random.uniform(0.3, 1.0, (S, 1))).astype(np.float32),
        "wgt": (np.random.uniform(0.5, 1.0, (S, 1)) * c[:, None]).astype(np.float32),
        "dual": (n((S, N)) / np.sqrt(S) / c[:, None]).astype(np.float32),
        "offs": striped(np.random.permutation(T)[:S]),
        "qry": striped(np.random.permutation(W)[:V]),
    }


def reference(x_words, x_scales, e_words, e_scales, half, own, wgt, dual, offs, qry):
    xq = unpack_weight(x_words, x_scales)[:, unstriped(offs)]
    e_qry = unpack_weight(e_words, e_scales)[:, unstriped(qry)]
    ee = np.exp(0.5 * (xq.T @ e_qry) + f64(own) - (f64(half)[:1][:, unstriped(qry)]))
    a = f64(wgt) * ee
    out_0 = mxq(f64(dual), 0, "e4m3").T @ mxq(a, 0, "e4m3")
    return (out_0,) + planes(out_0)

@@ -1,0 +1,168 @@
+from contextlib import ExitStack
+
+import concourse.mybir as mybir
+from concourse.masks import make_identity
+
+K, T, S, N, V = 512, 2048, 512, 512, 512
+FLOPS = 2 * K * S * V + 2 * S * N * V
+
+F32 = mybir.dt.float32
+BF16 = mybir.dt.bfloat16
+I32 = mybir.dt.int32
+U32 = mybir.dt.uint32
+U16 = mybir.dt.uint16
+U8 = mybir.dt.uint8
+FP8X4 = mybir.dt.float8_e4m3fn_x4
+ALU = mybir.AluOpType
+ACT = mybir.ActivationFunctionType
+
+P = 128
+PACK = 4
+QUADS = 4
+CHUNK = 128
+HALFV = 256
+
+
+def tile_picked_ykrr_lin_po_kernel(
+    tc, x_words, x_scales, e_words, e_scales, half, own, wgt, dual, offs, qry, out_0, out_1, out_2
+):
+    nc = tc.nc
+    with ExitStack() as ctx:
+        keep = ctx.enter_context(tc.tile_pool(name="keep", bufs=1))
+        ring = ctx.enter_context(tc.tile_pool(name="ring", bufs=4))
+        ps_turn = ctx.enter_context(tc.psum_pool(name="ps_turn", bufs=1))
+        ps_s = ctx.enter_context(tc.psum_pool(name="ps_s", bufs=3))
+        ps_y = ctx.enter_context(tc.psum_pool(name="ps_y", bufs=3))
+
+        offs_sb = keep.tile([P, S // 16], U16, name="offs_sb")
+        qry_sb = keep.tile([P, V // 16], U16, name="qry_sb")
+        xw = keep.tile([P, T], U32, name="xw")
+        ew = keep.tile([P, T], U32, name="ew")
+        xs = keep.tile([P, T], U8, name="xs")
+        es = keep.tile([P, T], U8, name="es")
+        hw = keep.tile([P, T], F32, name="hw")
+        own_sb = keep.tile([P, PACK], F32, name="own_sb")
+        wgt_sb = keep.tile([P, PACK], F32, name="wgt_sb")
+        dual_sb = keep.tile([P, PACK, N], F32, name="dual_sb")
+        ident = keep.tile([P, P], F32, name="ident")
+        warm = keep.tile([P, 1], F32, name="warm")
+
+        nc.vector.memset(xs[:].bitcast(I32), 0)
+        nc.vector.memset(es[:].bitcast(I32), 0)
+        nc.gpsimd.memset(hw[:], 0.0)
+        make_identity(nc, ident[:])
+
+        nc.sync.dma_start(offs_sb[:], offs)
+        nc.sync.dma_start(qry_sb[:], qry)
+        nc.sync.dma_start(xw[:].bitcast(I32), x_words[0].rearrange("p n t -> p (n t)").bitcast(I32))
+        for q in range(QUADS):
+            nc.scalar.dma_start(xs[32 * q : 32 * q + 4, :].bitcast(I32), x_scales[0, 4 * q : 4 * q + 4, :].bitcast(I32))
+        nc.scalar.dma_start(hw[0:1, :], half[0:1, :])
+        for q in range(QUADS):
+            nc.scalar.dma_start(es[32 * q : 32 * q + 4, :].bitcast(I32), e_scales[0, 4 * q : 4 * q + 4, :].bitcast(I32))
+        nc.gpsimd.dma_start(own_sb[:], own.rearrange("(p j) o -> p (j o)", j=PACK))
+        nc.gpsimd.dma_start(wgt_sb[:], wgt.rearrange("(p j) o -> p (j o)", j=PACK))
+        nc.sync.dma_start(dual_sb[:], dual.rearrange("(p j) m -> p j m", j=PACK))
+        nc.sync.dma_start(ew[:].bitcast(I32), e_words[0].rearrange("p n t -> p (n t)").bitcast(I32))
+
+        nc.scalar.activation(warm[:], ident[:, 0:1], ACT.Exp)
+
+        xs_g = keep.tile([P, S], U8, name="xs_g")
+        nc.vector.tensor_copy(xs_g[:], xs[:].indirect(offs_sb[:]))
+        hg = keep.tile([P, V], F32, name="hg")
+        nc.vector.tensor_copy(hg[:], hw[:].indirect(qry_sb[:]))
+        xs_d = keep.tile([P, S], U8, name="xs_d", align_bytes=64)
+        nc.vector.tensor_copy(xs_d[:].rearrange("p (j m) -> p m j", j=PACK), xs_g[:].rearrange("p (m j) -> p m j", j=PACK))
+        xw_d = keep.tile([P, S], U32, name="xw_d", align_bytes=64)
+        nc.vector.tensor_copy(xw_d[:].rearrange("p (j m) -> p m j", j=PACK), xw[:].indirect(offs_sb[:]))
+        es_g = keep.tile([P, V], U8, name="es_g", align_bytes=64)
+        nc.vector.tensor_copy(es_g[:], es[:].indirect(qry_sb[:]))
+
+        h_t = ps_turn.tile([P, V // P, P], F32, name="h_t")
+        for b in range(V // P):
+            nc.tensor.transpose(h_t[:, b, :], hg[:, b * P : (b + 1) * P], ident[:])
+        h_col = keep.tile([P, V // P], F32, name="h_col")
+        nc.scalar.copy(h_col[:], h_t[:, :, 0])
+        h_b = ps_turn.tile([P, V], F32, name="h_b")
+        for b in range(V // P):
+            nc.tensor.transpose(h_b[:, b * P : (b + 1) * P], h_col[:, b : b + 1].to_broadcast([P, P]), ident[:])
+        shift = []
+        for h in range(V // HALFV):
+            sh = keep.tile([P, PACK, HALFV], F32, name="shift%d" % h)
+            for j in range(PACK):
+                nc.scalar.activation(
+                    sh[:, j, :], h_b[:, h * HALFV : (h + 1) * HALFV], ACT.Identity, bias=own_sb[:, j : j + 1], scale=-1.0
+                )
+            shift.append(sh)
+
+        dual_bf = keep.tile([P, PACK, P, PACK], BF16, name="dual_bf", align_bytes=64)
+        nc.scalar.copy(dual_bf[:].rearrange("p t m j -> p m j t"), dual_sb[:].rearrange("p j (m t) -> p m j t", t=PACK))
+        d_codes = keep.tile([P, N], U32, name="d_codes", align_bytes=64)
+        d_scales = keep.tile([P, N], U8, name="d_scales", align_bytes=64)
+        nc.vector.quantize_mx(d_codes[:].bitcast(FP8X4), d_scales[:], dual_bf[:].rearrange("p t m j -> p (t m j)"))
+
+        ew_g = []
+        for h in range(V // HALFV):
+            g = keep.tile([P, HALFV], U32, name="ew_g%d" % h, align_bytes=64)
+            nc.vector.tensor_copy(g[:], ew[:].indirect(qry_sb[:, h * HALFV // 16 : (h + 1) * HALFV // 16]))
+            ew_g.append(g)
+
+        y_codes = keep.tile([P, V], U32, name="y_codes", align_bytes=64)
+        y_scales = keep.tile([P, V], U8, name="y_scales", align_bytes=64)
+        out_rows = out_0.rearrange("(p t) v -> p t v", t=PACK)
+        out_words = out_1[0].rearrange("p n t -> p (n t)").bitcast(I32)
+
+        for c in range(V // CHUNK):
+            cols = slice(c * CHUNK, (c + 1) * CHUNK)
+            h, within = divmod(c * CHUNK, HALFV)
+            local = slice(within, within + CHUNK)
+            s_ps = ps_s.tile([P, PACK, CHUNK], F32, name="s_ps")
+            for j in range(PACK):
+                nc.tensor.matmul_mx(
+                    s_ps[:, j, :],
+                    lhsT=xw_d[:, j * P : (j + 1) * P].bitcast(FP8X4),
+                    lhsT_scale=xs_d[:, j * P : (j + 1) * P],
+                    rhs=ew_g[h][:, local].bitcast(FP8X4),
+                    rhs_scale=es_g[:, cols],
+                    start=True,
+                    stop=True,
+                )
+            z = ring.tile([P, CHUNK, PACK], F32, name="z")
+            nc.vector.scalar_tensor_tensor(
+                z[:],
+                s_ps[:].rearrange("p j n -> p n j"),
+                0.5,
+                shift[h][:, :, local].rearrange("p j n -> p n j"),
+                ALU.mult,
+                ALU.add,
+            )
+            ee = ring.tile([P, CHUNK, PACK], F32, name="ee")
+            nc.scalar.activation(ee[:], z[:], ACT.Exp)
+            a_bf = ring.tile([P, CHUNK, PACK], BF16, name="a_bf", align_bytes=64)
+            nc.vector.tensor_tensor(a_bf[:], ee[:], wgt_sb[:].unsqueeze(1).to_broadcast([P, CHUNK, PACK]), ALU.mult)
+            a_codes = ring.tile([P, CHUNK], U32, name="a_codes", align_bytes=64)
+            a_scales = ring.tile([P, CHUNK], U8, name="a_scales", align_bytes=64)
+            nc.vector.quantize_mx(a_codes[:].bitcast(FP8X4), a_scales[:], a_bf[:].rearrange("p n j -> p (n j)"))
+            y_ps = ps_y.tile([P, PACK, CHUNK], F32, name="y_ps")
+            for t in range(PACK):
+                nc.tensor.matmul_mx(
+                    y_ps[:, t, :],
+                    lhsT=d_codes[:, t * P : (t + 1) * P].bitcast(FP8X4),
+                    lhsT_scale=d_scales[:, t * P : (t + 1) * P],
+                    rhs=a_codes[:].bitcast(FP8X4),
+                    rhs_scale=a_scales[:],
+                    start=True,
+                    stop=True,
+                )
+            y_bf = ring.tile([P, CHUNK, PACK], BF16, name="y_bf", align_bytes=64)
+            nc.scalar.copy(y_bf[:], y_ps[:].rearrange("p t n -> p n t"))
+            y = ring.tile([P, PACK, CHUNK], F32, name="y")
+            nc.scalar.copy(y[:], y_ps[:])
+            nc.vector.quantize_mx(
+                y_codes[:, cols].bitcast(FP8X4), y_scales[:, cols], y_bf[:].rearrange("p n t -> p (n t)")
+            )
+            nc.sync.dma_start(out_rows[:, :, cols], y[:])
+            nc.sync.dma_start(out_words[:, cols], y_codes[:, cols].bitcast(I32))
+
+        for q in range(QUADS):
+            nc.sync.dma_start(out_2[0, 4 * q : 4 * q + 4, :].bitcast(I32), y_scales[32 * q : 32 * q + 4, :].bitcast(I32))

@@ -43,34 +43,39 @@ def tile_picked_ykrr_lin_po_kernel(
         hw = keep.tile([P, T], F32, name="hw")
         own_sb = keep.tile([P, PACK], F32, name="own_sb")
         wgt_sb = keep.tile([P, PACK], F32, name="wgt_sb")
-        dual_sb = keep.tile([P, PACK, N], F32, name="dual_sb")
         ident = keep.tile([P, P], F32, name="ident")
         warm = keep.tile([P, 1], F32, name="warm")
 
-        nc.vector.memset(xs[:].bitcast(I32), 0)
-        nc.vector.memset(es[:].bitcast(I32), 0)
-        nc.gpsimd.memset(hw[:], 0.0)
+        nc.gpsimd.memset(es[:].bitcast(I32), 0)
+        nc.vector.memset(hw[32:64, :].bitcast(I32), 0)
+        nc.gpsimd.memset(hw[64:128, :].bitcast(I32), 0)
         make_identity(nc, ident[:])
 
-        nc.sync.dma_start(offs_sb[:], offs)
         nc.sync.dma_start(qry_sb[:], qry)
+        nc.sync.dma_start(hw[0:32, :], half[0:32, :])
+        nc.sync.dma_start(offs_sb[:], offs)
+        for q in range(QUADS):
+            rows = x_scales[0, 4 * q : 4 * q + 4, :].bitcast(I32)
+            nc.sync.dma_start(xs[32 * q : 32 * q + 32, :].bitcast(I32), rows.unsqueeze(0).to_broadcast([8, 4, T // 4]))
         nc.sync.dma_start(xw[:].bitcast(I32), x_words[0].rearrange("p n t -> p (n t)").bitcast(I32))
         for q in range(QUADS):
-            nc.scalar.dma_start(xs[32 * q : 32 * q + 4, :].bitcast(I32), x_scales[0, 4 * q : 4 * q + 4, :].bitcast(I32))
-        nc.scalar.dma_start(hw[0:1, :], half[0:1, :])
-        for q in range(QUADS):
-            nc.scalar.dma_start(es[32 * q : 32 * q + 4, :].bitcast(I32), e_scales[0, 4 * q : 4 * q + 4, :].bitcast(I32))
-        nc.gpsimd.dma_start(own_sb[:], own.rearrange("(p j) o -> p (j o)", j=PACK))
-        nc.gpsimd.dma_start(wgt_sb[:], wgt.rearrange("(p j) o -> p (j o)", j=PACK))
-        nc.sync.dma_start(dual_sb[:], dual.rearrange("(p j) m -> p j m", j=PACK))
+            nc.sync.dma_start(es[32 * q : 32 * q + 4, :].bitcast(I32), e_scales[0, 4 * q : 4 * q + 4, :].bitcast(I32))
+        nc.sync.dma_start(own_sb[:], own.rearrange("(p j) o -> p (j o)", j=PACK))
         nc.sync.dma_start(ew[:].bitcast(I32), e_words[0].rearrange("p n t -> p (n t)").bitcast(I32))
+        nc.sync.dma_start(wgt_sb[:], wgt.rearrange("(p j) o -> p (j o)", j=PACK))
+        dual_rows = dual.rearrange("(p j) m -> p j m", j=PACK)
+        dual_sb = []
+        for h in range(2):
+            part = keep.tile([P, PACK, N // 2], F32, name="dual_sb%d" % h)
+            nc.sync.dma_start(part[:], dual_rows[:, :, h * N // 2 : (h + 1) * N // 2])
+            dual_sb.append(part)
 
         nc.scalar.activation(warm[:], ident[:, 0:1], ACT.Exp)
 
-        xs_g = keep.tile([P, S], U8, name="xs_g")
-        nc.vector.tensor_copy(xs_g[:], xs[:].indirect(offs_sb[:]))
         hg = keep.tile([P, V], F32, name="hg")
         nc.vector.tensor_copy(hg[:], hw[:].indirect(qry_sb[:]))
+        xs_g = keep.tile([P, S], U8, name="xs_g")
+        nc.vector.tensor_copy(xs_g[:], xs[:].indirect(offs_sb[:]))
         xs_d = keep.tile([P, S], U8, name="xs_d", align_bytes=64)
         nc.vector.tensor_copy(xs_d[:].rearrange("p (j m) -> p m j", j=PACK), xs_g[:].rearrange("p (m j) -> p m j", j=PACK))
         xw_d = keep.tile([P, S], U32, name="xw_d", align_bytes=64)
@@ -95,17 +100,21 @@ def tile_picked_ykrr_lin_po_kernel(
                 )
             shift.append(sh)
 
-        dual_bf = keep.tile([P, PACK, P, PACK], BF16, name="dual_bf", align_bytes=64)
-        nc.scalar.copy(dual_bf[:].rearrange("p t m j -> p m j t"), dual_sb[:].rearrange("p j (m t) -> p m j t", t=PACK))
-        d_codes = keep.tile([P, N], U32, name="d_codes", align_bytes=64)
-        d_scales = keep.tile([P, N], U8, name="d_scales", align_bytes=64)
-        nc.vector.quantize_mx(d_codes[:].bitcast(FP8X4), d_scales[:], dual_bf[:].rearrange("p t m j -> p (t m j)"))
-
         ew_g = []
         for h in range(V // HALFV):
             g = keep.tile([P, HALFV], U32, name="ew_g%d" % h, align_bytes=64)
             nc.vector.tensor_copy(g[:], ew[:].indirect(qry_sb[:, h * HALFV // 16 : (h + 1) * HALFV // 16]))
             ew_g.append(g)
+
+        dual_bf = keep.tile([P, PACK, P, PACK], BF16, name="dual_bf", align_bytes=64)
+        for h, copy in enumerate((nc.scalar.copy, nc.vector.tensor_copy)):
+            copy(
+                dual_bf[:, :, h * P // 2 : (h + 1) * P // 2, :].rearrange("p t m j -> p m j t"),
+                dual_sb[h][:].rearrange("p j (m t) -> p m j t", t=PACK),
+            )
+        d_codes = keep.tile([P, N], U32, name="d_codes", align_bytes=64)
+        d_scales = keep.tile([P, N], U8, name="d_scales", align_bytes=64)
+        nc.vector.quantize_mx(d_codes[:].bitcast(FP8X4), d_scales[:], dual_bf[:].rearrange("p t m j -> p (t m j)"))
 
         y_codes = keep.tile([P, V], U32, name="y_codes", align_bytes=64)
         y_scales = keep.tile([P, V], U8, name="y_scales", align_bytes=64)

@@ -3,7 +3,11 @@ from contextlib import ExitStack
 import concourse.mybir as mybir
 from concourse.masks import make_identity
 
-K, T, S, N, V = 512, 2048, 512, 512, 512
+K = 512
+STORE = 2048
+S = 512
+V = 512
+N = 512
 FLOPS = 2 * K * S * V + 2 * S * N * V
 
 F32 = mybir.dt.float32
@@ -19,8 +23,13 @@ ACT = mybir.ActivationFunctionType
 P = 128
 PACK = 4
 QUADS = 4
+QUAD = P // QUADS
+SCALE_ROWS = 4
+LIST_ROWS = 16
 CHUNK = 128
-HALFV = 256
+CHUNKS = V // CHUNK
+PIECE = 256
+SCALAR_ROUNDS = 2
 
 
 def tile_picked_ykrr_lin_po_kernel(
@@ -29,39 +38,43 @@ def tile_picked_ykrr_lin_po_kernel(
     nc = tc.nc
     with ExitStack() as ctx:
         keep = ctx.enter_context(tc.tile_pool(name="keep", bufs=1))
-        ring = ctx.enter_context(tc.tile_pool(name="ring", bufs=4))
-        ps_turn = ctx.enter_context(tc.psum_pool(name="ps_turn", bufs=1))
-        ps_s = ctx.enter_context(tc.psum_pool(name="ps_s", bufs=3))
-        ps_y = ctx.enter_context(tc.psum_pool(name="ps_y", bufs=3))
+        ring = ctx.enter_context(tc.tile_pool(name="ring", bufs=CHUNKS))
+        ps_s = ctx.enter_context(tc.psum_pool(name="ps_s", bufs=CHUNKS))
+        ps_y = ctx.enter_context(tc.psum_pool(name="ps_y", bufs=CHUNKS))
 
-        offs_sb = keep.tile([P, S // 16], U16, name="offs_sb")
-        qry_sb = keep.tile([P, V // 16], U16, name="qry_sb")
-        xw = keep.tile([P, T], U32, name="xw")
-        ew = keep.tile([P, T], U32, name="ew")
-        xs = keep.tile([P, T], U8, name="xs")
-        es = keep.tile([P, T], U8, name="es")
-        hw = keep.tile([P, T], F32, name="hw")
+        offs_sb = keep.tile([P, S // LIST_ROWS], U16, name="offs_sb")
+        qry_sb = keep.tile([P, V // LIST_ROWS], U16, name="qry_sb")
+        xw = keep.tile([P, STORE], U32, name="xw")
+        ew = keep.tile([P, STORE], U32, name="ew")
+        xs = keep.tile([P, STORE], U8, name="xs")
+        es = keep.tile([P, STORE], U8, name="es")
+        hw = keep.tile([P, STORE], F32, name="hw")
         own_sb = keep.tile([P, PACK], F32, name="own_sb")
         wgt_sb = keep.tile([P, PACK], F32, name="wgt_sb")
         ident = keep.tile([P, P], F32, name="ident")
-        warm = keep.tile([P, 1], F32, name="warm")
 
         nc.gpsimd.memset(es[:].bitcast(I32), 0)
-        nc.vector.memset(hw[32:64, :].bitcast(I32), 0)
-        nc.gpsimd.memset(hw[64:128, :].bitcast(I32), 0)
+        nc.vector.memset(hw[QUAD : 2 * QUAD, :].bitcast(I32), 0)
+        nc.gpsimd.memset(hw[2 * QUAD :, :].bitcast(I32), 0)
         make_identity(nc, ident[:])
 
         nc.sync.dma_start(qry_sb[:], qry)
-        nc.sync.dma_start(hw[0:32, :], half[0:32, :])
+        nc.sync.dma_start(hw[:QUAD, :], half[:QUAD, :])
         nc.sync.dma_start(offs_sb[:], offs)
         for q in range(QUADS):
-            rows = x_scales[0, 4 * q : 4 * q + 4, :].bitcast(I32)
-            nc.sync.dma_start(xs[32 * q : 32 * q + 32, :].bitcast(I32), rows.unsqueeze(0).to_broadcast([8, 4, T // 4]))
-        nc.sync.dma_start(xw[:].bitcast(I32), x_words[0].rearrange("p n t -> p (n t)").bitcast(I32))
+            rows = x_scales[0, SCALE_ROWS * q : SCALE_ROWS * (q + 1), :].bitcast(I32)
+            nc.sync.dma_start(
+                xs[QUAD * q : QUAD * (q + 1), :].bitcast(I32),
+                rows.unsqueeze(0).to_broadcast([QUAD // SCALE_ROWS, SCALE_ROWS, STORE // 4]),
+            )
+        nc.sync.dma_start(xw[:].bitcast(I32), x_words[0].rearrange("p n r -> p (n r)").bitcast(I32))
         for q in range(QUADS):
-            nc.sync.dma_start(es[32 * q : 32 * q + 4, :].bitcast(I32), e_scales[0, 4 * q : 4 * q + 4, :].bitcast(I32))
+            nc.sync.dma_start(
+                es[QUAD * q : QUAD * q + SCALE_ROWS, :].bitcast(I32),
+                e_scales[0, SCALE_ROWS * q : SCALE_ROWS * (q + 1), :].bitcast(I32),
+            )
         nc.sync.dma_start(own_sb[:], own.rearrange("(p j) o -> p (j o)", j=PACK))
-        nc.sync.dma_start(ew[:].bitcast(I32), e_words[0].rearrange("p n t -> p (n t)").bitcast(I32))
+        nc.sync.dma_start(ew[:].bitcast(I32), e_words[0].rearrange("p n r -> p (n r)").bitcast(I32))
         nc.sync.dma_start(wgt_sb[:], wgt.rearrange("(p j) o -> p (j o)", j=PACK))
         dual_rows = dual.rearrange("(p j) m -> p j m", j=PACK)
         dual_sb = []
@@ -70,68 +83,76 @@ def tile_picked_ykrr_lin_po_kernel(
             nc.sync.dma_start(part[:], dual_rows[:, :, h * N // 2 : (h + 1) * N // 2])
             dual_sb.append(part)
 
-        nc.scalar.activation(warm[:], ident[:, 0:1], ACT.Exp)
-
         hg = keep.tile([P, V], F32, name="hg")
         nc.vector.tensor_copy(hg[:], hw[:].indirect(qry_sb[:]))
         xs_g = keep.tile([P, S], U8, name="xs_g")
         nc.vector.tensor_copy(xs_g[:], xs[:].indirect(offs_sb[:]))
         xs_d = keep.tile([P, S], U8, name="xs_d", align_bytes=64)
-        nc.vector.tensor_copy(xs_d[:].rearrange("p (j m) -> p m j", j=PACK), xs_g[:].rearrange("p (m j) -> p m j", j=PACK))
+        nc.vector.tensor_copy(
+            xs_d[:].rearrange("k (j p) -> k p j", j=PACK), xs_g[:].rearrange("k (p j) -> k p j", j=PACK)
+        )
         xw_d = keep.tile([P, S], U32, name="xw_d", align_bytes=64)
-        nc.vector.tensor_copy(xw_d[:].rearrange("p (j m) -> p m j", j=PACK), xw[:].indirect(offs_sb[:]))
+        nc.vector.tensor_copy(xw_d[:].rearrange("k (j p) -> k p j", j=PACK), xw[:].indirect(offs_sb[:]))
         es_g = keep.tile([P, V], U8, name="es_g", align_bytes=64)
         nc.vector.tensor_copy(es_g[:], es[:].indirect(qry_sb[:]))
 
-        h_t = ps_turn.tile([P, V // P, P], F32, name="h_t")
+        h_turned = ps_y.tile([P, V // P, P], F32, name="h_turned", tag="y_ps")
         for b in range(V // P):
-            nc.tensor.transpose(h_t[:, b, :], hg[:, b * P : (b + 1) * P], ident[:])
+            nc.tensor.transpose(h_turned[:, b, :], hg[:, b * P : (b + 1) * P], ident[:])
         h_col = keep.tile([P, V // P], F32, name="h_col")
-        nc.scalar.copy(h_col[:], h_t[:, :, 0])
-        h_b = ps_turn.tile([P, V], F32, name="h_b")
+        nc.scalar.copy(h_col[:], h_turned[:, :, 0])
+        h_rows = ps_y.tile([P, V], F32, name="h_rows", tag="y_ps")
         for b in range(V // P):
-            nc.tensor.transpose(h_b[:, b * P : (b + 1) * P], h_col[:, b : b + 1].to_broadcast([P, P]), ident[:])
+            nc.tensor.transpose(h_rows[:, b * P : (b + 1) * P], h_col[:, b : b + 1].to_broadcast([P, P]), ident[:])
+
         shift = []
-        for h in range(V // HALFV):
-            sh = keep.tile([P, PACK, HALFV], F32, name="shift%d" % h)
+        for i in range(V // PIECE):
+            shift_i = keep.tile([P, PACK, PIECE], F32, name="shift%d" % i)
             for j in range(PACK):
                 nc.scalar.activation(
-                    sh[:, j, :], h_b[:, h * HALFV : (h + 1) * HALFV], ACT.Identity, bias=own_sb[:, j : j + 1], scale=-1.0
+                    shift_i[:, j, :],
+                    h_rows[:, i * PIECE : (i + 1) * PIECE],
+                    ACT.Identity,
+                    bias=own_sb[:, j : j + 1],
+                    scale=-1.0,
                 )
-            shift.append(sh)
+            shift.append(shift_i)
 
         ew_g = []
-        for h in range(V // HALFV):
-            g = keep.tile([P, HALFV], U32, name="ew_g%d" % h, align_bytes=64)
-            nc.vector.tensor_copy(g[:], ew[:].indirect(qry_sb[:, h * HALFV // 16 : (h + 1) * HALFV // 16]))
-            ew_g.append(g)
+        for i in range(V // PIECE):
+            piece = keep.tile([P, PIECE], U32, name="ew_g%d" % i, align_bytes=64)
+            nc.vector.tensor_copy(
+                piece[:], ew[:].indirect(qry_sb[:, i * PIECE // LIST_ROWS : (i + 1) * PIECE // LIST_ROWS])
+            )
+            ew_g.append(piece)
 
         dual_bf = keep.tile([P, PACK, P, PACK], BF16, name="dual_bf", align_bytes=64)
         for h, copy in enumerate((nc.scalar.copy, nc.vector.tensor_copy)):
             copy(
-                dual_bf[:, :, h * P // 2 : (h + 1) * P // 2, :].rearrange("p t m j -> p m j t"),
-                dual_sb[h][:].rearrange("p j (m t) -> p m j t", t=PACK),
+                dual_bf[:, :, h * P // 2 : (h + 1) * P // 2, :].rearrange("p r c j -> p c j r"),
+                dual_sb[h][:].rearrange("p j (c r) -> p c j r", r=PACK),
             )
         d_codes = keep.tile([P, N], U32, name="d_codes", align_bytes=64)
         d_scales = keep.tile([P, N], U8, name="d_scales", align_bytes=64)
-        nc.vector.quantize_mx(d_codes[:].bitcast(FP8X4), d_scales[:], dual_bf[:].rearrange("p t m j -> p (t m j)"))
+        nc.vector.quantize_mx(d_codes[:].bitcast(FP8X4), d_scales[:], dual_bf[:].rearrange("p r c j -> p (r c j)"))
 
         y_codes = keep.tile([P, V], U32, name="y_codes", align_bytes=64)
         y_scales = keep.tile([P, V], U8, name="y_scales", align_bytes=64)
-        out_rows = out_0.rearrange("(p t) v -> p t v", t=PACK)
-        out_words = out_1[0].rearrange("p n t -> p (n t)").bitcast(I32)
+        out_rows = out_0.rearrange("(p r) v -> p r v", r=PACK)
+        out_words = out_1[0].rearrange("p n r -> p (n r)").bitcast(I32)
 
-        for c in range(V // CHUNK):
+        for c in range(CHUNKS):
             cols = slice(c * CHUNK, (c + 1) * CHUNK)
-            h, within = divmod(c * CHUNK, HALFV)
+            i, within = divmod(c * CHUNK, PIECE)
             local = slice(within, within + CHUNK)
+
             s_ps = ps_s.tile([P, PACK, CHUNK], F32, name="s_ps")
             for j in range(PACK):
                 nc.tensor.matmul_mx(
                     s_ps[:, j, :],
                     lhsT=xw_d[:, j * P : (j + 1) * P].bitcast(FP8X4),
                     lhsT_scale=xs_d[:, j * P : (j + 1) * P],
-                    rhs=ew_g[h][:, local].bitcast(FP8X4),
+                    rhs=ew_g[i][:, local].bitcast(FP8X4),
                     rhs_scale=es_g[:, cols],
                     start=True,
                     stop=True,
@@ -141,7 +162,7 @@ def tile_picked_ykrr_lin_po_kernel(
                 z[:],
                 s_ps[:].rearrange("p j n -> p n j"),
                 0.5,
-                shift[h][:, :, local].rearrange("p j n -> p n j"),
+                shift[i][:, :, local].rearrange("p j n -> p n j"),
                 ALU.mult,
                 ALU.add,
             )
@@ -152,26 +173,36 @@ def tile_picked_ykrr_lin_po_kernel(
             a_codes = ring.tile([P, CHUNK], U32, name="a_codes", align_bytes=64)
             a_scales = ring.tile([P, CHUNK], U8, name="a_scales", align_bytes=64)
             nc.vector.quantize_mx(a_codes[:].bitcast(FP8X4), a_scales[:], a_bf[:].rearrange("p n j -> p (n j)"))
+
             y_ps = ps_y.tile([P, PACK, CHUNK], F32, name="y_ps")
-            for t in range(PACK):
+            for r in range(PACK):
                 nc.tensor.matmul_mx(
-                    y_ps[:, t, :],
-                    lhsT=d_codes[:, t * P : (t + 1) * P].bitcast(FP8X4),
-                    lhsT_scale=d_scales[:, t * P : (t + 1) * P],
+                    y_ps[:, r, :],
+                    lhsT=d_codes[:, r * P : (r + 1) * P].bitcast(FP8X4),
+                    lhsT_scale=d_scales[:, r * P : (r + 1) * P],
                     rhs=a_codes[:].bitcast(FP8X4),
                     rhs_scale=a_scales[:],
                     start=True,
                     stop=True,
                 )
-            y_bf = ring.tile([P, CHUNK, PACK], BF16, name="y_bf", align_bytes=64)
-            nc.scalar.copy(y_bf[:], y_ps[:].rearrange("p t n -> p n t"))
-            y = ring.tile([P, PACK, CHUNK], F32, name="y")
-            nc.scalar.copy(y[:], y_ps[:])
-            nc.vector.quantize_mx(
-                y_codes[:, cols].bitcast(FP8X4), y_scales[:, cols], y_bf[:].rearrange("p n t -> p (n t)")
-            )
-            nc.sync.dma_start(out_rows[:, :, cols], y[:])
-            nc.sync.dma_start(out_words[:, cols], y_codes[:, cols].bitcast(I32))
 
+            y = ring.tile([P, PACK, CHUNK], F32, name="y")
+            y_bf = ring.tile([P, CHUNK, PACK], BF16, name="y_bf", align_bytes=64)
+            if c < SCALAR_ROUNDS:
+                nc.scalar.copy(y[:], y_ps[:])
+                nc.scalar.copy(y_bf[:], y_ps[:].rearrange("p r n -> p n r"))
+            else:
+                nc.vector.tensor_copy(y_bf[:], y_ps[:].rearrange("p r n -> p n r"))
+                nc.scalar.copy(y[:], y_ps[:])
+            queue = nc.scalar if c == CHUNKS - 1 else nc.sync
+            queue.dma_start(out_rows[:, :, cols], y[:])
+            nc.vector.quantize_mx(
+                y_codes[:, cols].bitcast(FP8X4), y_scales[:, cols], y_bf[:].rearrange("p n r -> p (n r)")
+            )
+
+        nc.sync.dma_start(out_words, y_codes[:].bitcast(I32))
         for q in range(QUADS):
-            nc.sync.dma_start(out_2[0, 4 * q : 4 * q + 4, :].bitcast(I32), y_scales[32 * q : 32 * q + 4, :].bitcast(I32))
+            nc.sync.dma_start(
+                out_2[0, SCALE_ROWS * q : SCALE_ROWS * (q + 1), :].bitcast(I32),
+                y_scales[QUAD * q : QUAD * q + SCALE_ROWS, :].bitcast(I32),
+            )

@@ -28,8 +28,8 @@ SCALE_ROWS = 4
 LIST_ROWS = 16
 CHUNK = 128
 CHUNKS = V // CHUNK
+UNIT = 8
 PIECE = 256
-SCALAR_ROUNDS = 2
 
 
 def tile_picked_ykrr_lin_po_kernel(
@@ -53,29 +53,29 @@ def tile_picked_ykrr_lin_po_kernel(
         wgt_sb = keep.tile([P, PACK], F32, name="wgt_sb")
         ident = keep.tile([P, P], F32, name="ident")
 
-        nc.gpsimd.memset(es[:].bitcast(I32), 0)
-        nc.vector.memset(hw[QUAD : 2 * QUAD, :].bitcast(I32), 0)
-        nc.gpsimd.memset(hw[2 * QUAD :, :].bitcast(I32), 0)
+        nc.gpsimd.memset(xs[:].bitcast(I32), 0)
+        nc.vector.memset(hw[: P - 1, : STORE // 2].bitcast(I32), 0)
+        nc.gpsimd.memset(hw[: P - 1, STORE // 2 :].bitcast(I32), 0)
         make_identity(nc, ident[:])
 
+        nc.sync.dma_start(wgt_sb[:], wgt.rearrange("(p j) o -> p (j o)", j=PACK))
         nc.sync.dma_start(qry_sb[:], qry)
-        nc.sync.dma_start(hw[:QUAD, :], half[:QUAD, :])
-        nc.sync.dma_start(offs_sb[:], offs)
+        nc.sync.dma_start(hw[P - 1 :, :], half[:1, :])
         for q in range(QUADS):
-            rows = x_scales[0, SCALE_ROWS * q : SCALE_ROWS * (q + 1), :].bitcast(I32)
+            rows = e_scales[0, SCALE_ROWS * q : SCALE_ROWS * (q + 1), :].bitcast(I32)
             nc.sync.dma_start(
-                xs[QUAD * q : QUAD * (q + 1), :].bitcast(I32),
+                es[QUAD * q : QUAD * (q + 1), :].bitcast(I32),
                 rows.unsqueeze(0).to_broadcast([QUAD // SCALE_ROWS, SCALE_ROWS, STORE // 4]),
             )
         nc.sync.dma_start(xw[:].bitcast(I32), x_words[0].rearrange("p n r -> p (n r)").bitcast(I32))
+        nc.sync.dma_start(offs_sb[:], offs)
         for q in range(QUADS):
             nc.sync.dma_start(
-                es[QUAD * q : QUAD * q + SCALE_ROWS, :].bitcast(I32),
-                e_scales[0, SCALE_ROWS * q : SCALE_ROWS * (q + 1), :].bitcast(I32),
+                xs[QUAD * q : QUAD * q + SCALE_ROWS, :].bitcast(I32),
+                x_scales[0, SCALE_ROWS * q : SCALE_ROWS * (q + 1), :].bitcast(I32),
             )
         nc.sync.dma_start(own_sb[:], own.rearrange("(p j) o -> p (j o)", j=PACK))
         nc.sync.dma_start(ew[:].bitcast(I32), e_words[0].rearrange("p n r -> p (n r)").bitcast(I32))
-        nc.sync.dma_start(wgt_sb[:], wgt.rearrange("(p j) o -> p (j o)", j=PACK))
         dual_rows = dual.rearrange("(p j) m -> p j m", j=PACK)
         dual_sb = []
         for h in range(2):
@@ -83,51 +83,90 @@ def tile_picked_ykrr_lin_po_kernel(
             nc.sync.dma_start(part[:], dual_rows[:, :, h * N // 2 : (h + 1) * N // 2])
             dual_sb.append(part)
 
+        square = keep.tile([P, PACK], F32, name="square")
+        held = keep.tile([P, PACK], F32, name="held")
+        nc.vector.tensor_tensor(square[:], wgt_sb[:], wgt_sb[:], ALU.mult)
+        nc.vector.tensor_scalar(held[:], square[:], 2.0**-64, 2.0**63, ALU.max, ALU.min)
+        ln_held = keep.tile([P, PACK], F32, name="ln_held")
+        nc.scalar.activation(ln_held[:], held[:], ACT.Ln)
+        inv_size = keep.tile([P, PACK], F32, name="inv_size")
+        nc.scalar.activation(inv_size[:], ln_held[:], ACT.Exp, scale=-0.5)
+        own2 = keep.tile([P, PACK], F32, name="own2")
+        nc.gpsimd.tensor_tensor(own2[:], own_sb[:], own_sb[:], ALU.add)
+        bias2 = keep.tile([P, PACK], F32, name="bias2")
+        nc.gpsimd.tensor_tensor(bias2[:], ln_held[:], own2[:], ALU.add)
+        unit = keep.tile([P, UNIT, PACK], BF16, name="unit")
+        nc.gpsimd.tensor_tensor(
+            unit[:],
+            wgt_sb[:].unsqueeze(1).to_broadcast([P, UNIT, PACK]),
+            inv_size[:].unsqueeze(1).to_broadcast([P, UNIT, PACK]),
+            ALU.mult,
+        )
+
         hg = keep.tile([P, V], F32, name="hg")
         nc.vector.tensor_copy(hg[:], hw[:].indirect(qry_sb[:]))
+        es_g = keep.tile([P, V], U8, name="es_g", align_bytes=64)
+        nc.vector.tensor_copy(es_g[:], es[:].indirect(qry_sb[:]))
+        xw_d = keep.tile([P, S], U32, name="xw_d", align_bytes=64)
+        nc.vector.tensor_copy(xw_d[:].rearrange("k (j p) -> k p j", j=PACK), xw[:].indirect(offs_sb[:]))
         xs_g = keep.tile([P, S], U8, name="xs_g")
         nc.vector.tensor_copy(xs_g[:], xs[:].indirect(offs_sb[:]))
         xs_d = keep.tile([P, S], U8, name="xs_d", align_bytes=64)
         nc.vector.tensor_copy(
             xs_d[:].rearrange("k (j p) -> k p j", j=PACK), xs_g[:].rearrange("k (p j) -> k p j", j=PACK)
         )
-        xw_d = keep.tile([P, S], U32, name="xw_d", align_bytes=64)
-        nc.vector.tensor_copy(xw_d[:].rearrange("k (j p) -> k p j", j=PACK), xw[:].indirect(offs_sb[:]))
-        es_g = keep.tile([P, V], U8, name="es_g", align_bytes=64)
-        nc.vector.tensor_copy(es_g[:], es[:].indirect(qry_sb[:]))
 
         h_turned = ps_y.tile([P, V // P, P], F32, name="h_turned", tag="y_ps")
         for b in range(V // P):
             nc.tensor.transpose(h_turned[:, b, :], hg[:, b * P : (b + 1) * P], ident[:])
         h_col = keep.tile([P, V // P], F32, name="h_col")
-        nc.scalar.copy(h_col[:], h_turned[:, :, 0])
+        nc.scalar.copy(h_col[:], h_turned[:, :, P - 1])
         h_rows = ps_y.tile([P, V], F32, name="h_rows", tag="y_ps")
         for b in range(V // P):
             nc.tensor.transpose(h_rows[:, b * P : (b + 1) * P], h_col[:, b : b + 1].to_broadcast([P, P]), ident[:])
 
-        shift = []
-        for i in range(V // PIECE):
-            shift_i = keep.tile([P, PACK, PIECE], F32, name="shift%d" % i)
-            for j in range(PACK):
-                nc.scalar.activation(
-                    shift_i[:, j, :],
-                    h_rows[:, i * PIECE : (i + 1) * PIECE],
-                    ACT.Identity,
-                    bias=own_sb[:, j : j + 1],
-                    scale=-1.0,
-                )
-            shift.append(shift_i)
+        h2 = keep.tile([P, V], F32, name="h2")
+        nc.scalar.activation(h2[:], h_rows[:], ACT.Copy, scale=-2.0)
 
-        ew_g = []
+        y_codes = keep.tile([P, V], U32, name="y_codes", align_bytes=64)
+        y_scales = keep.tile([P, V], U8, name="y_scales", align_bytes=64)
+        out_rows = out_0.rearrange("(p r) v -> p r v", r=PACK)
+        out_words = out_1[0].rearrange("p n r -> p (n r)").bitcast(I32)
+
+        picked = []
         for i in range(V // PIECE):
-            piece = keep.tile([P, PIECE], U32, name="ew_g%d" % i, align_bytes=64)
-            nc.vector.tensor_copy(
-                piece[:], ew[:].indirect(qry_sb[:, i * PIECE // LIST_ROWS : (i + 1) * PIECE // LIST_ROWS])
-            )
-            ew_g.append(piece)
+            entries = qry_sb[:, i * PIECE // LIST_ROWS : (i + 1) * PIECE // LIST_ROWS]
+            ew_g = keep.tile([P, PIECE], U32, name="ew_g%d" % i, align_bytes=64)
+            nc.vector.tensor_copy(ew_g[:], ew[:].indirect(entries))
+            picked.append(ew_g)
+
+        z2 = []
+        for i in range(V // PIECE):
+            cols = slice(i * PIECE, (i + 1) * PIECE)
+            ew_g = picked[i]
+            z2_i = keep.tile([P, PACK, PIECE], F32, name="z2_%d" % i)
+            for jj in range(PACK // 2):
+                s_ps = ps_s.tile([P, 2, PIECE], F32, name="s_ps")
+                for u in range(2):
+                    j = 2 * jj + u
+                    nc.tensor.matmul_mx(
+                        s_ps[:, u, :],
+                        lhsT=xw_d[:, j * P : (j + 1) * P].bitcast(FP8X4),
+                        lhsT_scale=xs_d[:, j * P : (j + 1) * P],
+                        rhs=ew_g[:].bitcast(FP8X4),
+                        rhs_scale=es_g[:, cols],
+                        start=True,
+                        stop=True,
+                    )
+                for u in range(2):
+                    j = 2 * jj + u
+                    nc.vector.scalar_tensor_tensor(
+                        z2_i[:, j, :], s_ps[:, u, :], bias2[:, j : j + 1], h2[:, cols], ALU.add, ALU.add
+                    )
+            z2.append(z2_i)
 
         dual_bf = keep.tile([P, PACK, P, PACK], BF16, name="dual_bf", align_bytes=64)
-        for h, copy in enumerate((nc.scalar.copy, nc.vector.tensor_copy)):
+        for h, copy in enumerate((nc.scalar.copy, nc.scalar.copy)):
             copy(
                 dual_bf[:, :, h * P // 2 : (h + 1) * P // 2, :].rearrange("p r c j -> p c j r"),
                 dual_sb[h][:].rearrange("p j (c r) -> p c j r", r=PACK),
@@ -136,40 +175,24 @@ def tile_picked_ykrr_lin_po_kernel(
         d_scales = keep.tile([P, N], U8, name="d_scales", align_bytes=64)
         nc.vector.quantize_mx(d_codes[:].bitcast(FP8X4), d_scales[:], dual_bf[:].rearrange("p r c j -> p (r c j)"))
 
-        y_codes = keep.tile([P, V], U32, name="y_codes", align_bytes=64)
-        y_scales = keep.tile([P, V], U8, name="y_scales", align_bytes=64)
-        out_rows = out_0.rearrange("(p r) v -> p r v", r=PACK)
-        out_words = out_1[0].rearrange("p n r -> p (n r)").bitcast(I32)
-
+        y_banks = []
         for c in range(CHUNKS):
-            cols = slice(c * CHUNK, (c + 1) * CHUNK)
             i, within = divmod(c * CHUNK, PIECE)
             local = slice(within, within + CHUNK)
-
-            s_ps = ps_s.tile([P, PACK, CHUNK], F32, name="s_ps")
-            for j in range(PACK):
-                nc.tensor.matmul_mx(
-                    s_ps[:, j, :],
-                    lhsT=xw_d[:, j * P : (j + 1) * P].bitcast(FP8X4),
-                    lhsT_scale=xs_d[:, j * P : (j + 1) * P],
-                    rhs=ew_g[i][:, local].bitcast(FP8X4),
-                    rhs_scale=es_g[:, cols],
-                    start=True,
-                    stop=True,
-                )
-            z = ring.tile([P, CHUNK, PACK], F32, name="z")
-            nc.vector.scalar_tensor_tensor(
-                z[:],
-                s_ps[:].rearrange("p j n -> p n j"),
-                0.5,
-                shift[i][:, :, local].rearrange("p j n -> p n j"),
-                ALU.mult,
-                ALU.add,
+            ee = ring.tile([P, CHUNK, PACK], BF16, name="ee")
+            nc.scalar.activation(
+                ee[:].rearrange("p (c i) j -> p c j i", i=PACK),
+                z2[i][:, :, local].rearrange("p j (c i) -> p c j i", i=PACK),
+                ACT.Exp,
+                scale=0.5,
             )
-            ee = ring.tile([P, CHUNK, PACK], F32, name="ee")
-            nc.scalar.activation(ee[:], z[:], ACT.Exp)
             a_bf = ring.tile([P, CHUNK, PACK], BF16, name="a_bf", align_bytes=64)
-            nc.vector.tensor_tensor(a_bf[:], ee[:], wgt_sb[:].unsqueeze(1).to_broadcast([P, CHUNK, PACK]), ALU.mult)
+            nc.vector.tensor_tensor(
+                a_bf[:].rearrange("p (g n) j -> p g (n j)", n=UNIT),
+                ee[:].rearrange("p (g n) j -> p g (n j)", n=UNIT),
+                unit[:].rearrange("p n j -> p (n j)").unsqueeze(1).to_broadcast([P, CHUNK // UNIT, UNIT * PACK]),
+                ALU.mult,
+            )
             a_codes = ring.tile([P, CHUNK], U32, name="a_codes", align_bytes=64)
             a_scales = ring.tile([P, CHUNK], U8, name="a_scales", align_bytes=64)
             nc.vector.quantize_mx(a_codes[:].bitcast(FP8X4), a_scales[:], a_bf[:].rearrange("p n j -> p (n j)"))
@@ -185,12 +208,17 @@ def tile_picked_ykrr_lin_po_kernel(
                     start=True,
                     stop=True,
                 )
+            y_banks.append(y_ps)
 
+        for c, y_ps in enumerate(y_banks):
+            cols = slice(c * CHUNK, (c + 1) * CHUNK)
             y = ring.tile([P, PACK, CHUNK], F32, name="y")
             y_bf = ring.tile([P, CHUNK, PACK], BF16, name="y_bf", align_bytes=64)
-            if c < SCALAR_ROUNDS:
+            if c < CHUNKS - 1:
                 nc.scalar.copy(y[:], y_ps[:])
-                nc.scalar.copy(y_bf[:], y_ps[:].rearrange("p r n -> p n r"))
+                nc.vector.tensor_copy(
+                    y_bf[:].rearrange("p (c i) r -> p c r i", i=PACK), y[:].rearrange("p r (c i) -> p c r i", i=PACK)
+                )
             else:
                 nc.vector.tensor_copy(y_bf[:], y_ps[:].rearrange("p r n -> p n r"))
                 nc.scalar.copy(y[:], y_ps[:])
@@ -200,7 +228,10 @@ def tile_picked_ykrr_lin_po_kernel(
                 y_codes[:, cols].bitcast(FP8X4), y_scales[:, cols], y_bf[:].rearrange("p n r -> p (n r)")
             )
 
-        nc.sync.dma_start(out_words, y_codes[:].bitcast(I32))
+            if c >= CHUNKS - 2:
+                done = slice(0, (c + 1) * CHUNK) if c == CHUNKS - 2 else cols
+                nc.sync.dma_start(out_words[:, done], y_codes[:, done].bitcast(I32))
+
         for q in range(QUADS):
             nc.sync.dma_start(
                 out_2[0, SCALE_ROWS * q : SCALE_ROWS * (q + 1), :].bitcast(I32),

@@ -29,6 +29,8 @@ LIST_ROWS = 16
 CHUNK = 128
 CHUNKS = V // CHUNK
 UNIT = 8
+BANK = 512
+STAGES = ((0, 128), (128, 128), (256, 128), (384, 64), (448, 64))
 PIECE = 256
 
 
@@ -69,12 +71,12 @@ def tile_picked_ykrr_lin_po_kernel(
             )
         nc.sync.dma_start(xw[:].bitcast(I32), x_words[0].rearrange("p n r -> p (n r)").bitcast(I32))
         nc.sync.dma_start(offs_sb[:], offs)
+        nc.sync.dma_start(own_sb[:], own.rearrange("(p j) o -> p (j o)", j=PACK))
         for q in range(QUADS):
             nc.sync.dma_start(
                 xs[QUAD * q : QUAD * q + SCALE_ROWS, :].bitcast(I32),
                 x_scales[0, SCALE_ROWS * q : SCALE_ROWS * (q + 1), :].bitcast(I32),
             )
-        nc.sync.dma_start(own_sb[:], own.rearrange("(p j) o -> p (j o)", j=PACK))
         nc.sync.dma_start(ew[:].bitcast(I32), e_words[0].rearrange("p n r -> p (n r)").bitcast(I32))
         dual_rows = dual.rearrange("(p j) m -> p j m", j=PACK)
         dual_sb = []
@@ -125,13 +127,9 @@ def tile_picked_ykrr_lin_po_kernel(
         for b in range(V // P):
             nc.tensor.transpose(h_rows[:, b * P : (b + 1) * P], h_col[:, b : b + 1].to_broadcast([P, P]), ident[:])
 
-        h2 = keep.tile([P, V], F32, name="h2")
-        nc.scalar.activation(h2[:], h_rows[:], ACT.Copy, scale=-2.0)
-
-        y_codes = keep.tile([P, V], U32, name="y_codes", align_bytes=64)
-        y_scales = keep.tile([P, V], U8, name="y_scales", align_bytes=64)
-        out_rows = out_0.rearrange("(p r) v -> p r v", r=PACK)
-        out_words = out_1[0].rearrange("p n r -> p (n r)").bitcast(I32)
+        shift2 = keep.tile([P, PACK, V], F32, name="shift2")
+        for j in range(PACK):
+            nc.scalar.activation(shift2[:, j, :], h_rows[:], ACT.Identity, bias=bias2[:, j : j + 1], scale=-2.0)
 
         picked = []
         for i in range(V // PIECE):
@@ -140,33 +138,32 @@ def tile_picked_ykrr_lin_po_kernel(
             nc.vector.tensor_copy(ew_g[:], ew[:].indirect(entries))
             picked.append(ew_g)
 
-        z2 = []
-        for i in range(V // PIECE):
-            cols = slice(i * PIECE, (i + 1) * PIECE)
-            ew_g = picked[i]
-            z2_i = keep.tile([P, PACK, PIECE], F32, name="z2_%d" % i)
-            for jj in range(PACK // 2):
-                s_ps = ps_s.tile([P, 2, PIECE], F32, name="s_ps")
-                for u in range(2):
-                    j = 2 * jj + u
-                    nc.tensor.matmul_mx(
-                        s_ps[:, u, :],
-                        lhsT=xw_d[:, j * P : (j + 1) * P].bitcast(FP8X4),
-                        lhsT_scale=xs_d[:, j * P : (j + 1) * P],
-                        rhs=ew_g[:].bitcast(FP8X4),
-                        rhs_scale=es_g[:, cols],
-                        start=True,
-                        stop=True,
-                    )
-                for u in range(2):
-                    j = 2 * jj + u
-                    nc.vector.scalar_tensor_tensor(
-                        z2_i[:, j, :], s_ps[:, u, :], bias2[:, j : j + 1], h2[:, cols], ALU.add, ALU.add
-                    )
-            z2.append(z2_i)
+        y_codes = keep.tile([P, V], U32, name="y_codes", align_bytes=64)
+        y_scales = keep.tile([P, V], U8, name="y_scales", align_bytes=64)
+        out_rows = out_0.rearrange("(p r) v -> p r v", r=PACK)
+        out_words = out_1[0].rearrange("p n r -> p (n r)").bitcast(I32)
+
+        z2 = keep.tile([P, PACK, V], F32, name="z2")
+        for c in range(CHUNKS):
+            cols = slice(c * CHUNK, (c + 1) * CHUNK)
+            i, within = divmod(c * CHUNK, PIECE)
+            s_ps = ps_s.tile([P, PACK, CHUNK], F32, name="s_ps")
+            for j in range(PACK):
+                nc.tensor.matmul_mx(
+                    s_ps[:, j, :],
+                    lhsT=xw_d[:, j * P : (j + 1) * P].bitcast(FP8X4),
+                    lhsT_scale=xs_d[:, j * P : (j + 1) * P],
+                    rhs=picked[i][:, within : within + CHUNK].bitcast(FP8X4),
+                    rhs_scale=es_g[:, cols],
+                    start=True,
+                    stop=True,
+                )
+            nc.vector.tensor_tensor(z2[:, :, cols], s_ps[:], shift2[:, :, cols], ALU.add)
 
         dual_bf = keep.tile([P, PACK, P, PACK], BF16, name="dual_bf", align_bytes=64)
-        for h, copy in enumerate((nc.scalar.copy, nc.scalar.copy)):
+        for h, copy in enumerate(
+            (nc.scalar.copy, nc.scalar.copy)
+        ):
             copy(
                 dual_bf[:, :, h * P // 2 : (h + 1) * P // 2, :].rearrange("p r c j -> p c j r"),
                 dual_sb[h][:].rearrange("p j (c r) -> p c j r", r=PACK),
@@ -175,65 +172,68 @@ def tile_picked_ykrr_lin_po_kernel(
         d_scales = keep.tile([P, N], U8, name="d_scales", align_bytes=64)
         nc.vector.quantize_mx(d_codes[:].bitcast(FP8X4), d_scales[:], dual_bf[:].rearrange("p r c j -> p (r c j)"))
 
-        y_banks = []
-        for c in range(CHUNKS):
-            i, within = divmod(c * CHUNK, PIECE)
-            local = slice(within, within + CHUNK)
-            ee = ring.tile([P, CHUNK, PACK], BF16, name="ee")
+        stages = []
+        for first, width in STAGES:
+            cols = slice(first, first + width)
+            ee = keep.tile([P, width, PACK], BF16, name="ee%d" % first)
             nc.scalar.activation(
-                ee[:].rearrange("p (c i) j -> p c j i", i=PACK),
-                z2[i][:, :, local].rearrange("p j (c i) -> p c j i", i=PACK),
+                ee[:].rearrange("p (g i) j -> p g j i", i=PACK),
+                z2[:, :, cols].rearrange("p j (g i) -> p g j i", i=PACK),
                 ACT.Exp,
                 scale=0.5,
             )
-            a_bf = ring.tile([P, CHUNK, PACK], BF16, name="a_bf", align_bytes=64)
+            a_bf = keep.tile([P, width, PACK], BF16, name="a_bf%d" % first, align_bytes=64)
             nc.vector.tensor_tensor(
                 a_bf[:].rearrange("p (g n) j -> p g (n j)", n=UNIT),
                 ee[:].rearrange("p (g n) j -> p g (n j)", n=UNIT),
-                unit[:].rearrange("p n j -> p (n j)").unsqueeze(1).to_broadcast([P, CHUNK // UNIT, UNIT * PACK]),
+                unit[:].rearrange("p n j -> p (n j)").unsqueeze(1).to_broadcast([P, width // UNIT, UNIT * PACK]),
                 ALU.mult,
             )
-            a_codes = ring.tile([P, CHUNK], U32, name="a_codes", align_bytes=64)
-            a_scales = ring.tile([P, CHUNK], U8, name="a_scales", align_bytes=64)
+            a_codes = keep.tile([P, width], U32, name="a_codes%d" % first, align_bytes=64)
+            a_scales = keep.tile([P, width], U8, name="a_scales%d" % first, align_bytes=64)
             nc.vector.quantize_mx(a_codes[:].bitcast(FP8X4), a_scales[:], a_bf[:].rearrange("p n j -> p (n j)"))
 
-            y_ps = ps_y.tile([P, PACK, CHUNK], F32, name="y_ps")
-            for r in range(PACK):
-                nc.tensor.matmul_mx(
-                    y_ps[:, r, :],
-                    lhsT=d_codes[:, r * P : (r + 1) * P].bitcast(FP8X4),
-                    lhsT_scale=d_scales[:, r * P : (r + 1) * P],
-                    rhs=a_codes[:].bitcast(FP8X4),
-                    rhs_scale=a_scales[:],
-                    start=True,
-                    stop=True,
-                )
-            y_banks.append(y_ps)
+            banks = []
+            for r0 in range(0, PACK, min(PACK, BANK // width)):
+                y_ps = ps_y.tile([P, min(PACK, BANK // width), width], F32, name="y_ps")
+                for r in range(r0, r0 + min(PACK, BANK // width)):
+                    nc.tensor.matmul_mx(
+                        y_ps[:, r - r0, :],
+                        lhsT=d_codes[:, r * P : (r + 1) * P].bitcast(FP8X4),
+                        lhsT_scale=d_scales[:, r * P : (r + 1) * P],
+                        rhs=a_codes[:].bitcast(FP8X4),
+                        rhs_scale=a_scales[:],
+                        start=True,
+                        stop=True,
+                    )
+                banks.append((r0, y_ps))
+            stages.append((cols, width, banks))
 
-        for c, y_ps in enumerate(y_banks):
-            cols = slice(c * CHUNK, (c + 1) * CHUNK)
-            y = ring.tile([P, PACK, CHUNK], F32, name="y")
-            y_bf = ring.tile([P, CHUNK, PACK], BF16, name="y_bf", align_bytes=64)
-            if c < CHUNKS - 1:
-                nc.scalar.copy(y[:], y_ps[:])
+        for s, (cols, width, banks) in enumerate(stages):
+            y = keep.tile([P, PACK, width], F32, name="y%d" % s)
+            y_bf = keep.tile([P, width, PACK], BF16, name="y_bf%d" % s, align_bytes=64)
+            last = s == len(stages) - 1
+            if last:
+                nc.vector.tensor_copy(y_bf[:], banks[0][1][:].rearrange("p r n -> p n r"))
+            for r0, y_ps in banks:
+                rows = slice(r0, r0 + y_ps.shape[1])
+                nc.scalar.copy(y[:, rows, :], y_ps[:])
+                queue = nc.scalar if last else nc.sync
+                queue.dma_start(out_rows[:, rows, cols], y[:, rows, :])
+            if not last:
                 nc.vector.tensor_copy(
-                    y_bf[:].rearrange("p (c i) r -> p c r i", i=PACK), y[:].rearrange("p r (c i) -> p c r i", i=PACK)
+                    y_bf[:].rearrange("p (g i) r -> p g r i", i=PACK), y[:].rearrange("p r (g i) -> p g r i", i=PACK)
                 )
-            else:
-                nc.vector.tensor_copy(y_bf[:], y_ps[:].rearrange("p r n -> p n r"))
-                nc.scalar.copy(y[:], y_ps[:])
-            queue = nc.scalar if c == CHUNKS - 1 else nc.sync
-            queue.dma_start(out_rows[:, :, cols], y[:])
             nc.vector.quantize_mx(
                 y_codes[:, cols].bitcast(FP8X4), y_scales[:, cols], y_bf[:].rearrange("p n r -> p (n r)")
             )
-
-            if c >= CHUNKS - 2:
-                done = slice(0, (c + 1) * CHUNK) if c == CHUNKS - 2 else cols
-                nc.sync.dma_start(out_words[:, done], y_codes[:, done].bitcast(I32))
-
+            if s == 1:
+                nc.sync.dma_start(out_words[:, : V // 2], y_codes[:, : V // 2].bitcast(I32))
+        rest = slice(V // 2, V)
+        nc.sync.dma_start(out_words[:, rest], y_codes[:, rest].bitcast(I32))
         for q in range(QUADS):
-            nc.sync.dma_start(
+            queue = nc.scalar if q % 2 else nc.sync
+            queue.dma_start(
                 out_2[0, SCALE_ROWS * q : SCALE_ROWS * (q + 1), :].bitcast(I32),
                 y_scales[QUAD * q : QUAD * q + SCALE_ROWS, :].bitcast(I32),
             )

@@ -28,7 +28,7 @@ SCALE_ROWS = 4
 LIST_ROWS = 16
 CHUNK = 128
 CHUNKS = V // CHUNK
-UNIT = 8
+LN_RANGE = 2.0**63
 BANK = 512
 STAGES = ((0, 128), (128, 128), (256, 128), (384, 64), (448, 64))
 PIECE = 256
@@ -40,14 +40,13 @@ def tile_picked_ykrr_lin_po_kernel(
     nc = tc.nc
     with ExitStack() as ctx:
         keep = ctx.enter_context(tc.tile_pool(name="keep", bufs=1))
-        ring = ctx.enter_context(tc.tile_pool(name="ring", bufs=CHUNKS))
         ps_s = ctx.enter_context(tc.psum_pool(name="ps_s", bufs=CHUNKS))
         ps_y = ctx.enter_context(tc.psum_pool(name="ps_y", bufs=CHUNKS))
 
         offs_sb = keep.tile([P, S // LIST_ROWS], U16, name="offs_sb")
         qry_sb = keep.tile([P, V // LIST_ROWS], U16, name="qry_sb")
         xw = keep.tile([P, STORE], U32, name="xw")
-        ew = keep.tile([P, STORE], U32, name="ew")
+        ew = keep.tile([P, STORE], U32, name="ew", tag="ew", align_bytes=64)
         xs = keep.tile([P, STORE], U8, name="xs")
         es = keep.tile([P, STORE], U8, name="es")
         hw = keep.tile([P, STORE], F32, name="hw")
@@ -56,67 +55,63 @@ def tile_picked_ykrr_lin_po_kernel(
         ident = keep.tile([P, P], F32, name="ident")
 
         nc.gpsimd.memset(xs[:].bitcast(I32), 0)
+        nc.gpsimd.memset(es[:].bitcast(I32), 0)
         nc.vector.memset(hw[: P - 1, : STORE // 2].bitcast(I32), 0)
         nc.gpsimd.memset(hw[: P - 1, STORE // 2 :].bitcast(I32), 0)
         make_identity(nc, ident[:])
 
+        def load_scales(plane, scales):
+            for q in range(QUADS):
+                nc.sync.dma_start(
+                    plane[QUAD * q : QUAD * q + SCALE_ROWS, :].bitcast(I32),
+                    scales[0, SCALE_ROWS * q : SCALE_ROWS * (q + 1), :].bitcast(I32),
+                )
+
+        dual_sb = keep.tile([P, PACK, N], F32, name="dual_sb")
         nc.sync.dma_start(wgt_sb[:], wgt.rearrange("(p j) o -> p (j o)", j=PACK))
         nc.sync.dma_start(qry_sb[:], qry)
         nc.sync.dma_start(hw[P - 1 :, :], half[:1, :])
-        for q in range(QUADS):
-            rows = e_scales[0, SCALE_ROWS * q : SCALE_ROWS * (q + 1), :].bitcast(I32)
-            nc.sync.dma_start(
-                es[QUAD * q : QUAD * (q + 1), :].bitcast(I32),
-                rows.unsqueeze(0).to_broadcast([QUAD // SCALE_ROWS, SCALE_ROWS, STORE // 4]),
-            )
-        nc.sync.dma_start(xw[:].bitcast(I32), x_words[0].rearrange("p n r -> p (n r)").bitcast(I32))
+        nc.sync.dma_start(dual_sb[:], dual.rearrange("(p j) m -> p j m", j=PACK))
+        load_scales(xs, x_scales)
         nc.sync.dma_start(offs_sb[:], offs)
+        nc.sync.dma_start(xw[:].bitcast(I32), x_words[0].rearrange("p n r -> p (n r)").bitcast(I32))
         nc.sync.dma_start(own_sb[:], own.rearrange("(p j) o -> p (j o)", j=PACK))
-        for q in range(QUADS):
-            nc.sync.dma_start(
-                xs[QUAD * q : QUAD * q + SCALE_ROWS, :].bitcast(I32),
-                x_scales[0, SCALE_ROWS * q : SCALE_ROWS * (q + 1), :].bitcast(I32),
-            )
+        load_scales(es, e_scales)
         nc.sync.dma_start(ew[:].bitcast(I32), e_words[0].rearrange("p n r -> p (n r)").bitcast(I32))
-        dual_rows = dual.rearrange("(p j) m -> p j m", j=PACK)
-        dual_sb = []
-        for h in range(2):
-            part = keep.tile([P, PACK, N // 2], F32, name="dual_sb%d" % h)
-            nc.sync.dma_start(part[:], dual_rows[:, :, h * N // 2 : (h + 1) * N // 2])
-            dual_sb.append(part)
 
-        square = keep.tile([P, PACK], F32, name="square")
+        size = keep.tile([P, PACK], F32, name="size")
+        nc.vector.scalar_tensor_tensor(size[:], wgt_sb[:], -1.0, wgt_sb[:], ALU.mult, ALU.max)
+        capped = keep.tile([P, PACK], F32, name="capped")
+        nc.vector.tensor_scalar(capped[:], wgt_sb[:], LN_RANGE, 1.0, ALU.mult, ALU.min)
         held = keep.tile([P, PACK], F32, name="held")
-        nc.vector.tensor_tensor(square[:], wgt_sb[:], wgt_sb[:], ALU.mult)
-        nc.vector.tensor_scalar(held[:], square[:], 2.0**-64, 2.0**63, ALU.max, ALU.min)
+        nc.vector.tensor_scalar(held[:], size[:], 1.0 / LN_RANGE, LN_RANGE, ALU.max, ALU.min)
+        excess = keep.tile([P, PACK], F32, name="excess")
+        nc.vector.tensor_scalar(excess[:], size[:], 1.0 / LN_RANGE, 1.0, ALU.mult, ALU.max)
+        unit = keep.tile([P, PACK], F32, name="unit")
+        nc.vector.scalar_tensor_tensor(unit[:], capped[:], -1.0, excess[:], ALU.max, ALU.mult)
         ln_held = keep.tile([P, PACK], F32, name="ln_held")
         nc.scalar.activation(ln_held[:], held[:], ACT.Ln)
-        inv_size = keep.tile([P, PACK], F32, name="inv_size")
-        nc.scalar.activation(inv_size[:], ln_held[:], ACT.Exp, scale=-0.5)
-        own2 = keep.tile([P, PACK], F32, name="own2")
-        nc.gpsimd.tensor_tensor(own2[:], own_sb[:], own_sb[:], ALU.add)
+        bias = keep.tile([P, PACK], F32, name="bias")
+        nc.gpsimd.tensor_tensor(bias[:], ln_held[:], own_sb[:], ALU.add)
         bias2 = keep.tile([P, PACK], F32, name="bias2")
-        nc.gpsimd.tensor_tensor(bias2[:], ln_held[:], own2[:], ALU.add)
-        unit = keep.tile([P, UNIT, PACK], BF16, name="unit")
-        nc.gpsimd.tensor_tensor(
-            unit[:],
-            wgt_sb[:].unsqueeze(1).to_broadcast([P, UNIT, PACK]),
-            inv_size[:].unsqueeze(1).to_broadcast([P, UNIT, PACK]),
-            ALU.mult,
-        )
+        nc.gpsimd.tensor_tensor(bias2[:], bias[:], bias[:], ALU.add)
+
+        dual_r = keep.tile([P, PACK, N], BF16, name="dual_r")
+        for j in range(PACK):
+            nc.scalar.activation(dual_r[:, j, :], dual_sb[:, j, :], ACT.Copy, scale=unit[:, j : j + 1])
 
         hg = keep.tile([P, V], F32, name="hg")
         nc.vector.tensor_copy(hg[:], hw[:].indirect(qry_sb[:]))
-        es_g = keep.tile([P, V], U8, name="es_g", align_bytes=64)
-        nc.vector.tensor_copy(es_g[:], es[:].indirect(qry_sb[:]))
-        xw_d = keep.tile([P, S], U32, name="xw_d", align_bytes=64)
-        nc.vector.tensor_copy(xw_d[:].rearrange("k (j p) -> k p j", j=PACK), xw[:].indirect(offs_sb[:]))
         xs_g = keep.tile([P, S], U8, name="xs_g")
         nc.vector.tensor_copy(xs_g[:], xs[:].indirect(offs_sb[:]))
         xs_d = keep.tile([P, S], U8, name="xs_d", align_bytes=64)
         nc.vector.tensor_copy(
             xs_d[:].rearrange("k (j p) -> k p j", j=PACK), xs_g[:].rearrange("k (p j) -> k p j", j=PACK)
         )
+        xw_d = keep.tile([P, S], U32, name="xw_d", align_bytes=64)
+        nc.vector.tensor_copy(xw_d[:].rearrange("k (j p) -> k p j", j=PACK), xw[:].indirect(offs_sb[:]))
+        es_g = keep.tile([P, V], U8, name="es_g", align_bytes=64)
+        nc.vector.tensor_copy(es_g[:], es[:].indirect(qry_sb[:]))
 
         h_turned = ps_y.tile([P, V // P, P], F32, name="h_turned", tag="y_ps")
         for b in range(V // P):
@@ -127,9 +122,13 @@ def tile_picked_ykrr_lin_po_kernel(
         for b in range(V // P):
             nc.tensor.transpose(h_rows[:, b * P : (b + 1) * P], h_col[:, b : b + 1].to_broadcast([P, P]), ident[:])
 
-        shift2 = keep.tile([P, PACK, V], F32, name="shift2")
-        for j in range(PACK):
-            nc.scalar.activation(shift2[:, j, :], h_rows[:], ACT.Identity, bias=bias2[:, j : j + 1], scale=-2.0)
+        minus_half2 = keep.tile([P, V], F32, name="minus_half2")
+        nc.scalar.activation(minus_half2[:], h_rows[:], ACT.Copy, scale=-2.0)
+
+        dual_bf = keep.tile([P, PACK, P, PACK], BF16, name="dual_bf", align_bytes=64)
+        nc.scalar.copy(
+            dual_bf[:].rearrange("p r c j -> p c j r"), dual_r[:].rearrange("p j (c r) -> p c j r", r=PACK)
+        )
 
         picked = []
         for i in range(V // PIECE):
@@ -143,7 +142,7 @@ def tile_picked_ykrr_lin_po_kernel(
         out_rows = out_0.rearrange("(p r) v -> p r v", r=PACK)
         out_words = out_1[0].rearrange("p n r -> p (n r)").bitcast(I32)
 
-        z2 = keep.tile([P, PACK, V], F32, name="z2")
+        z2 = []
         for c in range(CHUNKS):
             cols = slice(c * CHUNK, (c + 1) * CHUNK)
             i, within = divmod(c * CHUNK, PIECE)
@@ -158,36 +157,26 @@ def tile_picked_ykrr_lin_po_kernel(
                     start=True,
                     stop=True,
                 )
-            nc.vector.tensor_tensor(z2[:, :, cols], s_ps[:], shift2[:, :, cols], ALU.add)
+            z_c = keep.tile([P, PACK, CHUNK], F32, name="z2_%d" % c)
+            z2.append(z_c)
+            for j in range(PACK):
+                nc.vector.scalar_tensor_tensor(
+                    z_c[:, j, :], s_ps[:, j, :], bias2[:, j : j + 1], minus_half2[:, cols], ALU.add, ALU.add
+                )
 
-        dual_bf = keep.tile([P, PACK, P, PACK], BF16, name="dual_bf", align_bytes=64)
-        for h, copy in enumerate(
-            (nc.scalar.copy, nc.scalar.copy)
-        ):
-            copy(
-                dual_bf[:, :, h * P // 2 : (h + 1) * P // 2, :].rearrange("p r c j -> p c j r"),
-                dual_sb[h][:].rearrange("p j (c r) -> p c j r", r=PACK),
-            )
-        d_codes = keep.tile([P, N], U32, name="d_codes", align_bytes=64)
+        d_codes = keep.tile([P, N], U32, name="d_codes", tag="ew", align_bytes=64)
         d_scales = keep.tile([P, N], U8, name="d_scales", align_bytes=64)
         nc.vector.quantize_mx(d_codes[:].bitcast(FP8X4), d_scales[:], dual_bf[:].rearrange("p r c j -> p (r c j)"))
 
         stages = []
         for first, width in STAGES:
             cols = slice(first, first + width)
-            ee = keep.tile([P, width, PACK], BF16, name="ee%d" % first)
+            a_bf = keep.tile([P, width, PACK], BF16, name="a_bf%d" % first, align_bytes=64)
             nc.scalar.activation(
-                ee[:].rearrange("p (g i) j -> p g j i", i=PACK),
-                z2[:, :, cols].rearrange("p j (g i) -> p g j i", i=PACK),
+                a_bf[:].rearrange("p (g i) j -> p g j i", i=PACK),
+                z2[first // CHUNK][:, :, first % CHUNK : first % CHUNK + width].rearrange("p j (g i) -> p g j i", i=PACK),
                 ACT.Exp,
                 scale=0.5,
-            )
-            a_bf = keep.tile([P, width, PACK], BF16, name="a_bf%d" % first, align_bytes=64)
-            nc.vector.tensor_tensor(
-                a_bf[:].rearrange("p (g n) j -> p g (n j)", n=UNIT),
-                ee[:].rearrange("p (g n) j -> p g (n j)", n=UNIT),
-                unit[:].rearrange("p n j -> p (n j)").unsqueeze(1).to_broadcast([P, width // UNIT, UNIT * PACK]),
-                ALU.mult,
             )
             a_codes = keep.tile([P, width], U32, name="a_codes%d" % first, align_bytes=64)
             a_scales = keep.tile([P, width], U8, name="a_scales%d" % first, align_bytes=64)
@@ -217,7 +206,7 @@ def tile_picked_ykrr_lin_po_kernel(
                 nc.vector.tensor_copy(y_bf[:], banks[0][1][:].rearrange("p r n -> p n r"))
             for r0, y_ps in banks:
                 rows = slice(r0, r0 + y_ps.shape[1])
-                nc.scalar.copy(y[:, rows, :], y_ps[:])
+                (nc.vector.tensor_copy if s == 0 else nc.scalar.copy)(y[:, rows, :], y_ps[:])
                 queue = nc.scalar if last else nc.sync
                 queue.dma_start(out_rows[:, rows, cols], y[:, rows, :])
             if not last:
@@ -227,10 +216,7 @@ def tile_picked_ykrr_lin_po_kernel(
             nc.vector.quantize_mx(
                 y_codes[:, cols].bitcast(FP8X4), y_scales[:, cols], y_bf[:].rearrange("p n r -> p (n r)")
             )
-            if s == 1:
-                nc.sync.dma_start(out_words[:, : V // 2], y_codes[:, : V // 2].bitcast(I32))
-        rest = slice(V // 2, V)
-        nc.sync.dma_start(out_words[:, rest], y_codes[:, rest].bitcast(I32))
+        nc.sync.dma_start(out_words, y_codes[:].bitcast(I32))
         for q in range(QUADS):
             queue = nc.scalar if q % 2 else nc.sync
             queue.dma_start(

@@ -143,7 +143,8 @@ def tile_picked_ykrr_lin_po_kernel(
         out_words = out_1[0].rearrange("p n r -> p (n r)").bitcast(I32)
 
         z2 = []
-        for c in range(CHUNKS):
+
+        def exponents(c):
             cols = slice(c * CHUNK, (c + 1) * CHUNK)
             i, within = divmod(c * CHUNK, PIECE)
             s_ps = ps_s.tile([P, PACK, CHUNK], F32, name="s_ps")
@@ -164,12 +165,9 @@ def tile_picked_ykrr_lin_po_kernel(
                     z_c[:, j, :], s_ps[:, j, :], bias2[:, j : j + 1], minus_half2[:, cols], ALU.add, ALU.add
                 )
 
-        d_codes = keep.tile([P, N], U32, name="d_codes", tag="ew", align_bytes=64)
-        d_scales = keep.tile([P, N], U8, name="d_scales", align_bytes=64)
-        nc.vector.quantize_mx(d_codes[:].bitcast(FP8X4), d_scales[:], dual_bf[:].rearrange("p r c j -> p (r c j)"))
-
         stages = []
-        for first, width in STAGES:
+
+        def kernels(first, width):
             cols = slice(first, first + width)
             a_bf = keep.tile([P, width, PACK], BF16, name="a_bf%d" % first, align_bytes=64)
             nc.scalar.activation(
@@ -198,6 +196,19 @@ def tile_picked_ykrr_lin_po_kernel(
                 banks.append((r0, y_ps))
             stages.append((cols, width, banks))
 
+        exponents(0)
+        d_codes = keep.tile([P, N], U32, name="d_codes", tag="ew", align_bytes=64)
+        d_scales = keep.tile([P, N], U8, name="d_scales", align_bytes=64)
+        nc.vector.quantize_mx(d_codes[:].bitcast(FP8X4), d_scales[:], dual_bf[:].rearrange("p r c j -> p (r c j)"))
+        exponents(1)
+        kernels(*STAGES[0])
+        exponents(2)
+        kernels(*STAGES[1])
+        exponents(3)
+        kernels(*STAGES[2])
+        kernels(*STAGES[3])
+        kernels(*STAGES[4])
+
         for s, (cols, width, banks) in enumerate(stages):
             y = keep.tile([P, PACK, width], F32, name="y%d" % s)
             y_bf = keep.tile([P, width, PACK], BF16, name="y_bf%d" % s, align_bytes=64)
@@ -206,7 +217,7 @@ def tile_picked_ykrr_lin_po_kernel(
                 nc.vector.tensor_copy(y_bf[:], banks[0][1][:].rearrange("p r n -> p n r"))
             for r0, y_ps in banks:
                 rows = slice(r0, r0 + y_ps.shape[1])
-                (nc.vector.tensor_copy if s == 0 else nc.scalar.copy)(y[:, rows, :], y_ps[:])
+                nc.scalar.copy(y[:, rows, :], y_ps[:])
                 queue = nc.scalar if last else nc.sync
                 queue.dma_start(out_rows[:, rows, cols], y[:, rows, :])
             if not last:

@@ -25,13 +25,14 @@ PACK = 4
 QUADS = 4
 QUAD = P // QUADS
 SCALE_ROWS = 4
+ROW_STEP = QUAD // SCALE_ROWS
 LIST_ROWS = 16
 CHUNK = 128
 CHUNKS = V // CHUNK
 LN_RANGE = 2.0**63
 BANK = 512
 STAGES = ((0, 128), (128, 128), (256, 128), (384, 64), (448, 64))
-PIECE = 256
+PIECES = ((0, CHUNK), (CHUNK, V - CHUNK))
 
 
 def tile_picked_ykrr_lin_po_kernel(
@@ -55,28 +56,34 @@ def tile_picked_ykrr_lin_po_kernel(
         ident = keep.tile([P, P], F32, name="ident")
 
         nc.gpsimd.memset(xs[:].bitcast(I32), 0)
-        nc.gpsimd.memset(es[:].bitcast(I32), 0)
+        nc.vector.memset(es[:].bitcast(I32), 0)
         nc.vector.memset(hw[: P - 1, : STORE // 2].bitcast(I32), 0)
         nc.gpsimd.memset(hw[: P - 1, STORE // 2 :].bitcast(I32), 0)
         make_identity(nc, ident[:])
 
         def load_scales(plane, scales):
-            for q in range(QUADS):
-                nc.sync.dma_start(
-                    plane[QUAD * q : QUAD * q + SCALE_ROWS, :].bitcast(I32),
-                    scales[0, SCALE_ROWS * q : SCALE_ROWS * (q + 1), :].bitcast(I32),
-                )
+            nc.sync.dma_start(plane[::ROW_STEP, :].bitcast(I32), scales[0].bitcast(I32))
 
-        dual_sb = keep.tile([P, PACK, N], F32, name="dual_sb")
+        def place_scales(spread, name):
+            plane = keep.tile([P, S], U8, name=name, align_bytes=64)
+            nc.vector.tensor_copy(plane[:].bitcast(I32), spread[:].bitcast(I32))
+            for i in range(1, SCALE_ROWS):
+                nc.sync.dma_start(plane[i::QUAD, :].bitcast(I32), spread[ROW_STEP * i :: QUAD, :].bitcast(I32))
+            return plane
+
+        dual_rows = dual.rearrange("(p j) m -> p j m", j=PACK)
+        dual_lo = keep.tile([P, PACK // 2, N], F32, name="dual_lo")
+        dual_hi = keep.tile([P, PACK // 2, N], F32, name="dual_hi")
         nc.sync.dma_start(wgt_sb[:], wgt.rearrange("(p j) o -> p (j o)", j=PACK))
         nc.sync.dma_start(qry_sb[:], qry)
         nc.sync.dma_start(hw[P - 1 :, :], half[:1, :])
-        nc.sync.dma_start(dual_sb[:], dual.rearrange("(p j) m -> p j m", j=PACK))
-        load_scales(xs, x_scales)
         nc.sync.dma_start(offs_sb[:], offs)
+        nc.sync.dma_start(dual_lo[:], dual_rows[:, : PACK // 2, :])
+        load_scales(xs, x_scales)
+        load_scales(es, e_scales)
+        nc.sync.dma_start(dual_hi[:], dual_rows[:, PACK // 2 :, :])
         nc.sync.dma_start(xw[:].bitcast(I32), x_words[0].rearrange("p n r -> p (n r)").bitcast(I32))
         nc.sync.dma_start(own_sb[:], own.rearrange("(p j) o -> p (j o)", j=PACK))
-        load_scales(es, e_scales)
         nc.sync.dma_start(ew[:].bitcast(I32), e_words[0].rearrange("p n r -> p (n r)").bitcast(I32))
 
         size = keep.tile([P, PACK], F32, name="size")
@@ -96,22 +103,23 @@ def tile_picked_ykrr_lin_po_kernel(
         bias2 = keep.tile([P, PACK], F32, name="bias2")
         nc.gpsimd.tensor_tensor(bias2[:], bias[:], bias[:], ALU.add)
 
-        dual_r = keep.tile([P, PACK, N], BF16, name="dual_r")
-        for j in range(PACK):
-            nc.scalar.activation(dual_r[:, j, :], dual_sb[:, j, :], ACT.Copy, scale=unit[:, j : j + 1])
-
         hg = keep.tile([P, V], F32, name="hg")
         nc.vector.tensor_copy(hg[:], hw[:].indirect(qry_sb[:]))
-        xs_g = keep.tile([P, S], U8, name="xs_g")
-        nc.vector.tensor_copy(xs_g[:], xs[:].indirect(offs_sb[:]))
-        xs_d = keep.tile([P, S], U8, name="xs_d", align_bytes=64)
-        nc.vector.tensor_copy(
-            xs_d[:].rearrange("k (j p) -> k p j", j=PACK), xs_g[:].rearrange("k (p j) -> k p j", j=PACK)
-        )
+        xs_dealt = keep.tile([P, S], U8, name="xs_dealt")
+        nc.vector.tensor_copy(xs_dealt[:].rearrange("k (j p) -> k p j", j=PACK), xs[:].indirect(offs_sb[:]))
+        xs_d = place_scales(xs_dealt, "xs_d")
+
+        dual_r = keep.tile([P, PACK, N], BF16, name="dual_r", tag="dual_r")
+        for j in range(PACK // 2):
+            nc.scalar.activation(dual_r[:, j, :], dual_lo[:, j, :], ACT.Copy, scale=unit[:, j : j + 1])
+        for j in range(PACK // 2, PACK):
+            nc.scalar.activation(dual_r[:, j, :], dual_hi[:, j - PACK // 2, :], ACT.Copy, scale=unit[:, j : j + 1])
+
+        es_spread = keep.tile([P, V], U8, name="es_spread")
+        nc.vector.tensor_copy(es_spread[:], es[:].indirect(qry_sb[:]))
+        es_g = place_scales(es_spread, "es_g")
         xw_d = keep.tile([P, S], U32, name="xw_d", align_bytes=64)
         nc.vector.tensor_copy(xw_d[:].rearrange("k (j p) -> k p j", j=PACK), xw[:].indirect(offs_sb[:]))
-        es_g = keep.tile([P, V], U8, name="es_g", align_bytes=64)
-        nc.vector.tensor_copy(es_g[:], es[:].indirect(qry_sb[:]))
 
         h_turned = ps_y.tile([P, V // P, P], F32, name="h_turned", tag="y_ps")
         for b in range(V // P):
@@ -122,20 +130,24 @@ def tile_picked_ykrr_lin_po_kernel(
         for b in range(V // P):
             nc.tensor.transpose(h_rows[:, b * P : (b + 1) * P], h_col[:, b : b + 1].to_broadcast([P, P]), ident[:])
 
-        minus_half2 = keep.tile([P, V], F32, name="minus_half2")
-        nc.scalar.activation(minus_half2[:], h_rows[:], ACT.Copy, scale=-2.0)
-
         dual_bf = keep.tile([P, PACK, P, PACK], BF16, name="dual_bf", align_bytes=64)
-        nc.scalar.copy(
-            dual_bf[:].rearrange("p r c j -> p c j r"), dual_r[:].rearrange("p j (c r) -> p c j r", r=PACK)
-        )
+        for c0, c1, copy in ((0, 3 * QUAD, nc.scalar.copy), (3 * QUAD, P, nc.vector.tensor_copy)):
+            copy(
+                dual_bf[:, :, c0:c1, :].rearrange("p r c j -> p c j r"),
+                dual_r[:, :, PACK * c0 : PACK * c1].rearrange("p j (c r) -> p c j r", r=PACK),
+            )
+        minus_half2 = keep.tile([P, V], F32, name="minus_half2", tag="dual_r")
+        nc.scalar.activation(minus_half2[:], h_rows[:], ACT.Copy, scale=-2.0)
+        d_codes = keep.tile([P, N], U32, name="d_codes", align_bytes=64)
+        d_scales = keep.tile([P, N], U8, name="d_scales", align_bytes=64)
+        nc.vector.quantize_mx(d_codes[:].bitcast(FP8X4), d_scales[:], dual_bf[:].rearrange("p r c j -> p (r c j)"))
 
         picked = []
-        for i in range(V // PIECE):
-            entries = qry_sb[:, i * PIECE // LIST_ROWS : (i + 1) * PIECE // LIST_ROWS]
-            ew_g = keep.tile([P, PIECE], U32, name="ew_g%d" % i, align_bytes=64)
+        for first, width in PIECES:
+            entries = qry_sb[:, first // LIST_ROWS : (first + width) // LIST_ROWS]
+            ew_g = keep.tile([P, width], U32, name="ew_g%d" % first, align_bytes=64)
             nc.vector.tensor_copy(ew_g[:], ew[:].indirect(entries))
-            picked.append(ew_g)
+            picked.extend(ew_g[:, c : c + CHUNK] for c in range(0, width, CHUNK))
 
         y_codes = keep.tile([P, V], U32, name="y_codes", align_bytes=64)
         y_scales = keep.tile([P, V], U8, name="y_scales", align_bytes=64)
@@ -146,14 +158,13 @@ def tile_picked_ykrr_lin_po_kernel(
 
         def exponents(c):
             cols = slice(c * CHUNK, (c + 1) * CHUNK)
-            i, within = divmod(c * CHUNK, PIECE)
             s_ps = ps_s.tile([P, PACK, CHUNK], F32, name="s_ps")
             for j in range(PACK):
                 nc.tensor.matmul_mx(
                     s_ps[:, j, :],
                     lhsT=xw_d[:, j * P : (j + 1) * P].bitcast(FP8X4),
                     lhsT_scale=xs_d[:, j * P : (j + 1) * P],
-                    rhs=picked[i][:, within : within + CHUNK].bitcast(FP8X4),
+                    rhs=picked[c].bitcast(FP8X4),
                     rhs_scale=es_g[:, cols],
                     start=True,
                     stop=True,
@@ -197,9 +208,6 @@ def tile_picked_ykrr_lin_po_kernel(
             stages.append((cols, width, banks))
 
         exponents(0)
-        d_codes = keep.tile([P, N], U32, name="d_codes", tag="ew", align_bytes=64)
-        d_scales = keep.tile([P, N], U8, name="d_scales", align_bytes=64)
-        nc.vector.quantize_mx(d_codes[:].bitcast(FP8X4), d_scales[:], dual_bf[:].rearrange("p r c j -> p (r c j)"))
         exponents(1)
         kernels(*STAGES[0])
         exponents(2)

@@ -30,7 +30,6 @@ LIST_ROWS = 16
 CHUNK = 128
 CHUNKS = V // CHUNK
 LN_RANGE = 2.0**63
-BANK = 512
 STAGES = ((0, 128), (128, 128), (256, 128), (384, 64), (448, 64))
 PIECES = ((0, CHUNK), (CHUNK, V - CHUNK))
 
@@ -83,8 +82,8 @@ def tile_picked_ykrr_lin_po_kernel(
         load_scales(es, e_scales)
         nc.sync.dma_start(dual_hi[:], dual_rows[:, PACK // 2 :, :])
         nc.sync.dma_start(xw[:].bitcast(I32), x_words[0].rearrange("p n r -> p (n r)").bitcast(I32))
-        nc.sync.dma_start(own_sb[:], own.rearrange("(p j) o -> p (j o)", j=PACK))
         nc.sync.dma_start(ew[:].bitcast(I32), e_words[0].rearrange("p n r -> p (n r)").bitcast(I32))
+        nc.sync.dma_start(own_sb[:], own.rearrange("(p j) o -> p (j o)", j=PACK))
 
         size = keep.tile([P, PACK], F32, name="size")
         nc.vector.scalar_tensor_tensor(size[:], wgt_sb[:], -1.0, wgt_sb[:], ALU.mult, ALU.max)
@@ -109,7 +108,7 @@ def tile_picked_ykrr_lin_po_kernel(
         nc.vector.tensor_copy(xs_dealt[:].rearrange("k (j p) -> k p j", j=PACK), xs[:].indirect(offs_sb[:]))
         xs_d = place_scales(xs_dealt, "xs_d")
 
-        dual_r = keep.tile([P, PACK, N], BF16, name="dual_r", tag="dual_r")
+        dual_r = keep.tile([P, PACK, N], BF16, name="dual_r")
         for j in range(PACK // 2):
             nc.scalar.activation(dual_r[:, j, :], dual_lo[:, j, :], ACT.Copy, scale=unit[:, j : j + 1])
         for j in range(PACK // 2, PACK):
@@ -136,7 +135,7 @@ def tile_picked_ykrr_lin_po_kernel(
                 dual_bf[:, :, c0:c1, :].rearrange("p r c j -> p c j r"),
                 dual_r[:, :, PACK * c0 : PACK * c1].rearrange("p j (c r) -> p c j r", r=PACK),
             )
-        minus_half2 = keep.tile([P, V], F32, name="minus_half2", tag="dual_r")
+        minus_half2 = keep.tile([P, V], F32, name="minus_half2")
         nc.scalar.activation(minus_half2[:], h_rows[:], ACT.Copy, scale=-2.0)
         d_codes = keep.tile([P, N], U32, name="d_codes", align_bytes=64)
         d_scales = keep.tile([P, N], U8, name="d_scales", align_bytes=64)
@@ -158,10 +157,12 @@ def tile_picked_ykrr_lin_po_kernel(
 
         def exponents(c):
             cols = slice(c * CHUNK, (c + 1) * CHUNK)
-            s_ps = ps_s.tile([P, PACK, CHUNK], F32, name="s_ps")
+            s_lo = ps_s.tile([P, PACK, CHUNK], F32, name="s_ps")
+            s_hi = ps_y.tile([P, PACK, CHUNK], F32, name="s_hi", tag="y_ps") if c == 0 else s_lo
+            s_ps = (s_lo, s_lo, s_hi, s_hi)
             for j in range(PACK):
                 nc.tensor.matmul_mx(
-                    s_ps[:, j, :],
+                    s_ps[j][:, j, :],
                     lhsT=xw_d[:, j * P : (j + 1) * P].bitcast(FP8X4),
                     lhsT_scale=xs_d[:, j * P : (j + 1) * P],
                     rhs=picked[c].bitcast(FP8X4),
@@ -173,7 +174,7 @@ def tile_picked_ykrr_lin_po_kernel(
             z2.append(z_c)
             for j in range(PACK):
                 nc.vector.scalar_tensor_tensor(
-                    z_c[:, j, :], s_ps[:, j, :], bias2[:, j : j + 1], minus_half2[:, cols], ALU.add, ALU.add
+                    z_c[:, j, :], s_ps[j][:, j, :], bias2[:, j : j + 1], minus_half2[:, cols], ALU.add, ALU.add
                 )
 
         stages = []
@@ -191,21 +192,53 @@ def tile_picked_ykrr_lin_po_kernel(
             a_scales = keep.tile([P, width], U8, name="a_scales%d" % first, align_bytes=64)
             nc.vector.quantize_mx(a_codes[:].bitcast(FP8X4), a_scales[:], a_bf[:].rearrange("p n j -> p (n j)"))
 
-            banks = []
-            for r0 in range(0, PACK, min(PACK, BANK // width)):
-                y_ps = ps_y.tile([P, min(PACK, BANK // width), width], F32, name="y_ps")
-                for r in range(r0, r0 + min(PACK, BANK // width)):
-                    nc.tensor.matmul_mx(
-                        y_ps[:, r - r0, :],
-                        lhsT=d_codes[:, r * P : (r + 1) * P].bitcast(FP8X4),
-                        lhsT_scale=d_scales[:, r * P : (r + 1) * P],
-                        rhs=a_codes[:].bitcast(FP8X4),
-                        rhs_scale=a_scales[:],
-                        start=True,
-                        stop=True,
-                    )
-                banks.append((r0, y_ps))
-            stages.append((cols, width, banks))
+            y_ps = ps_y.tile([P, PACK, width], F32, name="y_ps")
+            for r in range(PACK):
+                nc.tensor.matmul_mx(
+                    y_ps[:, r, :],
+                    lhsT=d_codes[:, r * P : (r + 1) * P].bitcast(FP8X4),
+                    lhsT_scale=d_scales[:, r * P : (r + 1) * P],
+                    rhs=a_codes[:].bitcast(FP8X4),
+                    rhs_scale=a_scales[:],
+                    start=True,
+                    stop=True,
+                )
+            stages.append((cols, width, y_ps))
+
+        ys = []
+        y_bf = {}
+        for first, last in ((0, 1), (2, 2), (3, 4)):
+            start, stop = STAGES[first][0], sum(STAGES[last])
+            group = keep.tile([P, stop - start, PACK], BF16, name="y_bf%d" % first, align_bytes=64)
+            y_bf[first, last] = group[:]
+            for s in range(first, last + 1):
+                y_bf[s] = group[:, STAGES[s][0] - start : sum(STAGES[s]) - start, :]
+
+        def results(s):
+            cols, width, y_ps = stages[s]
+            y = keep.tile([P, PACK, width], F32, name="y%d" % s)
+            nc.scalar.copy(y[:], y_ps[:])
+            queue = nc.scalar if s == len(STAGES) - 1 else nc.sync
+            queue.dma_start(out_rows[:, :, cols], y[:])
+            ys.append(y)
+
+        def rounded(s):
+            cols, width, y_ps = stages[s]
+            if s == len(STAGES) - 1:
+                nc.scalar.copy(y_bf[s], y_ps[:].rearrange("p r n -> p n r"))
+                results(s)
+            else:
+                results(s)
+                nc.vector.tensor_copy(
+                    y_bf[s].rearrange("p (g i) r -> p g r i", i=PACK),
+                    ys[s][:].rearrange("p r (g i) -> p g r i", i=PACK),
+                )
+
+        def planes(first, last):
+            cols = slice(stages[first][0].start, stages[last][0].stop)
+            nc.vector.quantize_mx(
+                y_codes[:, cols].bitcast(FP8X4), y_scales[:, cols], y_bf[first, last].rearrange("p n r -> p (n r)")
+            )
 
         exponents(0)
         exponents(1)
@@ -216,25 +249,14 @@ def tile_picked_ykrr_lin_po_kernel(
         kernels(*STAGES[2])
         kernels(*STAGES[3])
         kernels(*STAGES[4])
-
-        for s, (cols, width, banks) in enumerate(stages):
-            y = keep.tile([P, PACK, width], F32, name="y%d" % s)
-            y_bf = keep.tile([P, width, PACK], BF16, name="y_bf%d" % s, align_bytes=64)
-            last = s == len(stages) - 1
-            if last:
-                nc.vector.tensor_copy(y_bf[:], banks[0][1][:].rearrange("p r n -> p n r"))
-            for r0, y_ps in banks:
-                rows = slice(r0, r0 + y_ps.shape[1])
-                nc.scalar.copy(y[:, rows, :], y_ps[:])
-                queue = nc.scalar if last else nc.sync
-                queue.dma_start(out_rows[:, rows, cols], y[:, rows, :])
-            if not last:
-                nc.vector.tensor_copy(
-                    y_bf[:].rearrange("p (g i) r -> p g r i", i=PACK), y[:].rearrange("p r (g i) -> p g r i", i=PACK)
-                )
-            nc.vector.quantize_mx(
-                y_codes[:, cols].bitcast(FP8X4), y_scales[:, cols], y_bf[:].rearrange("p n r -> p (n r)")
-            )
+        rounded(0)
+        rounded(1)
+        rounded(2)
+        planes(0, 1)
+        rounded(3)
+        planes(2, 2)
+        rounded(4)
+        planes(3, 4)
         nc.sync.dma_start(out_words, y_codes[:].bitcast(I32))
         for q in range(QUADS):
             queue = nc.scalar if q % 2 else nc.sync

@@ -217,7 +217,8 @@ def tile_picked_ykrr_lin_po_kernel(
         def results(s):
             cols, width, y_ps = stages[s]
             y = keep.tile([P, PACK, width], F32, name="y%d" % s)
-            nc.scalar.copy(y[:], y_ps[:])
+            copy = nc.vector.tensor_copy if s == 1 else nc.scalar.copy
+            copy(y[:], y_ps[:])
             queue = nc.scalar if s == len(STAGES) - 1 else nc.sync
             queue.dma_start(out_rows[:, :, cols], y[:])
             ys.append(y)

@@ -31,7 +31,7 @@ CHUNK = 128
 CHUNKS = V // CHUNK
 LN_RANGE = 2.0**63
 STAGES = ((0, 128), (128, 128), (256, 128), (384, 64), (448, 64))
-PIECES = ((0, CHUNK), (CHUNK, V - CHUNK))
+PIECES = ((0, CHUNK), (CHUNK, CHUNK), (2 * CHUNK, 2 * CHUNK))
 
 
 def tile_picked_ykrr_lin_po_kernel(
@@ -153,7 +153,7 @@ def tile_picked_ykrr_lin_po_kernel(
         out_rows = out_0.rearrange("(p r) v -> p r v", r=PACK)
         out_words = out_1[0].rearrange("p n r -> p (n r)").bitcast(I32)
 
-        z2 = []
+        z2 = {}
 
         def exponents(c):
             cols = slice(c * CHUNK, (c + 1) * CHUNK)
@@ -170,12 +170,20 @@ def tile_picked_ykrr_lin_po_kernel(
                     start=True,
                     stop=True,
                 )
-            z_c = keep.tile([P, PACK, CHUNK], F32, name="z2_%d" % c)
-            z2.append(z_c)
-            for j in range(PACK):
-                nc.vector.scalar_tensor_tensor(
-                    z_c[:, j, :], s_ps[j][:, j, :], bias2[:, j : j + 1], minus_half2[:, cols], ALU.add, ALU.add
-                )
+            for first, width in STAGES:
+                if first // CHUNK == c:
+                    part = slice(first % CHUNK, first % CHUNK + width)
+                    z = keep.tile([P, PACK, width], F32, name="z2_%d" % first)
+                    z2[first] = z
+                    for j in range(PACK):
+                        nc.vector.scalar_tensor_tensor(
+                            z[:, j, :],
+                            s_ps[j][:, j, part],
+                            bias2[:, j : j + 1],
+                            minus_half2[:, first : first + width],
+                            ALU.add,
+                            ALU.add,
+                        )
 
         stages = []
 
@@ -184,7 +192,7 @@ def tile_picked_ykrr_lin_po_kernel(
             a_bf = keep.tile([P, width, PACK], BF16, name="a_bf%d" % first, align_bytes=64)
             nc.scalar.activation(
                 a_bf[:].rearrange("p (g i) j -> p g j i", i=PACK),
-                z2[first // CHUNK][:, :, first % CHUNK : first % CHUNK + width].rearrange("p j (g i) -> p g j i", i=PACK),
+                z2[first][:].rearrange("p j (g i) -> p g j i", i=PACK),
                 ACT.Exp,
                 scale=0.5,
             )
@@ -229,7 +237,8 @@ def tile_picked_ykrr_lin_po_kernel(
                 nc.scalar.copy(y_bf[s], y_ps[:].rearrange("p r n -> p n r"))
                 results(s)
             else:
-                results(s)
+                if s > 0:
+                    results(s)
                 nc.vector.tensor_copy(
                     y_bf[s].rearrange("p (g i) r -> p g r i", i=PACK),
                     ys[s][:].rearrange("p r (g i) -> p g r i", i=PACK),
@@ -246,6 +255,7 @@ def tile_picked_ykrr_lin_po_kernel(
         kernels(*STAGES[0])
         exponents(2)
         kernels(*STAGES[1])
+        results(0)
         exponents(3)
         kernels(*STAGES[2])
         kernels(*STAGES[3])

@@ -30,7 +30,7 @@ LIST_ROWS = 16
 CHUNK = 128
 CHUNKS = V // CHUNK
 LN_RANGE = 2.0**63
-STAGES = ((0, 128), (128, 128), (256, 128), (384, 64), (448, 64))
+STAGES = ((0, 64), (64, 64), (128, 128), (256, 128), (384, 64), (448, 64))
 PIECES = ((0, CHUNK), (CHUNK, CHUNK), (2 * CHUNK, 2 * CHUNK))
 
 
@@ -215,7 +215,7 @@ def tile_picked_ykrr_lin_po_kernel(
 
         ys = []
         y_bf = {}
-        for first, last in ((0, 1), (2, 2), (3, 4)):
+        for first, last in ((0, 2), (3, 3), (4, 5)):
             start, stop = STAGES[first][0], sum(STAGES[last])
             group = keep.tile([P, stop - start, PACK], BF16, name="y_bf%d" % first, align_bytes=64)
             y_bf[first, last] = group[:]
@@ -225,7 +225,7 @@ def tile_picked_ykrr_lin_po_kernel(
         def results(s):
             cols, width, y_ps = stages[s]
             y = keep.tile([P, PACK, width], F32, name="y%d" % s)
-            copy = nc.vector.tensor_copy if s == 1 else nc.scalar.copy
+            copy = nc.vector.tensor_copy if s == 2 else nc.scalar.copy
             copy(y[:], y_ps[:])
             queue = nc.scalar if s == len(STAGES) - 1 else nc.sync
             queue.dma_start(out_rows[:, :, cols], y[:])
@@ -237,7 +237,7 @@ def tile_picked_ykrr_lin_po_kernel(
                 nc.scalar.copy(y_bf[s], y_ps[:].rearrange("p r n -> p n r"))
                 results(s)
             else:
-                if s > 0:
+                if s > 1:
                     results(s)
                 nc.vector.tensor_copy(
                     y_bf[s].rearrange("p (g i) r -> p g r i", i=PACK),
@@ -251,23 +251,26 @@ def tile_picked_ykrr_lin_po_kernel(
             )
 
         exponents(0)
-        exponents(1)
         kernels(*STAGES[0])
-        exponents(2)
+        exponents(1)
         kernels(*STAGES[1])
         results(0)
-        exponents(3)
+        exponents(2)
         kernels(*STAGES[2])
+        results(1)
+        exponents(3)
         kernels(*STAGES[3])
         kernels(*STAGES[4])
+        kernels(*STAGES[5])
         rounded(0)
         rounded(1)
         rounded(2)
-        planes(0, 1)
         rounded(3)
-        planes(2, 2)
+        planes(0, 2)
         rounded(4)
-        planes(3, 4)
+        planes(3, 3)
+        rounded(5)
+        planes(4, 5)
         nc.sync.dma_start(out_words, y_codes[:].bitcast(I32))
         for q in range(QUADS):
             queue = nc.scalar if q % 2 else nc.sync

@@ -30,8 +30,13 @@ LIST_ROWS = 16
 CHUNK = 128
 CHUNKS = V // CHUNK
 LN_RANGE = 2.0**63
-STAGES = ((0, 64), (64, 64), (128, 128), (256, 128), (384, 64), (448, 64))
 PIECES = ((0, CHUNK), (CHUNK, CHUNK), (2 * CHUNK, 2 * CHUNK))
+STAGES = ((0, 64), (64, 64), (128, 128), (256, 128), (384, 64), (448, 64))
+LAST = len(STAGES) - 1
+EARLY = 2
+BY_VECTOR = 2
+GROUPS = ((0, 2), (3, 3), (4, 5))
+BY_SCALAR = 96
 
 
 def tile_picked_ykrr_lin_po_kernel(
@@ -46,10 +51,10 @@ def tile_picked_ykrr_lin_po_kernel(
         offs_sb = keep.tile([P, S // LIST_ROWS], U16, name="offs_sb")
         qry_sb = keep.tile([P, V // LIST_ROWS], U16, name="qry_sb")
         xw = keep.tile([P, STORE], U32, name="xw")
-        ew = keep.tile([P, STORE], U32, name="ew", tag="ew", align_bytes=64)
+        ew = keep.tile([P, STORE], U32, name="ew", align_bytes=64)
         xs = keep.tile([P, STORE], U8, name="xs")
         es = keep.tile([P, STORE], U8, name="es")
-        hw = keep.tile([P, STORE], F32, name="hw")
+        hw = keep.tile([P, STORE], F32, name="hw", tag="hw")
         own_sb = keep.tile([P, PACK], F32, name="own_sb")
         wgt_sb = keep.tile([P, PACK], F32, name="wgt_sb")
         ident = keep.tile([P, P], F32, name="ident")
@@ -60,24 +65,24 @@ def tile_picked_ykrr_lin_po_kernel(
         nc.gpsimd.memset(hw[: P - 1, STORE // 2 :].bitcast(I32), 0)
         make_identity(nc, ident[:])
 
-        def load_scales(plane, scales):
-            nc.sync.dma_start(plane[::ROW_STEP, :].bitcast(I32), scales[0].bitcast(I32))
+        def load_scales(table, scales):
+            nc.sync.dma_start(table[::ROW_STEP, :].bitcast(I32), scales[0].bitcast(I32))
 
         def place_scales(spread, name):
-            plane = keep.tile([P, S], U8, name=name, align_bytes=64)
-            nc.vector.tensor_copy(plane[:].bitcast(I32), spread[:].bitcast(I32))
+            placed = keep.tile([P, S], U8, name=name, align_bytes=64)
+            nc.vector.tensor_copy(placed[:].bitcast(I32), spread[:].bitcast(I32))
             for i in range(1, SCALE_ROWS):
-                nc.sync.dma_start(plane[i::QUAD, :].bitcast(I32), spread[ROW_STEP * i :: QUAD, :].bitcast(I32))
-            return plane
+                nc.sync.dma_start(placed[i::QUAD, :].bitcast(I32), spread[ROW_STEP * i :: QUAD, :].bitcast(I32))
+            return placed
 
         dual_rows = dual.rearrange("(p j) m -> p j m", j=PACK)
         dual_lo = keep.tile([P, PACK // 2, N], F32, name="dual_lo")
         dual_hi = keep.tile([P, PACK // 2, N], F32, name="dual_hi")
-        nc.sync.dma_start(wgt_sb[:], wgt.rearrange("(p j) o -> p (j o)", j=PACK))
+        nc.scalar.dma_start(wgt_sb[:], wgt.rearrange("(p j) o -> p (j o)", j=PACK))
+        nc.scalar.dma_start(hw[P - 1 :, :], half[:1, :])
         nc.sync.dma_start(qry_sb[:], qry)
-        nc.sync.dma_start(hw[P - 1 :, :], half[:1, :])
-        nc.sync.dma_start(offs_sb[:], offs)
         nc.sync.dma_start(dual_lo[:], dual_rows[:, : PACK // 2, :])
+        nc.sync.dma_start(offs_sb[:], offs)
         load_scales(xs, x_scales)
         load_scales(es, e_scales)
         nc.sync.dma_start(dual_hi[:], dual_rows[:, PACK // 2 :, :])
@@ -104,15 +109,14 @@ def tile_picked_ykrr_lin_po_kernel(
 
         hg = keep.tile([P, V], F32, name="hg")
         nc.vector.tensor_copy(hg[:], hw[:].indirect(qry_sb[:]))
-        xs_dealt = keep.tile([P, S], U8, name="xs_dealt")
+        xs_dealt = keep.tile([P, S], U8, name="xs_dealt", tag="hw")
         nc.vector.tensor_copy(xs_dealt[:].rearrange("k (j p) -> k p j", j=PACK), xs[:].indirect(offs_sb[:]))
         xs_d = place_scales(xs_dealt, "xs_d")
 
         dual_r = keep.tile([P, PACK, N], BF16, name="dual_r")
-        for j in range(PACK // 2):
-            nc.scalar.activation(dual_r[:, j, :], dual_lo[:, j, :], ACT.Copy, scale=unit[:, j : j + 1])
-        for j in range(PACK // 2, PACK):
-            nc.scalar.activation(dual_r[:, j, :], dual_hi[:, j - PACK // 2, :], ACT.Copy, scale=unit[:, j : j + 1])
+        for j in range(PACK):
+            rows = (dual_lo, dual_hi)[j // 2][:, j % 2, :]
+            nc.scalar.activation(dual_r[:, j, :], rows, ACT.Copy, scale=unit[:, j : j + 1])
 
         es_spread = keep.tile([P, V], U8, name="es_spread")
         nc.vector.tensor_copy(es_spread[:], es[:].indirect(qry_sb[:]))
@@ -130,7 +134,7 @@ def tile_picked_ykrr_lin_po_kernel(
             nc.tensor.transpose(h_rows[:, b * P : (b + 1) * P], h_col[:, b : b + 1].to_broadcast([P, P]), ident[:])
 
         dual_bf = keep.tile([P, PACK, P, PACK], BF16, name="dual_bf", align_bytes=64)
-        for c0, c1, copy in ((0, 3 * QUAD, nc.scalar.copy), (3 * QUAD, P, nc.vector.tensor_copy)):
+        for c0, c1, copy in ((0, BY_SCALAR, nc.scalar.copy), (BY_SCALAR, P, nc.vector.tensor_copy)):
             copy(
                 dual_bf[:, :, c0:c1, :].rearrange("p r c j -> p c j r"),
                 dual_r[:, :, PACK * c0 : PACK * c1].rearrange("p j (c r) -> p c j r", r=PACK),
@@ -187,7 +191,8 @@ def tile_picked_ykrr_lin_po_kernel(
 
         stages = []
 
-        def kernels(first, width):
+        def kernels(s):
+            first, width = STAGES[s]
             cols = slice(first, first + width)
             a_bf = keep.tile([P, width, PACK], BF16, name="a_bf%d" % first, align_bytes=64)
             nc.scalar.activation(
@@ -214,63 +219,54 @@ def tile_picked_ykrr_lin_po_kernel(
             stages.append((cols, width, y_ps))
 
         ys = []
-        y_bf = {}
-        for first, last in ((0, 2), (3, 3), (4, 5)):
-            start, stop = STAGES[first][0], sum(STAGES[last])
-            group = keep.tile([P, stop - start, PACK], BF16, name="y_bf%d" % first, align_bytes=64)
-            y_bf[first, last] = group[:]
-            for s in range(first, last + 1):
-                y_bf[s] = group[:, STAGES[s][0] - start : sum(STAGES[s]) - start, :]
+        y_bf = []
+        y_groups = {}
+        for s0, s1 in GROUPS:
+            start, stop = STAGES[s0][0], sum(STAGES[s1])
+            group = keep.tile([P, stop - start, PACK], BF16, name="y_bf%d" % s0, align_bytes=64)
+            y_groups[s1] = (slice(start, stop), group)
+            y_bf.extend(group[:, first - start : first - start + width, :] for first, width in STAGES[s0 : s1 + 1])
 
         def results(s):
             cols, width, y_ps = stages[s]
             y = keep.tile([P, PACK, width], F32, name="y%d" % s)
-            copy = nc.vector.tensor_copy if s == 2 else nc.scalar.copy
+            copy = nc.vector.tensor_copy if s == BY_VECTOR else nc.scalar.copy
             copy(y[:], y_ps[:])
-            queue = nc.scalar if s == len(STAGES) - 1 else nc.sync
+            queue = nc.scalar if s == LAST else nc.sync
             queue.dma_start(out_rows[:, :, cols], y[:])
             ys.append(y)
 
         def rounded(s):
-            cols, width, y_ps = stages[s]
-            if s == len(STAGES) - 1:
-                nc.scalar.copy(y_bf[s], y_ps[:].rearrange("p r n -> p n r"))
+            if s == LAST:
+                nc.scalar.copy(y_bf[s], stages[s][2][:].rearrange("p r n -> p n r"))
                 results(s)
             else:
-                if s > 1:
+                if s >= EARLY:
                     results(s)
                 nc.vector.tensor_copy(
                     y_bf[s].rearrange("p (g i) r -> p g r i", i=PACK),
                     ys[s][:].rearrange("p r (g i) -> p g r i", i=PACK),
                 )
 
-        def planes(first, last):
-            cols = slice(stages[first][0].start, stages[last][0].stop)
+        def quantised(s):
+            cols, group = y_groups[s]
             nc.vector.quantize_mx(
-                y_codes[:, cols].bitcast(FP8X4), y_scales[:, cols], y_bf[first, last].rearrange("p n r -> p (n r)")
+                y_codes[:, cols].bitcast(FP8X4), y_scales[:, cols], group[:].rearrange("p n r -> p (n r)")
             )
 
-        exponents(0)
-        kernels(*STAGES[0])
-        exponents(1)
-        kernels(*STAGES[1])
-        results(0)
-        exponents(2)
-        kernels(*STAGES[2])
-        results(1)
-        exponents(3)
-        kernels(*STAGES[3])
-        kernels(*STAGES[4])
-        kernels(*STAGES[5])
-        rounded(0)
-        rounded(1)
-        rounded(2)
-        rounded(3)
-        planes(0, 2)
-        rounded(4)
-        planes(3, 3)
-        rounded(5)
-        planes(4, 5)
+        for c in range(CHUNKS):
+            exponents(c)
+            kernels(c)
+            if 0 < c <= EARLY:
+                results(c - 1)
+        for s in range(CHUNKS, len(STAGES)):
+            kernels(s)
+        for s in range(len(STAGES)):
+            rounded(s)
+            if s - 1 in y_groups:
+                quantised(s - 1)
+        quantised(LAST)
+
         nc.sync.dma_start(out_words, y_codes[:].bitcast(I32))
         for q in range(QUADS):
             queue = nc.scalar if q % 2 else nc.sync

@@ -53,7 +53,7 @@ def tile_picked_ykrr_lin_po_kernel(
         xw = keep.tile([P, STORE], U32, name="xw")
         ew = keep.tile([P, STORE], U32, name="ew", align_bytes=64)
         xs = keep.tile([P, STORE], U8, name="xs")
-        es = keep.tile([P, STORE], U8, name="es")
+        es = keep.tile([P, STORE], U8, name="es", tag="es")
         hw = keep.tile([P, STORE], F32, name="hw", tag="hw")
         own_sb = keep.tile([P, PACK], F32, name="own_sb")
         wgt_sb = keep.tile([P, PACK], F32, name="wgt_sb")
@@ -68,18 +68,12 @@ def tile_picked_ykrr_lin_po_kernel(
         def load_scales(table, scales):
             nc.sync.dma_start(table[::ROW_STEP, :].bitcast(I32), scales[0].bitcast(I32))
 
-        def place_scales(spread, name):
-            placed = keep.tile([P, S], U8, name=name, align_bytes=64)
-            nc.vector.tensor_copy(placed[:].bitcast(I32), spread[:].bitcast(I32))
-            for i in range(1, SCALE_ROWS):
-                nc.sync.dma_start(placed[i::QUAD, :].bitcast(I32), spread[ROW_STEP * i :: QUAD, :].bitcast(I32))
-            return placed
-
         dual_rows = dual.rearrange("(p j) m -> p j m", j=PACK)
         dual_lo = keep.tile([P, PACK // 2, N], F32, name="dual_lo")
         dual_hi = keep.tile([P, PACK // 2, N], F32, name="dual_hi")
         nc.scalar.dma_start(wgt_sb[:], wgt.rearrange("(p j) o -> p (j o)", j=PACK))
         nc.scalar.dma_start(hw[P - 1 :, :], half[:1, :])
+        nc.scalar.dma_start(own_sb[:], own.rearrange("(p j) o -> p (j o)", j=PACK))
         nc.sync.dma_start(qry_sb[:], qry)
         nc.sync.dma_start(dual_lo[:], dual_rows[:, : PACK // 2, :])
         nc.sync.dma_start(offs_sb[:], offs)
@@ -88,7 +82,6 @@ def tile_picked_ykrr_lin_po_kernel(
         nc.sync.dma_start(dual_hi[:], dual_rows[:, PACK // 2 :, :])
         nc.sync.dma_start(xw[:].bitcast(I32), x_words[0].rearrange("p n r -> p (n r)").bitcast(I32))
         nc.sync.dma_start(ew[:].bitcast(I32), e_words[0].rearrange("p n r -> p (n r)").bitcast(I32))
-        nc.sync.dma_start(own_sb[:], own.rearrange("(p j) o -> p (j o)", j=PACK))
 
         size = keep.tile([P, PACK], F32, name="size")
         nc.vector.scalar_tensor_tensor(size[:], wgt_sb[:], -1.0, wgt_sb[:], ALU.mult, ALU.max)
@@ -102,25 +95,26 @@ def tile_picked_ykrr_lin_po_kernel(
         nc.vector.scalar_tensor_tensor(unit[:], capped[:], -1.0, excess[:], ALU.max, ALU.mult)
         ln_held = keep.tile([P, PACK], F32, name="ln_held")
         nc.scalar.activation(ln_held[:], held[:], ACT.Ln)
-        bias = keep.tile([P, PACK], F32, name="bias")
-        nc.gpsimd.tensor_tensor(bias[:], ln_held[:], own_sb[:], ALU.add)
-        bias2 = keep.tile([P, PACK], F32, name="bias2")
-        nc.gpsimd.tensor_tensor(bias2[:], bias[:], bias[:], ALU.add)
+        own2 = keep.tile([P, PACK], F32, name="own2")
+        nc.vector.tensor_scalar(own2[:], own_sb[:], 2.0, 0.0, ALU.mult, ALU.add)
 
         hg = keep.tile([P, V], F32, name="hg")
         nc.vector.tensor_copy(hg[:], hw[:].indirect(qry_sb[:]))
-        xs_dealt = keep.tile([P, S], U8, name="xs_dealt", tag="hw")
-        nc.vector.tensor_copy(xs_dealt[:].rearrange("k (j p) -> k p j", j=PACK), xs[:].indirect(offs_sb[:]))
-        xs_d = place_scales(xs_dealt, "xs_d")
+        spread = keep.tile([P, S + V], U8, name="spread", tag="hw")
+        nc.vector.tensor_copy(spread[:, :S].rearrange("k (j p) -> k p j", j=PACK), xs[:].indirect(offs_sb[:]))
 
         dual_r = keep.tile([P, PACK, N], BF16, name="dual_r")
         for j in range(PACK):
             rows = (dual_lo, dual_hi)[j // 2][:, j % 2, :]
             nc.scalar.activation(dual_r[:, j, :], rows, ACT.Copy, scale=unit[:, j : j + 1])
 
-        es_spread = keep.tile([P, V], U8, name="es_spread")
-        nc.vector.tensor_copy(es_spread[:], es[:].indirect(qry_sb[:]))
-        es_g = place_scales(es_spread, "es_g")
+        nc.vector.tensor_copy(spread[:, S:], es[:].indirect(qry_sb[:]))
+        placed = keep.tile([P, S + V], U8, name="placed", align_bytes=64)
+        nc.vector.tensor_copy(placed[:].bitcast(I32), spread[:].bitcast(I32))
+        for i in range(1, SCALE_ROWS):
+            nc.sync.dma_start(placed[i::QUAD, :].bitcast(I32), spread[ROW_STEP * i :: QUAD, :].bitcast(I32))
+        bias2 = keep.tile([P, PACK], F32, name="bias2", tag="es")
+        nc.vector.scalar_tensor_tensor(bias2[:], ln_held[:], 2.0, own2[:], ALU.mult, ALU.add)
         xw_d = keep.tile([P, S], U32, name="xw_d", align_bytes=64)
         nc.vector.tensor_copy(xw_d[:].rearrange("k (j p) -> k p j", j=PACK), xw[:].indirect(offs_sb[:]))
 
@@ -160,7 +154,6 @@ def tile_picked_ykrr_lin_po_kernel(
         z2 = {}
 
         def exponents(c):
-            cols = slice(c * CHUNK, (c + 1) * CHUNK)
             s_lo = ps_s.tile([P, PACK, CHUNK], F32, name="s_ps")
             s_hi = ps_y.tile([P, PACK, CHUNK], F32, name="s_hi", tag="y_ps") if c == 0 else s_lo
             s_ps = (s_lo, s_lo, s_hi, s_hi)
@@ -168,9 +161,9 @@ def tile_picked_ykrr_lin_po_kernel(
                 nc.tensor.matmul_mx(
                     s_ps[j][:, j, :],
                     lhsT=xw_d[:, j * P : (j + 1) * P].bitcast(FP8X4),
-                    lhsT_scale=xs_d[:, j * P : (j + 1) * P],
+                    lhsT_scale=placed[:, j * P : (j + 1) * P],
                     rhs=picked[c].bitcast(FP8X4),
-                    rhs_scale=es_g[:, cols],
+                    rhs_scale=placed[:, S + c * CHUNK : S + (c + 1) * CHUNK],
                     start=True,
                     stop=True,
                 )

@@ -33,9 +33,8 @@ LN_RANGE = 2.0**63
 PIECES = ((0, CHUNK), (CHUNK, CHUNK), (2 * CHUNK, 2 * CHUNK))
 STAGES = ((0, 64), (64, 64), (128, 128), (256, 128), (384, 64), (448, 64))
 LAST = len(STAGES) - 1
-EARLY = 2
-BY_VECTOR = 2
-GROUPS = ((0, 2), (3, 3), (4, 5))
+BY_VECTOR = (1, 4)
+GROUPS = ((0, 1), (2, 3), (4, 5))
 BY_SCALAR = 96
 
 
@@ -53,7 +52,7 @@ def tile_picked_ykrr_lin_po_kernel(
         xw = keep.tile([P, STORE], U32, name="xw")
         ew = keep.tile([P, STORE], U32, name="ew", align_bytes=64)
         xs = keep.tile([P, STORE], U8, name="xs")
-        es = keep.tile([P, STORE], U8, name="es", tag="es")
+        es = keep.tile([P, STORE], U8, name="es")
         hw = keep.tile([P, STORE], F32, name="hw", tag="hw")
         own_sb = keep.tile([P, PACK], F32, name="own_sb")
         wgt_sb = keep.tile([P, PACK], F32, name="wgt_sb")
@@ -73,7 +72,6 @@ def tile_picked_ykrr_lin_po_kernel(
         dual_hi = keep.tile([P, PACK // 2, N], F32, name="dual_hi")
         nc.scalar.dma_start(wgt_sb[:], wgt.rearrange("(p j) o -> p (j o)", j=PACK))
         nc.scalar.dma_start(hw[P - 1 :, :], half[:1, :])
-        nc.scalar.dma_start(own_sb[:], own.rearrange("(p j) o -> p (j o)", j=PACK))
         nc.sync.dma_start(qry_sb[:], qry)
         nc.sync.dma_start(dual_lo[:], dual_rows[:, : PACK // 2, :])
         nc.sync.dma_start(offs_sb[:], offs)
@@ -81,6 +79,7 @@ def tile_picked_ykrr_lin_po_kernel(
         load_scales(es, e_scales)
         nc.sync.dma_start(dual_hi[:], dual_rows[:, PACK // 2 :, :])
         nc.sync.dma_start(xw[:].bitcast(I32), x_words[0].rearrange("p n r -> p (n r)").bitcast(I32))
+        nc.sync.dma_start(own_sb[:], own.rearrange("(p j) o -> p (j o)", j=PACK))
         nc.sync.dma_start(ew[:].bitcast(I32), e_words[0].rearrange("p n r -> p (n r)").bitcast(I32))
 
         size = keep.tile([P, PACK], F32, name="size")
@@ -95,8 +94,10 @@ def tile_picked_ykrr_lin_po_kernel(
         nc.vector.scalar_tensor_tensor(unit[:], capped[:], -1.0, excess[:], ALU.max, ALU.mult)
         ln_held = keep.tile([P, PACK], F32, name="ln_held")
         nc.scalar.activation(ln_held[:], held[:], ACT.Ln)
-        own2 = keep.tile([P, PACK], F32, name="own2")
-        nc.vector.tensor_scalar(own2[:], own_sb[:], 2.0, 0.0, ALU.mult, ALU.add)
+        bias = keep.tile([P, PACK], F32, name="bias")
+        nc.gpsimd.tensor_tensor(bias[:], ln_held[:], own_sb[:], ALU.add)
+        bias2 = keep.tile([P, PACK], F32, name="bias2")
+        nc.gpsimd.tensor_tensor(bias2[:], bias[:], bias[:], ALU.add)
 
         hg = keep.tile([P, V], F32, name="hg")
         nc.vector.tensor_copy(hg[:], hw[:].indirect(qry_sb[:]))
@@ -113,8 +114,6 @@ def tile_picked_ykrr_lin_po_kernel(
         nc.vector.tensor_copy(placed[:].bitcast(I32), spread[:].bitcast(I32))
         for i in range(1, SCALE_ROWS):
             nc.sync.dma_start(placed[i::QUAD, :].bitcast(I32), spread[ROW_STEP * i :: QUAD, :].bitcast(I32))
-        bias2 = keep.tile([P, PACK], F32, name="bias2", tag="es")
-        nc.vector.scalar_tensor_tensor(bias2[:], ln_held[:], 2.0, own2[:], ALU.mult, ALU.add)
         xw_d = keep.tile([P, S], U32, name="xw_d", align_bytes=64)
         nc.vector.tensor_copy(xw_d[:].rearrange("k (j p) -> k p j", j=PACK), xw[:].indirect(offs_sb[:]))
 
@@ -223,7 +222,7 @@ def tile_picked_ykrr_lin_po_kernel(
         def results(s):
             cols, width, y_ps = stages[s]
             y = keep.tile([P, PACK, width], F32, name="y%d" % s)
-            copy = nc.vector.tensor_copy if s == BY_VECTOR else nc.scalar.copy
+            copy = nc.vector.tensor_copy if s in BY_VECTOR else nc.scalar.copy
             copy(y[:], y_ps[:])
             queue = nc.scalar if s == LAST else nc.sync
             queue.dma_start(out_rows[:, :, cols], y[:])
@@ -234,8 +233,6 @@ def tile_picked_ykrr_lin_po_kernel(
                 nc.scalar.copy(y_bf[s], stages[s][2][:].rearrange("p r n -> p n r"))
                 results(s)
             else:
-                if s >= EARLY:
-                    results(s)
                 nc.vector.tensor_copy(
                     y_bf[s].rearrange("p (g i) r -> p g r i", i=PACK),
                     ys[s][:].rearrange("p r (g i) -> p g r i", i=PACK),
@@ -250,15 +247,23 @@ def tile_picked_ykrr_lin_po_kernel(
         for c in range(CHUNKS):
             exponents(c)
             kernels(c)
-            if 0 < c <= EARLY:
-                results(c - 1)
+            if c == 2:
+                results(0)
         for s in range(CHUNKS, len(STAGES)):
             kernels(s)
-        for s in range(len(STAGES)):
-            rounded(s)
-            if s - 1 in y_groups:
-                quantised(s - 1)
-        quantised(LAST)
+        results(1)
+        rounded(0)
+        rounded(1)
+        results(2)
+        quantised(1)
+        results(3)
+        rounded(2)
+        results(4)
+        rounded(3)
+        rounded(4)
+        rounded(5)
+        quantised(3)
+        quantised(5)
 
         nc.sync.dma_start(out_words, y_codes[:].bitcast(I32))
         for q in range(QUADS):

@@ -58,10 +58,9 @@ def tile_picked_ykrr_lin_po_kernel(
         wgt_sb = keep.tile([P, PACK], F32, name="wgt_sb")
         ident = keep.tile([P, P], F32, name="ident")
 
-        nc.gpsimd.memset(xs[:].bitcast(I32), 0)
+        nc.vector.memset(xs[:].bitcast(I32), 0)
         nc.vector.memset(es[:].bitcast(I32), 0)
-        nc.vector.memset(hw[: P - 1, : STORE // 2].bitcast(I32), 0)
-        nc.gpsimd.memset(hw[: P - 1, STORE // 2 :].bitcast(I32), 0)
+        nc.vector.memset(hw[: P - 1, :].bitcast(I32), 0)
         make_identity(nc, ident[:])
 
         def load_scales(table, scales):

@@ -36,6 +36,7 @@ LAST = len(STAGES) - 1
 BY_VECTOR = (1, 4)
 GROUPS = ((0, 1), (2, 3), (4, 5))
 BY_SCALAR = 96
+PART = 64
 
 
 def tile_picked_ykrr_lin_po_kernel(
@@ -60,15 +61,16 @@ def tile_picked_ykrr_lin_po_kernel(
 
         nc.vector.memset(xs[:].bitcast(I32), 0)
         nc.vector.memset(es[:].bitcast(I32), 0)
+        nc.vector.memset(ident[:], 0.0)
         nc.vector.memset(hw[: P - 1, :].bitcast(I32), 0)
-        make_identity(nc, ident[:])
+        make_identity(nc, ident[:], nomemset=True)
 
         def load_scales(table, scales):
             nc.sync.dma_start(table[::ROW_STEP, :].bitcast(I32), scales[0].bitcast(I32))
 
         dual_rows = dual.rearrange("(p j) m -> p j m", j=PACK)
         dual_lo = keep.tile([P, PACK // 2, N], F32, name="dual_lo")
-        dual_hi = keep.tile([P, PACK // 2, N], F32, name="dual_hi")
+        dual_hi = keep.tile([P, PACK // 2, N], F32, name="dual_hi", tag="dual_hi")
         nc.scalar.dma_start(wgt_sb[:], wgt.rearrange("(p j) o -> p (j o)", j=PACK))
         nc.scalar.dma_start(hw[P - 1 :, :], half[:1, :])
         nc.sync.dma_start(qry_sb[:], qry)
@@ -85,16 +87,17 @@ def tile_picked_ykrr_lin_po_kernel(
         nc.vector.scalar_tensor_tensor(size[:], wgt_sb[:], -1.0, wgt_sb[:], ALU.mult, ALU.max)
         capped = keep.tile([P, PACK], F32, name="capped")
         nc.vector.tensor_scalar(capped[:], wgt_sb[:], LN_RANGE, 1.0, ALU.mult, ALU.min)
-        held = keep.tile([P, PACK], F32, name="held")
-        nc.vector.tensor_scalar(held[:], size[:], 1.0 / LN_RANGE, LN_RANGE, ALU.max, ALU.min)
-        excess = keep.tile([P, PACK], F32, name="excess")
-        nc.vector.tensor_scalar(excess[:], size[:], 1.0 / LN_RANGE, 1.0, ALU.mult, ALU.max)
+        factors = keep.tile([P, 2, PACK], F32, name="factors")
+        nc.vector.tensor_scalar(factors[:, 0, :], size[:], 1.0 / LN_RANGE, LN_RANGE, ALU.max, ALU.min)
+        nc.vector.tensor_scalar(factors[:, 1, :], size[:], 1.0 / LN_RANGE, 1.0, ALU.mult, ALU.max)
         unit = keep.tile([P, PACK], F32, name="unit")
-        nc.vector.scalar_tensor_tensor(unit[:], capped[:], -1.0, excess[:], ALU.max, ALU.mult)
-        ln_held = keep.tile([P, PACK], F32, name="ln_held")
-        nc.scalar.activation(ln_held[:], held[:], ACT.Ln)
+        nc.vector.tensor_scalar(unit[:], capped[:], -1.0, 1.0, ALU.max, ALU.mult)
+        logs = keep.tile([P, 2, PACK], F32, name="logs")
+        nc.scalar.activation(logs[:], factors[:], ACT.Ln)
+        ln_size = keep.tile([P, PACK], F32, name="ln_size")
+        nc.gpsimd.tensor_tensor(ln_size[:], logs[:, 0, :], logs[:, 1, :], ALU.add)
         bias = keep.tile([P, PACK], F32, name="bias")
-        nc.gpsimd.tensor_tensor(bias[:], ln_held[:], own_sb[:], ALU.add)
+        nc.gpsimd.tensor_tensor(bias[:], ln_size[:], own_sb[:], ALU.add)
         bias2 = keep.tile([P, PACK], F32, name="bias2")
         nc.gpsimd.tensor_tensor(bias2[:], bias[:], bias[:], ALU.add)
 
@@ -125,17 +128,25 @@ def tile_picked_ykrr_lin_po_kernel(
         for b in range(V // P):
             nc.tensor.transpose(h_rows[:, b * P : (b + 1) * P], h_col[:, b : b + 1].to_broadcast([P, P]), ident[:])
 
-        dual_bf = keep.tile([P, PACK, P, PACK], BF16, name="dual_bf", align_bytes=64)
-        for c0, c1, copy in ((0, BY_SCALAR, nc.scalar.copy), (BY_SCALAR, P, nc.vector.tensor_copy)):
-            copy(
-                dual_bf[:, :, c0:c1, :].rearrange("p r c j -> p c j r"),
-                dual_r[:, :, PACK * c0 : PACK * c1].rearrange("p j (c r) -> p c j r", r=PACK),
-            )
-        minus_half2 = keep.tile([P, V], F32, name="minus_half2")
-        nc.scalar.activation(minus_half2[:], h_rows[:], ACT.Copy, scale=-2.0)
         d_codes = keep.tile([P, N], U32, name="d_codes", align_bytes=64)
         d_scales = keep.tile([P, N], U8, name="d_scales", align_bytes=64)
-        nc.vector.quantize_mx(d_codes[:].bitcast(FP8X4), d_scales[:], dual_bf[:].rearrange("p r c j -> p (r c j)"))
+        shares = (((0, PART, nc.scalar.copy),), ((PART, BY_SCALAR, nc.scalar.copy), (BY_SCALAR, P, nc.vector.tensor_copy)))
+        for h in range(P // PART):
+            dual_bf = keep.tile([P, PACK, PART, PACK], BF16, name="dual_bf%d" % h, align_bytes=64)
+            for c0, c1, copy in shares[h]:
+                copy(
+                    dual_bf[:, :, c0 - h * PART : c1 - h * PART, :].rearrange("p r c j -> p c j r"),
+                    dual_r[:, :, PACK * c0 : PACK * c1].rearrange("p j (c r) -> p c j r", r=PACK),
+                )
+            for r in range(PACK):
+                cols = slice(r * P + h * PART, r * P + (h + 1) * PART)
+                nc.vector.quantize_mx(
+                    d_codes[:, cols].bitcast(FP8X4),
+                    d_scales[:, cols],
+                    dual_bf[:, r, :, :].rearrange("p c j -> p (c j)"),
+                )
+        minus_half2 = keep.tile([P, V], F32, name="minus_half2", tag="dual_hi")
+        nc.scalar.activation(minus_half2[:], h_rows[:], ACT.Copy, scale=-2.0)
 
         picked = []
         for first, width in PIECES:

@@ -33,7 +33,7 @@ LN_RANGE = 2.0**63
 PIECES = ((0, CHUNK), (CHUNK, CHUNK), (2 * CHUNK, 2 * CHUNK))
 STAGES = ((0, 64), (64, 64), (128, 128), (256, 128), (384, 64), (448, 64))
 LAST = len(STAGES) - 1
-BY_VECTOR = (1, 4)
+BY_VECTOR = (0, 1, 4)
 GROUPS = ((0, 1), (2, 3), (4, 5))
 BY_SCALAR = 96
 PART = 64
@@ -55,7 +55,6 @@ def tile_picked_ykrr_lin_po_kernel(
         xs = keep.tile([P, STORE], U8, name="xs")
         es = keep.tile([P, STORE], U8, name="es")
         hw = keep.tile([P, STORE], F32, name="hw", tag="hw")
-        own_sb = keep.tile([P, PACK], F32, name="own_sb")
         wgt_sb = keep.tile([P, PACK], F32, name="wgt_sb")
         ident = keep.tile([P, P], F32, name="ident")
 
@@ -73,27 +72,28 @@ def tile_picked_ykrr_lin_po_kernel(
         dual_hi = keep.tile([P, PACK // 2, N], F32, name="dual_hi", tag="dual_hi")
         nc.scalar.dma_start(wgt_sb[:], wgt.rearrange("(p j) o -> p (j o)", j=PACK))
         nc.scalar.dma_start(hw[P - 1 :, :], half[:1, :])
-        nc.sync.dma_start(qry_sb[:], qry)
         nc.sync.dma_start(dual_lo[:], dual_rows[:, : PACK // 2, :])
+        nc.sync.dma_start(qry_sb[:], qry)
         nc.sync.dma_start(offs_sb[:], offs)
         load_scales(xs, x_scales)
         load_scales(es, e_scales)
         nc.sync.dma_start(dual_hi[:], dual_rows[:, PACK // 2 :, :])
         nc.sync.dma_start(xw[:].bitcast(I32), x_words[0].rearrange("p n r -> p (n r)").bitcast(I32))
-        nc.sync.dma_start(own_sb[:], own.rearrange("(p j) o -> p (j o)", j=PACK))
         nc.sync.dma_start(ew[:].bitcast(I32), e_words[0].rearrange("p n r -> p (n r)").bitcast(I32))
 
         size = keep.tile([P, PACK], F32, name="size")
         nc.vector.scalar_tensor_tensor(size[:], wgt_sb[:], -1.0, wgt_sb[:], ALU.mult, ALU.max)
         capped = keep.tile([P, PACK], F32, name="capped")
         nc.vector.tensor_scalar(capped[:], wgt_sb[:], LN_RANGE, 1.0, ALU.mult, ALU.min)
-        factors = keep.tile([P, 2, PACK], F32, name="factors")
+        factors = keep.tile([P, 2, PACK], F32, name="factors", tag="factors")
         nc.vector.tensor_scalar(factors[:, 0, :], size[:], 1.0 / LN_RANGE, LN_RANGE, ALU.max, ALU.min)
         nc.vector.tensor_scalar(factors[:, 1, :], size[:], 1.0 / LN_RANGE, 1.0, ALU.mult, ALU.max)
         unit = keep.tile([P, PACK], F32, name="unit")
         nc.vector.tensor_scalar(unit[:], capped[:], -1.0, 1.0, ALU.max, ALU.mult)
         logs = keep.tile([P, 2, PACK], F32, name="logs")
         nc.scalar.activation(logs[:], factors[:], ACT.Ln)
+        own_sb = keep.tile([P, PACK], F32, name="own_sb", tag="factors")
+        nc.scalar.dma_start(own_sb[:], own.rearrange("(p j) o -> p (j o)", j=PACK))
         ln_size = keep.tile([P, PACK], F32, name="ln_size")
         nc.gpsimd.tensor_tensor(ln_size[:], logs[:, 0, :], logs[:, 1, :], ALU.add)
         bias = keep.tile([P, PACK], F32, name="bias")
@@ -257,10 +257,9 @@ def tile_picked_ykrr_lin_po_kernel(
         for c in range(CHUNKS):
             exponents(c)
             kernels(c)
-            if c == 2:
-                results(0)
         for s in range(CHUNKS, len(STAGES)):
             kernels(s)
+        results(0)
         results(1)
         rounded(0)
         rounded(1)

@@ -35,8 +35,7 @@ STAGES = ((0, 64), (64, 64), (128, 128), (256, 128), (384, 64), (448, 64))
 LAST = len(STAGES) - 1
 BY_VECTOR = (0, 1, 4)
 GROUPS = ((0, 1), (2, 3), (4, 5))
-BY_SCALAR = 96
-PART = 64
+BY_SCALAR = 64
 
 
 def tile_picked_ykrr_lin_po_kernel(
@@ -54,7 +53,7 @@ def tile_picked_ykrr_lin_po_kernel(
         ew = keep.tile([P, STORE], U32, name="ew", align_bytes=64)
         xs = keep.tile([P, STORE], U8, name="xs")
         es = keep.tile([P, STORE], U8, name="es")
-        hw = keep.tile([P, STORE], F32, name="hw", tag="hw")
+        hw = keep.tile([P, STORE], F32, name="hw")
         wgt_sb = keep.tile([P, PACK], F32, name="wgt_sb")
         ident = keep.tile([P, P], F32, name="ident")
 
@@ -94,22 +93,17 @@ def tile_picked_ykrr_lin_po_kernel(
         nc.scalar.activation(logs[:], factors[:], ACT.Ln)
         own_sb = keep.tile([P, PACK], F32, name="own_sb", tag="factors")
         nc.scalar.dma_start(own_sb[:], own.rearrange("(p j) o -> p (j o)", j=PACK))
-        ln_size = keep.tile([P, PACK], F32, name="ln_size")
-        nc.gpsimd.tensor_tensor(ln_size[:], logs[:, 0, :], logs[:, 1, :], ALU.add)
-        bias = keep.tile([P, PACK], F32, name="bias")
-        nc.gpsimd.tensor_tensor(bias[:], ln_size[:], own_sb[:], ALU.add)
-        bias2 = keep.tile([P, PACK], F32, name="bias2")
-        nc.gpsimd.tensor_tensor(bias2[:], bias[:], bias[:], ALU.add)
 
         hg = keep.tile([P, V], F32, name="hg")
-        nc.vector.tensor_copy(hg[:], hw[:].indirect(qry_sb[:]))
-        spread = keep.tile([P, S + V], U8, name="spread", tag="hw")
+        nc.scalar.activation(hg[:], hw[:].indirect(qry_sb[:]), ACT.Copy)
+        spread = keep.tile([P, S + V], U8, name="spread")
         nc.vector.tensor_copy(spread[:, :S].rearrange("k (j p) -> k p j", j=PACK), xs[:].indirect(offs_sb[:]))
 
         dual_r = keep.tile([P, PACK, N], BF16, name="dual_r")
-        for j in range(PACK):
-            rows = (dual_lo, dual_hi)[j // 2][:, j % 2, :]
-            nc.scalar.activation(dual_r[:, j, :], rows, ACT.Copy, scale=unit[:, j : j + 1])
+        for j in range(PACK // 2):
+            nc.gpsimd.tensor_scalar(dual_r[:, j, :], dual_lo[:, j, :], unit[:, j : j + 1], 0.0, ALU.mult, ALU.add)
+        for j in range(PACK // 2, PACK):
+            nc.scalar.activation(dual_r[:, j, :], dual_hi[:, j % 2, :], ACT.Copy, scale=unit[:, j : j + 1])
 
         nc.vector.tensor_copy(spread[:, S:], es[:].indirect(qry_sb[:]))
         placed = keep.tile([P, S + V], U8, name="placed", align_bytes=64)
@@ -130,23 +124,22 @@ def tile_picked_ykrr_lin_po_kernel(
 
         d_codes = keep.tile([P, N], U32, name="d_codes", align_bytes=64)
         d_scales = keep.tile([P, N], U8, name="d_scales", align_bytes=64)
-        shares = (((0, PART, nc.scalar.copy),), ((PART, BY_SCALAR, nc.scalar.copy), (BY_SCALAR, P, nc.vector.tensor_copy)))
-        for h in range(P // PART):
-            dual_bf = keep.tile([P, PACK, PART, PACK], BF16, name="dual_bf%d" % h, align_bytes=64)
-            for c0, c1, copy in shares[h]:
-                copy(
-                    dual_bf[:, :, c0 - h * PART : c1 - h * PART, :].rearrange("p r c j -> p c j r"),
-                    dual_r[:, :, PACK * c0 : PACK * c1].rearrange("p j (c r) -> p c j r", r=PACK),
-                )
-            for r in range(PACK):
-                cols = slice(r * P + h * PART, r * P + (h + 1) * PART)
-                nc.vector.quantize_mx(
-                    d_codes[:, cols].bitcast(FP8X4),
-                    d_scales[:, cols],
-                    dual_bf[:, r, :, :].rearrange("p c j -> p (c j)"),
-                )
+        dual_bf = keep.tile([P, PACK, P, PACK], BF16, name="dual_bf", align_bytes=64)
+        for c0, c1, copy in ((0, BY_SCALAR, nc.scalar.copy), (BY_SCALAR, P, nc.vector.tensor_copy)):
+            copy(
+                dual_bf[:, :, c0:c1, :].rearrange("p r c j -> p c j r"),
+                dual_r[:, :, PACK * c0 : PACK * c1].rearrange("p j (c r) -> p c j r", r=PACK),
+            )
+        nc.vector.quantize_mx(d_codes[:].bitcast(FP8X4), d_scales[:], dual_bf[:].rearrange("p r c j -> p (r c j)"))
         minus_half2 = keep.tile([P, V], F32, name="minus_half2", tag="dual_hi")
         nc.scalar.activation(minus_half2[:], h_rows[:], ACT.Copy, scale=-2.0)
+
+        ln_size = keep.tile([P, PACK], F32, name="ln_size")
+        nc.gpsimd.tensor_tensor(ln_size[:], logs[:, 0, :], logs[:, 1, :], ALU.add)
+        bias = keep.tile([P, PACK], F32, name="bias")
+        nc.gpsimd.tensor_tensor(bias[:], ln_size[:], own_sb[:], ALU.add)
+        bias2 = keep.tile([P, PACK], F32, name="bias2")
+        nc.gpsimd.tensor_tensor(bias2[:], bias[:], bias[:], ALU.add)
 
         picked = []
         for first, width in PIECES:

@@ -33,9 +33,11 @@ LN_RANGE = 2.0**63
 PIECES = ((0, CHUNK), (CHUNK, CHUNK), (2 * CHUNK, 2 * CHUNK))
 STAGES = ((0, 64), (64, 64), (128, 128), (256, 128), (384, 64), (448, 64))
 LAST = len(STAGES) - 1
+RUN = 64
 BY_VECTOR = (0, 1, 4)
 GROUPS = ((0, 1), (2, 3), (4, 5))
 BY_SCALAR = 64
+SLOT_BY_SCALAR = 3
 
 
 def tile_picked_ykrr_lin_po_kernel(
@@ -68,7 +70,7 @@ def tile_picked_ykrr_lin_po_kernel(
 
         dual_rows = dual.rearrange("(p j) m -> p j m", j=PACK)
         dual_lo = keep.tile([P, PACK // 2, N], F32, name="dual_lo")
-        dual_hi = keep.tile([P, PACK // 2, N], F32, name="dual_hi", tag="dual_hi")
+        dual_hi = keep.tile([P, PACK // 2, N], F32, name="dual_hi", tag="dual_hi", align_bytes=64)
         nc.scalar.dma_start(wgt_sb[:], wgt.rearrange("(p j) o -> p (j o)", j=PACK))
         nc.scalar.dma_start(hw[P - 1 :, :], half[:1, :])
         nc.sync.dma_start(dual_lo[:], dual_rows[:, : PACK // 2, :])
@@ -99,19 +101,19 @@ def tile_picked_ykrr_lin_po_kernel(
         spread = keep.tile([P, S + V], U8, name="spread")
         nc.vector.tensor_copy(spread[:, :S].rearrange("k (j p) -> k p j", j=PACK), xs[:].indirect(offs_sb[:]))
 
-        dual_r = keep.tile([P, PACK, N], BF16, name="dual_r")
-        for j in range(PACK // 2):
-            nc.gpsimd.tensor_scalar(dual_r[:, j, :], dual_lo[:, j, :], unit[:, j : j + 1], 0.0, ALU.mult, ALU.add)
-        for j in range(PACK // 2, PACK):
-            nc.scalar.activation(dual_r[:, j, :], dual_hi[:, j % 2, :], ACT.Copy, scale=unit[:, j : j + 1])
+        dual_r = keep.tile([P, PACK, N], BF16, name="dual_r", tag="dual_r")
+        for j in range(PACK):
+            rows = (dual_lo, dual_hi)[j // 2][:, j % 2, :]
+            if j == SLOT_BY_SCALAR:
+                nc.scalar.activation(dual_r[:, j, :], rows, ACT.Copy, scale=unit[:, j : j + 1])
+            else:
+                nc.gpsimd.tensor_scalar(dual_r[:, j, :], rows, unit[:, j : j + 1], 0.0, ALU.mult, ALU.add)
 
         nc.vector.tensor_copy(spread[:, S:], es[:].indirect(qry_sb[:]))
         placed = keep.tile([P, S + V], U8, name="placed", align_bytes=64)
         nc.vector.tensor_copy(placed[:].bitcast(I32), spread[:].bitcast(I32))
         for i in range(1, SCALE_ROWS):
             nc.sync.dma_start(placed[i::QUAD, :].bitcast(I32), spread[ROW_STEP * i :: QUAD, :].bitcast(I32))
-        xw_d = keep.tile([P, S], U32, name="xw_d", align_bytes=64)
-        nc.vector.tensor_copy(xw_d[:].rearrange("k (j p) -> k p j", j=PACK), xw[:].indirect(offs_sb[:]))
 
         h_turned = ps_y.tile([P, V // P, P], F32, name="h_turned", tag="y_ps")
         for b in range(V // P):
@@ -130,8 +132,10 @@ def tile_picked_ykrr_lin_po_kernel(
                 dual_bf[:, :, c0:c1, :].rearrange("p r c j -> p c j r"),
                 dual_r[:, :, PACK * c0 : PACK * c1].rearrange("p j (c r) -> p c j r", r=PACK),
             )
+        xw_d = keep.tile([P, S], U32, name="xw_d", tag="dual_hi", align_bytes=64)
+        nc.vector.tensor_copy(xw_d[:].rearrange("k (j p) -> k p j", j=PACK), xw[:].indirect(offs_sb[:]))
         nc.vector.quantize_mx(d_codes[:].bitcast(FP8X4), d_scales[:], dual_bf[:].rearrange("p r c j -> p (r c j)"))
-        minus_half2 = keep.tile([P, V], F32, name="minus_half2", tag="dual_hi")
+        minus_half2 = keep.tile([P, V], F32, name="minus_half2", tag="dual_r")
         nc.scalar.activation(minus_half2[:], h_rows[:], ACT.Copy, scale=-2.0)
 
         ln_size = keep.tile([P, PACK], F32, name="ln_size")
@@ -169,20 +173,19 @@ def tile_picked_ykrr_lin_po_kernel(
                     start=True,
                     stop=True,
                 )
-            for first, width in STAGES:
-                if first // CHUNK == c:
-                    part = slice(first % CHUNK, first % CHUNK + width)
-                    z = keep.tile([P, PACK, width], F32, name="z2_%d" % first)
-                    z2[first] = z
-                    for j in range(PACK):
-                        nc.vector.scalar_tensor_tensor(
-                            z[:, j, :],
-                            s_ps[j][:, j, part],
-                            bias2[:, j : j + 1],
-                            minus_half2[:, first : first + width],
-                            ALU.add,
-                            ALU.add,
-                        )
+            for first in range(c * CHUNK, (c + 1) * CHUNK, RUN):
+                part = slice(first % CHUNK, first % CHUNK + RUN)
+                z = keep.tile([P, PACK, RUN], F32, name="z2_%d" % first)
+                z2[first] = z
+                for j in range(PACK):
+                    nc.vector.scalar_tensor_tensor(
+                        z[:, j, :],
+                        s_ps[j][:, j, part],
+                        bias2[:, j : j + 1],
+                        minus_half2[:, first : first + RUN],
+                        ALU.add,
+                        ALU.add,
+                    )
 
         stages = []
 
@@ -190,12 +193,13 @@ def tile_picked_ykrr_lin_po_kernel(
             first, width = STAGES[s]
             cols = slice(first, first + width)
             a_bf = keep.tile([P, width, PACK], BF16, name="a_bf%d" % first, align_bytes=64)
-            nc.scalar.activation(
-                a_bf[:].rearrange("p (g i) j -> p g j i", i=PACK),
-                z2[first][:].rearrange("p j (g i) -> p g j i", i=PACK),
-                ACT.Exp,
-                scale=0.5,
-            )
+            for n in range(0, width, RUN):
+                nc.scalar.activation(
+                    a_bf[:, n : n + RUN, :].rearrange("p (g i) j -> p g j i", i=PACK),
+                    z2[first + n][:].rearrange("p j (g i) -> p g j i", i=PACK),
+                    ACT.Exp,
+                    scale=0.5,
+                )
             a_codes = keep.tile([P, width], U32, name="a_codes%d" % first, align_bytes=64)
             a_scales = keep.tile([P, width], U8, name="a_scales%d" % first, align_bytes=64)
             nc.vector.quantize_mx(a_codes[:].bitcast(FP8X4), a_scales[:], a_bf[:].rearrange("p n j -> p (n j)"))

@@ -218,6 +218,8 @@ def tile_picked_ykrr_lin_po_kernel(
             stages.append((cols, width, y_ps))
 
         ys = []
+        end_cols = slice(V - CHUNK, V)
+        y_end = keep.tile([P, PACK, CHUNK], F32, name="y_end")
         y_bf = []
         y_groups = {}
         for s0, s1 in GROUPS:
@@ -228,12 +230,18 @@ def tile_picked_ykrr_lin_po_kernel(
 
         def results(s):
             cols, width, y_ps = stages[s]
-            y = keep.tile([P, PACK, width], F32, name="y%d" % s)
             copy = nc.vector.tensor_copy if s in BY_VECTOR else nc.scalar.copy
-            copy(y[:], y_ps[:])
-            queue = nc.scalar if s == LAST else nc.sync
-            queue.dma_start(out_rows[:, :, cols], y[:])
-            ys.append(y)
+            if cols.start < end_cols.start:
+                y = keep.tile([P, PACK, width], F32, name="y%d" % s)
+                copy(y[:], y_ps[:])
+                nc.sync.dma_start(out_rows[:, :, cols], y[:])
+                ys.append(y[:])
+            else:
+                y_part = y_end[:, :, cols.start - end_cols.start : cols.stop - end_cols.start]
+                copy(y_part, y_ps[:])
+                ys.append(y_part)
+                if s == LAST:
+                    nc.scalar.dma_start(out_rows[:, :, end_cols], y_end[:])
 
         def rounded(s):
             if s == LAST:
@@ -242,7 +250,7 @@ def tile_picked_ykrr_lin_po_kernel(
             else:
                 nc.vector.tensor_copy(
                     y_bf[s].rearrange("p (g i) r -> p g r i", i=PACK),
-                    ys[s][:].rearrange("p r (g i) -> p g r i", i=PACK),
+                    ys[s].rearrange("p r (g i) -> p g r i", i=PACK),
                 )
 
         def quantised(s):
@@ -256,20 +264,19 @@ def tile_picked_ykrr_lin_po_kernel(
             kernels(c)
         for s in range(CHUNKS, len(STAGES)):
             kernels(s)
-        results(0)
-        results(1)
-        rounded(0)
-        rounded(1)
-        results(2)
-        quantised(1)
-        results(3)
-        rounded(2)
-        results(4)
-        rounded(3)
-        rounded(4)
-        rounded(5)
-        quantised(3)
-        quantised(5)
+        (first_stage, second_stage), *later_groups = GROUPS
+        for step in (results, rounded):
+            step(first_stage)
+            step(second_stage)
+        results(second_stage + 1)
+        quantised(second_stage)
+        for s in range(second_stage + 2, LAST):
+            results(s)
+            rounded(s - 1)
+        rounded(LAST - 1)
+        rounded(LAST)
+        for s0, s1 in later_groups:
+            quantised(s1)
 
         nc.sync.dma_start(out_words, y_codes[:].bitcast(I32))
         for q in range(QUADS):

@@ -31,11 +31,11 @@ CHUNK = 128
 CHUNKS = V // CHUNK
 LN_RANGE = 2.0**63
 PIECES = ((0, CHUNK), (CHUNK, CHUNK), (2 * CHUNK, 2 * CHUNK))
-STAGES = ((0, 64), (64, 64), (128, 128), (256, 128), (384, 64), (448, 64))
+STAGES = ((0, 128), (128, 128), (256, 128), (384, 64), (448, 64))
 LAST = len(STAGES) - 1
 RUN = 64
-BY_VECTOR = (0, 1, 4)
-GROUPS = ((0, 1), (2, 3), (4, 5))
+BY_VECTOR = (0, 3)
+GROUPS = ((0, 0), (1, 2), (3, 4))
 BY_SCALAR = 64
 SLOT_BY_SCALAR = 3
 
@@ -205,9 +205,10 @@ def tile_picked_ykrr_lin_po_kernel(
             nc.vector.quantize_mx(a_codes[:].bitcast(FP8X4), a_scales[:], a_bf[:].rearrange("p n j -> p (n j)"))
 
             y_ps = ps_y.tile([P, PACK, width], F32, name="y_ps")
+            y_hi = ps_y.tile([P, PACK, width], F32, name="y_hi", tag="y_ps") if s == 0 else y_ps
             for r in range(PACK):
                 nc.tensor.matmul_mx(
-                    y_ps[:, r, :],
+                    (y_ps, y_hi)[r // 2][:, r, :],
                     lhsT=d_codes[:, r * P : (r + 1) * P].bitcast(FP8X4),
                     lhsT_scale=d_scales[:, r * P : (r + 1) * P],
                     rhs=a_codes[:].bitcast(FP8X4),
@@ -215,7 +216,7 @@ def tile_picked_ykrr_lin_po_kernel(
                     start=True,
                     stop=True,
                 )
-            stages.append((cols, width, y_ps))
+            stages.append((cols, width, y_ps, y_hi))
 
         ys = []
         end_cols = slice(V - CHUNK, V)
@@ -229,12 +230,13 @@ def tile_picked_ykrr_lin_po_kernel(
             y_bf.extend(group[:, first - start : first - start + width, :] for first, width in STAGES[s0 : s1 + 1])
 
         def results(s):
-            cols, width, y_ps = stages[s]
+            cols, width, y_ps, y_hi = stages[s]
             copy = nc.vector.tensor_copy if s in BY_VECTOR else nc.scalar.copy
             if cols.start < end_cols.start:
                 y = keep.tile([P, PACK, width], F32, name="y%d" % s)
-                copy(y[:], y_ps[:])
-                nc.sync.dma_start(out_rows[:, :, cols], y[:])
+                for rows, bank in ((slice(0, 2), y_ps), (slice(2, PACK), y_hi)) if s == 0 else ((slice(0, PACK), y_ps),):
+                    copy(y[:, rows, :], bank[:, rows, :])
+                    nc.sync.dma_start(out_rows[:, rows, cols], y[:, rows, :])
                 ys.append(y[:])
             else:
                 y_part = y_end[:, :, cols.start - end_cols.start : cols.stop - end_cols.start]
@@ -264,19 +266,18 @@ def tile_picked_ykrr_lin_po_kernel(
             kernels(c)
         for s in range(CHUNKS, len(STAGES)):
             kernels(s)
-        (first_stage, second_stage), *later_groups = GROUPS
-        for step in (results, rounded):
-            step(first_stage)
-            step(second_stage)
-        results(second_stage + 1)
-        quantised(second_stage)
-        for s in range(second_stage + 2, LAST):
-            results(s)
-            rounded(s - 1)
-        rounded(LAST - 1)
-        rounded(LAST)
-        for s0, s1 in later_groups:
-            quantised(s1)
+        results(0)
+        rounded(0)
+        results(1)
+        quantised(0)
+        results(2)
+        rounded(1)
+        results(3)
+        rounded(2)
+        rounded(3)
+        rounded(4)
+        quantised(2)
+        quantised(4)
 
         nc.sync.dma_start(out_words, y_codes[:].bitcast(I32))
         for q in range(QUADS):

@@ -35,7 +35,7 @@ STAGES = ((0, 128), (128, 128), (256, 128), (384, 64), (448, 64))
 LAST = len(STAGES) - 1
 RUN = 64
 BY_VECTOR = (0, 3)
-GROUPS = ((0, 0), (1, 2), (3, 4))
+GROUPS = ((0, 1), (2, 2), (3, 4))
 BY_SCALAR = 64
 SLOT_BY_SCALAR = 3
 
@@ -269,17 +269,18 @@ def tile_picked_ykrr_lin_po_kernel(
         results(0)
         rounded(0)
         results(1)
-        quantised(0)
         results(2)
         rounded(1)
         results(3)
+        quantised(1)
+        nc.sync.dma_start(out_words[:, : V // 2], y_codes[:, : V // 2].bitcast(I32))
         rounded(2)
         rounded(3)
         rounded(4)
         quantised(2)
         quantised(4)
 
-        nc.sync.dma_start(out_words, y_codes[:].bitcast(I32))
+        nc.sync.dma_start(out_words[:, V // 2 :], y_codes[:, V // 2 :].bitcast(I32))
         for q in range(QUADS):
             queue = nc.scalar if q % 2 else nc.sync
             queue.dma_start(

@@ -247,8 +247,8 @@ def tile_picked_ykrr_lin_po_kernel(
 
         def rounded(s):
             if s == LAST:
-                nc.scalar.copy(y_bf[s], stages[s][2][:].rearrange("p r n -> p n r"))
                 results(s)
+                nc.scalar.copy(y_bf[s], stages[s][2][:].rearrange("p r n -> p n r"))
             else:
                 nc.vector.tensor_copy(
                     y_bf[s].rearrange("p (g i) r -> p g r i", i=PACK),

@@ -82,19 +82,20 @@ def tile_picked_ykrr_lin_po_kernel(
         nc.sync.dma_start(xw[:].bitcast(I32), x_words[0].rearrange("p n r -> p (n r)").bitcast(I32))
         nc.sync.dma_start(ew[:].bitcast(I32), e_words[0].rearrange("p n r -> p (n r)").bitcast(I32))
 
+        own_sb = keep.tile([P, PACK], F32, name="own_sb")
+        nc.sync.dma_start(own_sb[:], own.rearrange("(p j) o -> p (j o)", j=PACK))
+
         size = keep.tile([P, PACK], F32, name="size")
         nc.vector.scalar_tensor_tensor(size[:], wgt_sb[:], -1.0, wgt_sb[:], ALU.mult, ALU.max)
         capped = keep.tile([P, PACK], F32, name="capped")
         nc.vector.tensor_scalar(capped[:], wgt_sb[:], LN_RANGE, 1.0, ALU.mult, ALU.min)
-        factors = keep.tile([P, 2, PACK], F32, name="factors", tag="factors")
+        factors = keep.tile([P, 2, PACK], F32, name="factors")
         nc.vector.tensor_scalar(factors[:, 0, :], size[:], 1.0 / LN_RANGE, LN_RANGE, ALU.max, ALU.min)
         nc.vector.tensor_scalar(factors[:, 1, :], size[:], 1.0 / LN_RANGE, 1.0, ALU.mult, ALU.max)
         unit = keep.tile([P, PACK], F32, name="unit")
         nc.vector.tensor_scalar(unit[:], capped[:], -1.0, 1.0, ALU.max, ALU.mult)
         logs = keep.tile([P, 2, PACK], F32, name="logs")
         nc.scalar.activation(logs[:], factors[:], ACT.Ln)
-        own_sb = keep.tile([P, PACK], F32, name="own_sb", tag="factors")
-        nc.scalar.dma_start(own_sb[:], own.rearrange("(p j) o -> p (j o)", j=PACK))
 
         hg = keep.tile([P, V], F32, name="hg")
         nc.scalar.activation(hg[:], hw[:].indirect(qry_sb[:]), ACT.Copy)
@@ -140,10 +141,10 @@ def tile_picked_ykrr_lin_po_kernel(
 
         ln_size = keep.tile([P, PACK], F32, name="ln_size")
         nc.gpsimd.tensor_tensor(ln_size[:], logs[:, 0, :], logs[:, 1, :], ALU.add)
-        bias = keep.tile([P, PACK], F32, name="bias")
-        nc.gpsimd.tensor_tensor(bias[:], ln_size[:], own_sb[:], ALU.add)
         bias2 = keep.tile([P, PACK], F32, name="bias2")
-        nc.gpsimd.tensor_tensor(bias2[:], bias[:], bias[:], ALU.add)
+        for j in range(PACK):
+            slot = slice(j, j + 1)
+            nc.gpsimd.tensor_scalar(bias2[:, slot], own_sb[:, slot], ln_size[:, slot], 2.0, ALU.add, ALU.mult)
 
         picked = []
         for first, width in PIECES:

@@ -29,14 +29,16 @@ ROW_STEP = QUAD // SCALE_ROWS
 LIST_ROWS = 16
 CHUNK = 128
 CHUNKS = V // CHUNK
+CLEARED_FIRST = 3 * STORE // 4
 LN_RANGE = 2.0**63
 PIECES = ((0, CHUNK), (CHUNK, CHUNK), (2 * CHUNK, 2 * CHUNK))
-STAGES = ((0, 128), (128, 128), (256, 128), (384, 64), (448, 64))
+STAGES = ((0, CHUNK), (CHUNK, CHUNK), (2 * CHUNK, CHUNK), (3 * CHUNK, CHUNK // 2), (3 * CHUNK + CHUNK // 2, CHUNK // 2))
 LAST = len(STAGES) - 1
 RUN = 64
-BY_VECTOR = (0, 3)
+BY_VECTOR = (0, LAST - 1)
 GROUPS = ((0, 1), (2, 2), (3, 4))
-BY_SCALAR = 64
+HALVES = (slice(0, PACK // 2), slice(PACK // 2, PACK))
+BY_SCALAR = 88
 SLOT_BY_SCALAR = 3
 
 
@@ -62,7 +64,7 @@ def tile_picked_ykrr_lin_po_kernel(
         nc.vector.memset(xs[:].bitcast(I32), 0)
         nc.vector.memset(es[:].bitcast(I32), 0)
         nc.vector.memset(ident[:], 0.0)
-        nc.vector.memset(hw[: P - 1, :].bitcast(I32), 0)
+        nc.vector.memset(hw[: P - 1, :CLEARED_FIRST].bitcast(I32), 0)
         make_identity(nc, ident[:], nomemset=True)
 
         def load_scales(table, scales):
@@ -81,7 +83,6 @@ def tile_picked_ykrr_lin_po_kernel(
         nc.sync.dma_start(dual_hi[:], dual_rows[:, PACK // 2 :, :])
         nc.sync.dma_start(xw[:].bitcast(I32), x_words[0].rearrange("p n r -> p (n r)").bitcast(I32))
         nc.sync.dma_start(ew[:].bitcast(I32), e_words[0].rearrange("p n r -> p (n r)").bitcast(I32))
-
         own_sb = keep.tile([P, PACK], F32, name="own_sb")
         nc.sync.dma_start(own_sb[:], own.rearrange("(p j) o -> p (j o)", j=PACK))
 
@@ -89,6 +90,7 @@ def tile_picked_ykrr_lin_po_kernel(
         nc.vector.scalar_tensor_tensor(size[:], wgt_sb[:], -1.0, wgt_sb[:], ALU.mult, ALU.max)
         capped = keep.tile([P, PACK], F32, name="capped")
         nc.vector.tensor_scalar(capped[:], wgt_sb[:], LN_RANGE, 1.0, ALU.mult, ALU.min)
+        nc.vector.memset(hw[: P - 1, CLEARED_FIRST:].bitcast(I32), 0)
         factors = keep.tile([P, 2, PACK], F32, name="factors")
         nc.vector.tensor_scalar(factors[:, 0, :], size[:], 1.0 / LN_RANGE, LN_RANGE, ALU.max, ALU.min)
         nc.vector.tensor_scalar(factors[:, 1, :], size[:], 1.0 / LN_RANGE, 1.0, ALU.mult, ALU.max)
@@ -209,7 +211,7 @@ def tile_picked_ykrr_lin_po_kernel(
             y_hi = ps_y.tile([P, PACK, width], F32, name="y_hi", tag="y_ps") if s == 0 else y_ps
             for r in range(PACK):
                 nc.tensor.matmul_mx(
-                    (y_ps, y_hi)[r // 2][:, r, :],
+                    (y_ps, y_ps, y_hi, y_hi)[r][:, r, :],
                     lhsT=d_codes[:, r * P : (r + 1) * P].bitcast(FP8X4),
                     lhsT_scale=d_scales[:, r * P : (r + 1) * P],
                     rhs=a_codes[:].bitcast(FP8X4),
@@ -235,7 +237,7 @@ def tile_picked_ykrr_lin_po_kernel(
             copy = nc.vector.tensor_copy if s in BY_VECTOR else nc.scalar.copy
             if cols.start < end_cols.start:
                 y = keep.tile([P, PACK, width], F32, name="y%d" % s)
-                for rows, bank in ((slice(0, 2), y_ps), (slice(2, PACK), y_hi)) if s == 0 else ((slice(0, PACK), y_ps),):
+                for rows, bank in zip(HALVES, (y_ps, y_hi)) if s == 0 else ((slice(0, PACK), y_ps),):
                     copy(y[:, rows, :], bank[:, rows, :])
                     nc.sync.dma_start(out_rows[:, rows, cols], y[:, rows, :])
                 ys.append(y[:])
@@ -248,7 +250,6 @@ def tile_picked_ykrr_lin_po_kernel(
 
         def rounded(s):
             if s == LAST:
-                results(s)
                 nc.scalar.copy(y_bf[s], stages[s][2][:].rearrange("p r n -> p n r"))
             else:
                 nc.vector.tensor_copy(
@@ -267,21 +268,24 @@ def tile_picked_ykrr_lin_po_kernel(
             kernels(c)
         for s in range(CHUNKS, len(STAGES)):
             kernels(s)
+        first_group, middle_group, last_group = (s1 for s0, s1 in GROUPS)
+        early_words = y_groups[first_group][0]
         results(0)
         rounded(0)
         results(1)
         results(2)
         rounded(1)
-        results(3)
-        quantised(1)
-        nc.sync.dma_start(out_words[:, : V // 2], y_codes[:, : V // 2].bitcast(I32))
+        results(LAST - 1)
+        quantised(first_group)
+        nc.sync.dma_start(out_words[:, early_words], y_codes[:, early_words].bitcast(I32))
         rounded(2)
-        rounded(3)
-        rounded(4)
-        quantised(2)
-        quantised(4)
+        rounded(LAST - 1)
+        results(LAST)
+        rounded(LAST)
+        quantised(middle_group)
+        quantised(last_group)
 
-        nc.sync.dma_start(out_words[:, V // 2 :], y_codes[:, V // 2 :].bitcast(I32))
+        nc.sync.dma_start(out_words[:, early_words.stop :], y_codes[:, early_words.stop :].bitcast(I32))
         for q in range(QUADS):
             queue = nc.scalar if q % 2 else nc.sync
             queue.dma_start(

@@ -1,3 +1,4 @@
+import math
 from contextlib import ExitStack
 
 import concourse.mybir as mybir
@@ -30,16 +31,17 @@ LIST_ROWS = 16
 CHUNK = 128
 CHUNKS = V // CHUNK
 CLEARED_FIRST = 3 * STORE // 4
-LN_RANGE = 2.0**63
+FLOOR = 2.0**-63
+SHRINK = 8.0
+BIT_LN = math.log(2.0) / 2**23
+BIT_OFFSET = (127.0 - 0.043) * math.log(2.0)
 PIECES = ((0, CHUNK), (CHUNK, CHUNK), (2 * CHUNK, 2 * CHUNK))
 STAGES = ((0, CHUNK), (CHUNK, CHUNK), (2 * CHUNK, CHUNK), (3 * CHUNK, CHUNK // 2), (3 * CHUNK + CHUNK // 2, CHUNK // 2))
 LAST = len(STAGES) - 1
 RUN = 64
-BY_VECTOR = (0, LAST - 1)
+BY_VECTOR = (1,)
 GROUPS = ((0, 1), (2, 2), (3, 4))
-HALVES = (slice(0, PACK // 2), slice(PACK // 2, PACK))
 BY_SCALAR = 88
-SLOT_BY_SCALAR = 3
 
 
 def tile_picked_ykrr_lin_po_kernel(
@@ -86,33 +88,52 @@ def tile_picked_ykrr_lin_po_kernel(
         own_sb = keep.tile([P, PACK], F32, name="own_sb")
         nc.sync.dma_start(own_sb[:], own.rearrange("(p j) o -> p (j o)", j=PACK))
 
-        size = keep.tile([P, PACK], F32, name="size")
-        nc.vector.scalar_tensor_tensor(size[:], wgt_sb[:], -1.0, wgt_sb[:], ALU.mult, ALU.max)
+        magnitude = keep.tile([P, PACK], F32, name="magnitude")
+        nc.vector.scalar_tensor_tensor(magnitude[:], wgt_sb[:], -1.0, wgt_sb[:], ALU.mult, ALU.max)
         capped = keep.tile([P, PACK], F32, name="capped")
-        nc.vector.tensor_scalar(capped[:], wgt_sb[:], LN_RANGE, 1.0, ALU.mult, ALU.min)
+        nc.vector.tensor_scalar(capped[:], wgt_sb[:], 1.0 / FLOOR, 1.0, ALU.mult, ALU.min)
         nc.vector.memset(hw[: P - 1, CLEARED_FIRST:].bitcast(I32), 0)
-        factors = keep.tile([P, 2, PACK], F32, name="factors")
-        nc.vector.tensor_scalar(factors[:, 0, :], size[:], 1.0 / LN_RANGE, LN_RANGE, ALU.max, ALU.min)
-        nc.vector.tensor_scalar(factors[:, 1, :], size[:], 1.0 / LN_RANGE, 1.0, ALU.mult, ALU.max)
+        size = keep.tile([P, PACK], F32, name="size")
+        nc.vector.tensor_scalar(size[:], magnitude[:], FLOOR, 1.0 / SHRINK, ALU.max, ALU.mult)
         unit = keep.tile([P, PACK], F32, name="unit")
         nc.vector.tensor_scalar(unit[:], capped[:], -1.0, 1.0, ALU.max, ALU.mult)
-        logs = keep.tile([P, 2, PACK], F32, name="logs")
-        nc.scalar.activation(logs[:], factors[:], ACT.Ln)
+
+        bits = size[:].bitcast(U32)
+        inverse0 = keep.tile([P, PACK], F32, name="inverse0")
+        nc.scalar.activation(inverse0[:], bits, ACT.Exp, scale=-BIT_LN, bias=BIT_OFFSET)
+        guess0 = keep.tile([P, PACK], F32, name="guess0")
+        nc.scalar.activation(guess0[:], bits, ACT.Copy, scale=BIT_LN, bias=-BIT_OFFSET - 1.0)
 
         hg = keep.tile([P, V], F32, name="hg")
         nc.scalar.activation(hg[:], hw[:].indirect(qry_sb[:]), ACT.Copy)
         spread = keep.tile([P, S + V], U8, name="spread")
         nc.vector.tensor_copy(spread[:, :S].rearrange("k (j p) -> k p j", j=PACK), xs[:].indirect(offs_sb[:]))
+        ratio0 = keep.tile([P, PACK], F32, name="ratio0")
+        nc.vector.tensor_tensor(ratio0[:], size[:], inverse0[:], ALU.mult)
 
         dual_r = keep.tile([P, PACK, N], BF16, name="dual_r", tag="dual_r")
         for j in range(PACK):
             rows = (dual_lo, dual_hi)[j // 2][:, j % 2, :]
-            if j == SLOT_BY_SCALAR:
+            if j == PACK - 1:
                 nc.scalar.activation(dual_r[:, j, :], rows, ACT.Copy, scale=unit[:, j : j + 1])
             else:
                 nc.gpsimd.tensor_scalar(dual_r[:, j, :], rows, unit[:, j : j + 1], 0.0, ALU.mult, ALU.add)
 
         nc.vector.tensor_copy(spread[:, S:], es[:].indirect(qry_sb[:]))
+        guess1 = keep.tile([P, PACK], F32, name="guess1")
+        nc.vector.tensor_tensor(guess1[:], ratio0[:], guess0[:], ALU.add)
+        inverse1 = keep.tile([P, PACK], F32, name="inverse1")
+        nc.scalar.activation(inverse1[:], guess1[:], ACT.Exp, scale=-1.0)
+        head = keep.tile([P, PACK], F32, name="head")
+        nc.gpsimd.tensor_scalar(head[:], guess1[:], 2.0, 2.0 * math.log(SHRINK) - 3.0, ALU.mult, ALU.add)
+        ratio1 = keep.tile([P, PACK], F32, name="ratio1")
+        nc.gpsimd.tensor_tensor(ratio1[:], size[:], inverse1[:], ALU.mult)
+        rest = keep.tile([P, PACK], F32, name="rest")
+        nc.gpsimd.tensor_scalar(rest[:], ratio1[:], -1.0, 4.0, ALU.mult, ALU.add)
+        series = keep.tile([P, PACK], F32, name="series")
+        nc.gpsimd.tensor_tensor(series[:], rest[:], ratio1[:], ALU.mult)
+        ln2x = keep.tile([P, PACK], F32, name="ln2x")
+        nc.gpsimd.tensor_tensor(ln2x[:], series[:], head[:], ALU.add)
         placed = keep.tile([P, S + V], U8, name="placed", align_bytes=64)
         nc.vector.tensor_copy(placed[:].bitcast(I32), spread[:].bitcast(I32))
         for i in range(1, SCALE_ROWS):
@@ -141,12 +162,10 @@ def tile_picked_ykrr_lin_po_kernel(
         minus_half2 = keep.tile([P, V], F32, name="minus_half2", tag="dual_r")
         nc.scalar.activation(minus_half2[:], h_rows[:], ACT.Copy, scale=-2.0)
 
-        ln_size = keep.tile([P, PACK], F32, name="ln_size")
-        nc.gpsimd.tensor_tensor(ln_size[:], logs[:, 0, :], logs[:, 1, :], ALU.add)
         bias2 = keep.tile([P, PACK], F32, name="bias2")
         for j in range(PACK):
             slot = slice(j, j + 1)
-            nc.gpsimd.tensor_scalar(bias2[:, slot], own_sb[:, slot], ln_size[:, slot], 2.0, ALU.add, ALU.mult)
+            nc.scalar.activation(bias2[:, slot], own_sb[:, slot], ACT.Identity, scale=2.0, bias=ln2x[:, slot])
 
         picked = []
         for first, width in PIECES:
@@ -190,28 +209,29 @@ def tile_picked_ykrr_lin_po_kernel(
                         ALU.add,
                     )
 
-        stages = []
+        a_bf = {}
+        banks = {}
 
         def kernels(s):
             first, width = STAGES[s]
-            cols = slice(first, first + width)
-            a_bf = keep.tile([P, width, PACK], BF16, name="a_bf%d" % first, align_bytes=64)
+            a_bf[s] = keep.tile([P, width, PACK], BF16, name="a_bf%d" % first, align_bytes=64)
             for n in range(0, width, RUN):
                 nc.scalar.activation(
-                    a_bf[:, n : n + RUN, :].rearrange("p (g i) j -> p g j i", i=PACK),
+                    a_bf[s][:, n : n + RUN, :].rearrange("p (g i) j -> p g j i", i=PACK),
                     z2[first + n][:].rearrange("p j (g i) -> p g j i", i=PACK),
                     ACT.Exp,
                     scale=0.5,
                 )
+
+        def products(s):
+            first, width = STAGES[s]
             a_codes = keep.tile([P, width], U32, name="a_codes%d" % first, align_bytes=64)
             a_scales = keep.tile([P, width], U8, name="a_scales%d" % first, align_bytes=64)
-            nc.vector.quantize_mx(a_codes[:].bitcast(FP8X4), a_scales[:], a_bf[:].rearrange("p n j -> p (n j)"))
-
-            y_ps = ps_y.tile([P, PACK, width], F32, name="y_ps")
-            y_hi = ps_y.tile([P, PACK, width], F32, name="y_hi", tag="y_ps") if s == 0 else y_ps
+            nc.vector.quantize_mx(a_codes[:].bitcast(FP8X4), a_scales[:], a_bf[s][:].rearrange("p n j -> p (n j)"))
+            banks[s] = ps_y.tile([P, PACK, width], F32, name="y_ps")
             for r in range(PACK):
                 nc.tensor.matmul_mx(
-                    (y_ps, y_ps, y_hi, y_hi)[r][:, r, :],
+                    banks[s][:, r, :],
                     lhsT=d_codes[:, r * P : (r + 1) * P].bitcast(FP8X4),
                     lhsT_scale=d_scales[:, r * P : (r + 1) * P],
                     rhs=a_codes[:].bitcast(FP8X4),
@@ -219,9 +239,8 @@ def tile_picked_ykrr_lin_po_kernel(
                     start=True,
                     stop=True,
                 )
-            stages.append((cols, width, y_ps, y_hi))
 
-        ys = []
+        ys = {}
         end_cols = slice(V - CHUNK, V)
         y_end = keep.tile([P, PACK, CHUNK], F32, name="y_end")
         y_bf = []
@@ -233,24 +252,22 @@ def tile_picked_ykrr_lin_po_kernel(
             y_bf.extend(group[:, first - start : first - start + width, :] for first, width in STAGES[s0 : s1 + 1])
 
         def results(s):
-            cols, width, y_ps, y_hi = stages[s]
+            first, width = STAGES[s]
             copy = nc.vector.tensor_copy if s in BY_VECTOR else nc.scalar.copy
-            if cols.start < end_cols.start:
+            if first < end_cols.start:
                 y = keep.tile([P, PACK, width], F32, name="y%d" % s)
-                for rows, bank in zip(HALVES, (y_ps, y_hi)) if s == 0 else ((slice(0, PACK), y_ps),):
-                    copy(y[:, rows, :], bank[:, rows, :])
-                    nc.sync.dma_start(out_rows[:, rows, cols], y[:, rows, :])
-                ys.append(y[:])
+                copy(y[:], banks[s][:])
+                nc.sync.dma_start(out_rows[:, :, first : first + width], y[:])
+                ys[s] = y[:]
             else:
-                y_part = y_end[:, :, cols.start - end_cols.start : cols.stop - end_cols.start]
-                copy(y_part, y_ps[:])
-                ys.append(y_part)
+                ys[s] = y_end[:, :, first - end_cols.start : first + width - end_cols.start]
+                copy(ys[s], banks[s][:])
                 if s == LAST:
                     nc.scalar.dma_start(out_rows[:, :, end_cols], y_end[:])
 
         def rounded(s):
             if s == LAST:
-                nc.scalar.copy(y_bf[s], stages[s][2][:].rearrange("p r n -> p n r"))
+                nc.scalar.copy(y_bf[s], banks[s][:].rearrange("p r n -> p n r"))
             else:
                 nc.vector.tensor_copy(
                     y_bf[s].rearrange("p (g i) r -> p g r i", i=PACK),
@@ -263,23 +280,27 @@ def tile_picked_ykrr_lin_po_kernel(
                 y_codes[:, cols].bitcast(FP8X4), y_scales[:, cols], group[:].rearrange("p n r -> p (n r)")
             )
 
-        for c in range(CHUNKS):
-            exponents(c)
-            kernels(c)
-        for s in range(CHUNKS, len(STAGES)):
-            kernels(s)
         first_group, middle_group, last_group = (s1 for s0, s1 in GROUPS)
         early_words = y_groups[first_group][0]
+        for c in range(CHUNKS - 1):
+            exponents(c)
+            kernels(c)
+            products(c)
         results(0)
-        rounded(0)
+        exponents(3)
+        kernels(3)
+        kernels(4)
         results(1)
+        products(3)
+        products(4)
+        rounded(0)
         results(2)
         rounded(1)
-        results(LAST - 1)
+        results(3)
         quantised(first_group)
         nc.sync.dma_start(out_words[:, early_words], y_codes[:, early_words].bitcast(I32))
         rounded(2)
-        rounded(LAST - 1)
+        rounded(3)
         results(LAST)
         rounded(LAST)
         quantised(middle_group)

@@ -30,16 +30,15 @@ ROW_STEP = QUAD // SCALE_ROWS
 LIST_ROWS = 16
 CHUNK = 128
 CHUNKS = V // CHUNK
-CLEARED_FIRST = 3 * STORE // 4
-FLOOR = 2.0**-63
-SHRINK = 8.0
+SHRINK = 16.0
 BIT_LN = math.log(2.0) / 2**23
 BIT_OFFSET = (127.0 - 0.043) * math.log(2.0)
 PIECES = ((0, CHUNK), (CHUNK, CHUNK), (2 * CHUNK, 2 * CHUNK))
 STAGES = ((0, CHUNK), (CHUNK, CHUNK), (2 * CHUNK, CHUNK), (3 * CHUNK, CHUNK // 2), (3 * CHUNK + CHUNK // 2, CHUNK // 2))
 LAST = len(STAGES) - 1
 RUN = 64
-BY_VECTOR = (1,)
+BY_VECTOR = (0, LAST - 1)
+HALVES = (slice(0, PACK // 2), slice(PACK // 2, PACK))
 GROUPS = ((0, 1), (2, 2), (3, 4))
 BY_SCALAR = 88
 
@@ -66,7 +65,7 @@ def tile_picked_ykrr_lin_po_kernel(
         nc.vector.memset(xs[:].bitcast(I32), 0)
         nc.vector.memset(es[:].bitcast(I32), 0)
         nc.vector.memset(ident[:], 0.0)
-        nc.vector.memset(hw[: P - 1, :CLEARED_FIRST].bitcast(I32), 0)
+        nc.vector.memset(hw[: P - 1, :].bitcast(I32), 0)
         make_identity(nc, ident[:], nomemset=True)
 
         def load_scales(table, scales):
@@ -88,15 +87,10 @@ def tile_picked_ykrr_lin_po_kernel(
         own_sb = keep.tile([P, PACK], F32, name="own_sb")
         nc.sync.dma_start(own_sb[:], own.rearrange("(p j) o -> p (j o)", j=PACK))
 
-        magnitude = keep.tile([P, PACK], F32, name="magnitude")
-        nc.vector.scalar_tensor_tensor(magnitude[:], wgt_sb[:], -1.0, wgt_sb[:], ALU.mult, ALU.max)
-        capped = keep.tile([P, PACK], F32, name="capped")
-        nc.vector.tensor_scalar(capped[:], wgt_sb[:], 1.0 / FLOOR, 1.0, ALU.mult, ALU.min)
-        nc.vector.memset(hw[: P - 1, CLEARED_FIRST:].bitcast(I32), 0)
         size = keep.tile([P, PACK], F32, name="size")
-        nc.vector.tensor_scalar(size[:], magnitude[:], FLOOR, 1.0 / SHRINK, ALU.max, ALU.mult)
+        nc.scalar.activation(size[:], wgt_sb[:], ACT.Abs, scale=1.0 / SHRINK)
         unit = keep.tile([P, PACK], F32, name="unit")
-        nc.vector.tensor_scalar(unit[:], capped[:], -1.0, 1.0, ALU.max, ALU.mult)
+        nc.scalar.activation(unit[:], wgt_sb[:], ACT.Sign)
 
         bits = size[:].bitcast(U32)
         inverse0 = keep.tile([P, PACK], F32, name="inverse0")
@@ -108,8 +102,6 @@ def tile_picked_ykrr_lin_po_kernel(
         nc.scalar.activation(hg[:], hw[:].indirect(qry_sb[:]), ACT.Copy)
         spread = keep.tile([P, S + V], U8, name="spread")
         nc.vector.tensor_copy(spread[:, :S].rearrange("k (j p) -> k p j", j=PACK), xs[:].indirect(offs_sb[:]))
-        ratio0 = keep.tile([P, PACK], F32, name="ratio0")
-        nc.vector.tensor_tensor(ratio0[:], size[:], inverse0[:], ALU.mult)
 
         dual_r = keep.tile([P, PACK, N], BF16, name="dual_r", tag="dual_r")
         for j in range(PACK):
@@ -120,16 +112,18 @@ def tile_picked_ykrr_lin_po_kernel(
                 nc.gpsimd.tensor_scalar(dual_r[:, j, :], rows, unit[:, j : j + 1], 0.0, ALU.mult, ALU.add)
 
         nc.vector.tensor_copy(spread[:, S:], es[:].indirect(qry_sb[:]))
+        ratio0 = keep.tile([P, PACK], F32, name="ratio0")
+        nc.gpsimd.tensor_tensor(ratio0[:], size[:], inverse0[:], ALU.mult)
         guess1 = keep.tile([P, PACK], F32, name="guess1")
-        nc.vector.tensor_tensor(guess1[:], ratio0[:], guess0[:], ALU.add)
+        nc.gpsimd.tensor_tensor(guess1[:], ratio0[:], guess0[:], ALU.add)
         inverse1 = keep.tile([P, PACK], F32, name="inverse1")
-        nc.scalar.activation(inverse1[:], guess1[:], ACT.Exp, scale=-1.0)
+        nc.scalar.activation(inverse1[:], guess1[:], ACT.Exp, scale=-1.0, bias=-1.0)
         head = keep.tile([P, PACK], F32, name="head")
         nc.gpsimd.tensor_scalar(head[:], guess1[:], 2.0, 2.0 * math.log(SHRINK) - 3.0, ALU.mult, ALU.add)
         ratio1 = keep.tile([P, PACK], F32, name="ratio1")
         nc.gpsimd.tensor_tensor(ratio1[:], size[:], inverse1[:], ALU.mult)
         rest = keep.tile([P, PACK], F32, name="rest")
-        nc.gpsimd.tensor_scalar(rest[:], ratio1[:], -1.0, 4.0, ALU.mult, ALU.add)
+        nc.gpsimd.tensor_scalar(rest[:], ratio1[:], -math.e * math.e, 4.0 * math.e, ALU.mult, ALU.add)
         series = keep.tile([P, PACK], F32, name="series")
         nc.gpsimd.tensor_tensor(series[:], rest[:], ratio1[:], ALU.mult)
         ln2x = keep.tile([P, PACK], F32, name="ln2x")
@@ -167,12 +161,10 @@ def tile_picked_ykrr_lin_po_kernel(
             slot = slice(j, j + 1)
             nc.scalar.activation(bias2[:, slot], own_sb[:, slot], ACT.Identity, scale=2.0, bias=ln2x[:, slot])
 
-        picked = []
+        ew_g = keep.tile([P, V], U32, name="ew_g", align_bytes=64)
         for first, width in PIECES:
             entries = qry_sb[:, first // LIST_ROWS : (first + width) // LIST_ROWS]
-            ew_g = keep.tile([P, width], U32, name="ew_g%d" % first, align_bytes=64)
-            nc.vector.tensor_copy(ew_g[:], ew[:].indirect(entries))
-            picked.extend(ew_g[:, c : c + CHUNK] for c in range(0, width, CHUNK))
+            nc.vector.tensor_copy(ew_g[:, first : first + width], ew[:].indirect(entries))
 
         y_codes = keep.tile([P, V], U32, name="y_codes", align_bytes=64)
         y_scales = keep.tile([P, V], U8, name="y_scales", align_bytes=64)
@@ -190,7 +182,7 @@ def tile_picked_ykrr_lin_po_kernel(
                     s_ps[j][:, j, :],
                     lhsT=xw_d[:, j * P : (j + 1) * P].bitcast(FP8X4),
                     lhsT_scale=placed[:, j * P : (j + 1) * P],
-                    rhs=picked[c].bitcast(FP8X4),
+                    rhs=ew_g[:, c * CHUNK : (c + 1) * CHUNK].bitcast(FP8X4),
                     rhs_scale=placed[:, S + c * CHUNK : S + (c + 1) * CHUNK],
                     start=True,
                     stop=True,
@@ -209,29 +201,28 @@ def tile_picked_ykrr_lin_po_kernel(
                         ALU.add,
                     )
 
-        a_bf = {}
-        banks = {}
+        stages = []
 
         def kernels(s):
             first, width = STAGES[s]
-            a_bf[s] = keep.tile([P, width, PACK], BF16, name="a_bf%d" % first, align_bytes=64)
+            cols = slice(first, first + width)
+            a_bf = keep.tile([P, width, PACK], BF16, name="a_bf%d" % first, align_bytes=64)
             for n in range(0, width, RUN):
                 nc.scalar.activation(
-                    a_bf[s][:, n : n + RUN, :].rearrange("p (g i) j -> p g j i", i=PACK),
+                    a_bf[:, n : n + RUN, :].rearrange("p (g i) j -> p g j i", i=PACK),
                     z2[first + n][:].rearrange("p j (g i) -> p g j i", i=PACK),
                     ACT.Exp,
                     scale=0.5,
                 )
-
-        def products(s):
-            first, width = STAGES[s]
             a_codes = keep.tile([P, width], U32, name="a_codes%d" % first, align_bytes=64)
             a_scales = keep.tile([P, width], U8, name="a_scales%d" % first, align_bytes=64)
-            nc.vector.quantize_mx(a_codes[:].bitcast(FP8X4), a_scales[:], a_bf[s][:].rearrange("p n j -> p (n j)"))
-            banks[s] = ps_y.tile([P, PACK, width], F32, name="y_ps")
+            nc.vector.quantize_mx(a_codes[:].bitcast(FP8X4), a_scales[:], a_bf[:].rearrange("p n j -> p (n j)"))
+
+            y_ps = ps_y.tile([P, PACK, width], F32, name="y_ps")
+            y_hi = ps_y.tile([P, PACK, width], F32, name="y_hi", tag="y_ps") if s == 0 else y_ps
             for r in range(PACK):
                 nc.tensor.matmul_mx(
-                    banks[s][:, r, :],
+                    (y_ps, y_ps, y_hi, y_hi)[r][:, r, :],
                     lhsT=d_codes[:, r * P : (r + 1) * P].bitcast(FP8X4),
                     lhsT_scale=d_scales[:, r * P : (r + 1) * P],
                     rhs=a_codes[:].bitcast(FP8X4),
@@ -239,8 +230,9 @@ def tile_picked_ykrr_lin_po_kernel(
                     start=True,
                     stop=True,
                 )
+            stages.append((cols, width, y_ps, y_hi))
 
-        ys = {}
+        ys = []
         end_cols = slice(V - CHUNK, V)
         y_end = keep.tile([P, PACK, CHUNK], F32, name="y_end")
         y_bf = []
@@ -252,22 +244,24 @@ def tile_picked_ykrr_lin_po_kernel(
             y_bf.extend(group[:, first - start : first - start + width, :] for first, width in STAGES[s0 : s1 + 1])
 
         def results(s):
-            first, width = STAGES[s]
+            cols, width, y_ps, y_hi = stages[s]
             copy = nc.vector.tensor_copy if s in BY_VECTOR else nc.scalar.copy
-            if first < end_cols.start:
+            if cols.start < end_cols.start:
                 y = keep.tile([P, PACK, width], F32, name="y%d" % s)
-                copy(y[:], banks[s][:])
-                nc.sync.dma_start(out_rows[:, :, first : first + width], y[:])
-                ys[s] = y[:]
+                for rows, bank in zip(HALVES, (y_ps, y_hi)) if s == 0 else ((slice(0, PACK), y_ps),):
+                    copy(y[:, rows, :], bank[:, rows, :])
+                    nc.sync.dma_start(out_rows[:, rows, cols], y[:, rows, :])
+                ys.append(y[:])
             else:
-                ys[s] = y_end[:, :, first - end_cols.start : first + width - end_cols.start]
-                copy(ys[s], banks[s][:])
+                y_part = y_end[:, :, cols.start - end_cols.start : cols.stop - end_cols.start]
+                copy(y_part, y_ps[:])
+                ys.append(y_part)
                 if s == LAST:
                     nc.scalar.dma_start(out_rows[:, :, end_cols], y_end[:])
 
         def rounded(s):
             if s == LAST:
-                nc.scalar.copy(y_bf[s], banks[s][:].rearrange("p r n -> p n r"))
+                nc.scalar.copy(y_bf[s], stages[s][2][:].rearrange("p r n -> p n r"))
             else:
                 nc.vector.tensor_copy(
                     y_bf[s].rearrange("p (g i) r -> p g r i", i=PACK),
@@ -280,27 +274,23 @@ def tile_picked_ykrr_lin_po_kernel(
                 y_codes[:, cols].bitcast(FP8X4), y_scales[:, cols], group[:].rearrange("p n r -> p (n r)")
             )
 
-        first_group, middle_group, last_group = (s1 for s0, s1 in GROUPS)
-        early_words = y_groups[first_group][0]
-        for c in range(CHUNKS - 1):
+        for c in range(CHUNKS):
             exponents(c)
             kernels(c)
-            products(c)
+        for s in range(CHUNKS, len(STAGES)):
+            kernels(s)
+        first_group, middle_group, last_group = (s1 for s0, s1 in GROUPS)
+        early_words = y_groups[first_group][0]
         results(0)
-        exponents(3)
-        kernels(3)
-        kernels(4)
-        results(1)
-        products(3)
-        products(4)
         rounded(0)
+        results(1)
         results(2)
         rounded(1)
-        results(3)
+        results(LAST - 1)
         quantised(first_group)
         nc.sync.dma_start(out_words[:, early_words], y_codes[:, early_words].bitcast(I32))
         rounded(2)
-        rounded(3)
+        rounded(LAST - 1)
         results(LAST)
         rounded(LAST)
         quantised(middle_group)

@@ -74,10 +74,10 @@ def tile_picked_ykrr_lin_po_kernel(
         dual_rows = dual.rearrange("(p j) m -> p j m", j=PACK)
         dual_lo = keep.tile([P, PACK // 2, N], F32, name="dual_lo")
         dual_hi = keep.tile([P, PACK // 2, N], F32, name="dual_hi", tag="dual_hi", align_bytes=64)
+        nc.sync.dma_start(qry_sb[:], qry)
         nc.scalar.dma_start(wgt_sb[:], wgt.rearrange("(p j) o -> p (j o)", j=PACK))
         nc.scalar.dma_start(hw[P - 1 :, :], half[:1, :])
         nc.sync.dma_start(dual_lo[:], dual_rows[:, : PACK // 2, :])
-        nc.sync.dma_start(qry_sb[:], qry)
         nc.sync.dma_start(offs_sb[:], offs)
         load_scales(xs, x_scales)
         load_scales(es, e_scales)

@@ -27,6 +27,7 @@ QUADS = 4
 QUAD = P // QUADS
 SCALE_ROWS = 4
 ROW_STEP = QUAD // SCALE_ROWS
+DMA_ALIGN = 256
 LIST_ROWS = 16
 CHUNK = 128
 CHUNKS = V // CHUNK
@@ -54,11 +55,11 @@ def tile_picked_ykrr_lin_po_kernel(
 
         offs_sb = keep.tile([P, S // LIST_ROWS], U16, name="offs_sb")
         qry_sb = keep.tile([P, V // LIST_ROWS], U16, name="qry_sb")
-        xw = keep.tile([P, STORE], U32, name="xw")
-        ew = keep.tile([P, STORE], U32, name="ew", align_bytes=64)
-        xs = keep.tile([P, STORE], U8, name="xs")
-        es = keep.tile([P, STORE], U8, name="es")
-        hw = keep.tile([P, STORE], F32, name="hw")
+        xw = keep.tile([P, STORE], U32, name="xw", align_bytes=DMA_ALIGN)
+        ew = keep.tile([P, STORE], U32, name="ew", align_bytes=DMA_ALIGN)
+        xs = keep.tile([P, STORE], U8, name="xs", align_bytes=DMA_ALIGN)
+        es = keep.tile([P, STORE], U8, name="es", align_bytes=DMA_ALIGN)
+        hw = keep.tile([P, STORE], F32, name="hw", align_bytes=DMA_ALIGN)
         wgt_sb = keep.tile([P, PACK], F32, name="wgt_sb")
         ident = keep.tile([P, P], F32, name="ident")
 
@@ -72,8 +73,8 @@ def tile_picked_ykrr_lin_po_kernel(
             nc.sync.dma_start(table[::ROW_STEP, :].bitcast(I32), scales[0].bitcast(I32))
 
         dual_rows = dual.rearrange("(p j) m -> p j m", j=PACK)
-        dual_lo = keep.tile([P, PACK // 2, N], F32, name="dual_lo")
-        dual_hi = keep.tile([P, PACK // 2, N], F32, name="dual_hi", tag="dual_hi", align_bytes=64)
+        dual_lo = keep.tile([P, PACK // 2, N], F32, name="dual_lo", align_bytes=DMA_ALIGN)
+        dual_hi = keep.tile([P, PACK // 2, N], F32, name="dual_hi", tag="dual_hi", align_bytes=DMA_ALIGN)
         nc.sync.dma_start(qry_sb[:], qry)
         nc.scalar.dma_start(wgt_sb[:], wgt.rearrange("(p j) o -> p (j o)", j=PACK))
         nc.scalar.dma_start(hw[P - 1 :, :], half[:1, :])
@@ -97,10 +98,16 @@ def tile_picked_ykrr_lin_po_kernel(
         nc.scalar.activation(inverse0[:], bits, ACT.Exp, scale=-BIT_LN, bias=BIT_OFFSET)
         guess0 = keep.tile([P, PACK], F32, name="guess0")
         nc.scalar.activation(guess0[:], bits, ACT.Copy, scale=BIT_LN, bias=-BIT_OFFSET - 1.0)
+        guess1 = keep.tile([P, PACK], F32, name="guess1")
+        for j in range(PACK):
+            slot = slice(j, j + 1)
+            nc.scalar.activation(
+                guess1[:, slot], inverse0[:, slot], ACT.Identity, scale=size[:, slot], bias=guess0[:, slot]
+            )
 
         hg = keep.tile([P, V], F32, name="hg")
         nc.scalar.activation(hg[:], hw[:].indirect(qry_sb[:]), ACT.Copy)
-        spread = keep.tile([P, S + V], U8, name="spread")
+        spread = keep.tile([P, S + V], U8, name="spread", align_bytes=DMA_ALIGN)
         nc.vector.tensor_copy(spread[:, :S].rearrange("k (j p) -> k p j", j=PACK), xs[:].indirect(offs_sb[:]))
 
         dual_r = keep.tile([P, PACK, N], BF16, name="dual_r", tag="dual_r")
@@ -112,10 +119,6 @@ def tile_picked_ykrr_lin_po_kernel(
                 nc.gpsimd.tensor_scalar(dual_r[:, j, :], rows, unit[:, j : j + 1], 0.0, ALU.mult, ALU.add)
 
         nc.vector.tensor_copy(spread[:, S:], es[:].indirect(qry_sb[:]))
-        ratio0 = keep.tile([P, PACK], F32, name="ratio0")
-        nc.gpsimd.tensor_tensor(ratio0[:], size[:], inverse0[:], ALU.mult)
-        guess1 = keep.tile([P, PACK], F32, name="guess1")
-        nc.gpsimd.tensor_tensor(guess1[:], ratio0[:], guess0[:], ALU.add)
         inverse1 = keep.tile([P, PACK], F32, name="inverse1")
         nc.scalar.activation(inverse1[:], guess1[:], ACT.Exp, scale=-1.0, bias=-1.0)
         head = keep.tile([P, PACK], F32, name="head")
@@ -128,7 +131,7 @@ def tile_picked_ykrr_lin_po_kernel(
         nc.gpsimd.tensor_tensor(series[:], rest[:], ratio1[:], ALU.mult)
         ln2x = keep.tile([P, PACK], F32, name="ln2x")
         nc.gpsimd.tensor_tensor(ln2x[:], series[:], head[:], ALU.add)
-        placed = keep.tile([P, S + V], U8, name="placed", align_bytes=64)
+        placed = keep.tile([P, S + V], U8, name="placed", align_bytes=DMA_ALIGN)
         nc.vector.tensor_copy(placed[:].bitcast(I32), spread[:].bitcast(I32))
         for i in range(1, SCALE_ROWS):
             nc.sync.dma_start(placed[i::QUAD, :].bitcast(I32), spread[ROW_STEP * i :: QUAD, :].bitcast(I32))
@@ -150,7 +153,7 @@ def tile_picked_ykrr_lin_po_kernel(
                 dual_bf[:, :, c0:c1, :].rearrange("p r c j -> p c j r"),
                 dual_r[:, :, PACK * c0 : PACK * c1].rearrange("p j (c r) -> p c j r", r=PACK),
             )
-        xw_d = keep.tile([P, S], U32, name="xw_d", tag="dual_hi", align_bytes=64)
+        xw_d = keep.tile([P, S], U32, name="xw_d", tag="dual_hi", align_bytes=DMA_ALIGN)
         nc.vector.tensor_copy(xw_d[:].rearrange("k (j p) -> k p j", j=PACK), xw[:].indirect(offs_sb[:]))
         nc.vector.quantize_mx(d_codes[:].bitcast(FP8X4), d_scales[:], dual_bf[:].rearrange("p r c j -> p (r c j)"))
         minus_half2 = keep.tile([P, V], F32, name="minus_half2", tag="dual_r")
@@ -166,8 +169,8 @@ def tile_picked_ykrr_lin_po_kernel(
             entries = qry_sb[:, first // LIST_ROWS : (first + width) // LIST_ROWS]
             nc.vector.tensor_copy(ew_g[:, first : first + width], ew[:].indirect(entries))
 
-        y_codes = keep.tile([P, V], U32, name="y_codes", align_bytes=64)
-        y_scales = keep.tile([P, V], U8, name="y_scales", align_bytes=64)
+        y_codes = keep.tile([P, V], U32, name="y_codes", align_bytes=DMA_ALIGN)
+        y_scales = keep.tile([P, V], U8, name="y_scales", align_bytes=DMA_ALIGN)
         out_rows = out_0.rearrange("(p r) v -> p r v", r=PACK)
         out_words = out_1[0].rearrange("p n r -> p (n r)").bitcast(I32)
 
@@ -234,7 +237,7 @@ def tile_picked_ykrr_lin_po_kernel(
 
         ys = []
         end_cols = slice(V - CHUNK, V)
-        y_end = keep.tile([P, PACK, CHUNK], F32, name="y_end")
+        y_end = keep.tile([P, PACK, CHUNK], F32, name="y_end", align_bytes=DMA_ALIGN)
         y_bf = []
         y_groups = {}
         for s0, s1 in GROUPS:
@@ -247,7 +250,7 @@ def tile_picked_ykrr_lin_po_kernel(
             cols, width, y_ps, y_hi = stages[s]
             copy = nc.vector.tensor_copy if s in BY_VECTOR else nc.scalar.copy
             if cols.start < end_cols.start:
-                y = keep.tile([P, PACK, width], F32, name="y%d" % s)
+                y = keep.tile([P, PACK, width], F32, name="y%d" % s, align_bytes=DMA_ALIGN)
                 for rows, bank in zip(HALVES, (y_ps, y_hi)) if s == 0 else ((slice(0, PACK), y_ps),):
                     copy(y[:, rows, :], bank[:, rows, :])
                     nc.sync.dma_start(out_rows[:, rows, cols], y[:, rows, :])

@@ -34,14 +34,14 @@ CHUNKS = V // CHUNK
 SHRINK = 16.0
 BIT_LN = math.log(2.0) / 2**23
 BIT_OFFSET = (127.0 - 0.043) * math.log(2.0)
-PIECES = ((0, CHUNK), (CHUNK, CHUNK), (2 * CHUNK, 2 * CHUNK))
+PIECES = tuple((c * CHUNK, CHUNK) for c in range(CHUNKS))
 STAGES = ((0, CHUNK), (CHUNK, CHUNK), (2 * CHUNK, CHUNK), (3 * CHUNK, CHUNK // 2), (3 * CHUNK + CHUNK // 2, CHUNK // 2))
 LAST = len(STAGES) - 1
 RUN = 64
 BY_VECTOR = (0, LAST - 1)
 HALVES = (slice(0, PACK // 2), slice(PACK // 2, PACK))
 GROUPS = ((0, 1), (2, 2), (3, 4))
-BY_SCALAR = 88
+BY_SCALAR = 76
 
 
 def tile_picked_ykrr_lin_po_kernel(
@@ -75,8 +75,8 @@ def tile_picked_ykrr_lin_po_kernel(
         dual_rows = dual.rearrange("(p j) m -> p j m", j=PACK)
         dual_lo = keep.tile([P, PACK // 2, N], F32, name="dual_lo", align_bytes=DMA_ALIGN)
         dual_hi = keep.tile([P, PACK // 2, N], F32, name="dual_hi", tag="dual_hi", align_bytes=DMA_ALIGN)
+        nc.sync.dma_start(wgt_sb[:], wgt.rearrange("(p j) o -> p (j o)", j=PACK))
         nc.sync.dma_start(qry_sb[:], qry)
-        nc.scalar.dma_start(wgt_sb[:], wgt.rearrange("(p j) o -> p (j o)", j=PACK))
         nc.scalar.dma_start(hw[P - 1 :, :], half[:1, :])
         nc.sync.dma_start(dual_lo[:], dual_rows[:, : PACK // 2, :])
         nc.sync.dma_start(offs_sb[:], offs)
@@ -165,7 +165,9 @@ def tile_picked_ykrr_lin_po_kernel(
             nc.scalar.activation(bias2[:, slot], own_sb[:, slot], ACT.Identity, scale=2.0, bias=ln2x[:, slot])
 
         ew_g = keep.tile([P, V], U32, name="ew_g", align_bytes=64)
-        for first, width in PIECES:
+
+        def gather(c):
+            first, width = PIECES[c]
             entries = qry_sb[:, first // LIST_ROWS : (first + width) // LIST_ROWS]
             nc.vector.tensor_copy(ew_g[:, first : first + width], ew[:].indirect(entries))
 
@@ -277,7 +279,10 @@ def tile_picked_ykrr_lin_po_kernel(
                 y_codes[:, cols].bitcast(FP8X4), y_scales[:, cols], group[:].rearrange("p n r -> p (n r)")
             )
 
+        gather(0)
         for c in range(CHUNKS):
+            if c + 1 < CHUNKS:
+                gather(c + 1)
             exponents(c)
             kernels(c)
         for s in range(CHUNKS, len(STAGES)):

import math
from contextlib import ExitStack

import concourse.mybir as mybir
from concourse.masks import make_identity

K = 512
STORE = 2048
S = 512
V = 512
N = 512
FLOPS = 2 * K * S * V + 2 * S * N * V

F32 = mybir.dt.float32
BF16 = mybir.dt.bfloat16
I32 = mybir.dt.int32
U32 = mybir.dt.uint32
U16 = mybir.dt.uint16
U8 = mybir.dt.uint8
FP8X4 = mybir.dt.float8_e4m3fn_x4
ALU = mybir.AluOpType
ACT = mybir.ActivationFunctionType

P = 128
PACK = 4
QUADS = 4
QUAD = P // QUADS
SCALE_ROWS = 4
ROW_STEP = QUAD // SCALE_ROWS
DMA_ALIGN = 256
LIST_ROWS = 16
CHUNK = 128
CHUNKS = V // CHUNK
SHRINK = 16.0
BIT_LN = math.log(2.0) / 2**23
BIT_OFFSET = (127.0 - 0.043) * math.log(2.0)
PIECES = tuple((c * CHUNK, CHUNK) for c in range(CHUNKS))
STAGES = ((0, CHUNK), (CHUNK, CHUNK), (2 * CHUNK, CHUNK), (3 * CHUNK, CHUNK // 2), (3 * CHUNK + CHUNK // 2, CHUNK // 2))
LAST = len(STAGES) - 1
RUN = 64
BY_VECTOR = (0, LAST - 1)
HALVES = (slice(0, PACK // 2), slice(PACK // 2, PACK))
GROUPS = ((0, 1), (2, 2), (3, 4))
BY_SCALAR = 76


def tile_picked_ykrr_lin_po_kernel(
    tc, x_words, x_scales, e_words, e_scales, half, own, wgt, dual, offs, qry, out_0, out_1, out_2
):
    nc = tc.nc
    with ExitStack() as ctx:
        keep = ctx.enter_context(tc.tile_pool(name="keep", bufs=1))
        ps_s = ctx.enter_context(tc.psum_pool(name="ps_s", bufs=CHUNKS))
        ps_y = ctx.enter_context(tc.psum_pool(name="ps_y", bufs=CHUNKS))

        offs_sb = keep.tile([P, S // LIST_ROWS], U16, name="offs_sb")
        qry_sb = keep.tile([P, V // LIST_ROWS], U16, name="qry_sb")
        xw = keep.tile([P, STORE], U32, name="xw", align_bytes=DMA_ALIGN)
        ew = keep.tile([P, STORE], U32, name="ew", align_bytes=DMA_ALIGN)
        xs = keep.tile([P, STORE], U8, name="xs", align_bytes=DMA_ALIGN)
        es = keep.tile([P, STORE], U8, name="es", align_bytes=DMA_ALIGN)
        hw = keep.tile([P, STORE], F32, name="hw", align_bytes=DMA_ALIGN)
        wgt_sb = keep.tile([P, PACK], F32, name="wgt_sb")
        ident = keep.tile([P, P], F32, name="ident")

        nc.vector.memset(xs[:].bitcast(I32), 0)
        nc.vector.memset(es[:].bitcast(I32), 0)
        nc.vector.memset(ident[:], 0.0)
        nc.vector.memset(hw[: P - 1, :].bitcast(I32), 0)
        make_identity(nc, ident[:], nomemset=True)

        def load_scales(table, scales):
            nc.sync.dma_start(table[::ROW_STEP, :].bitcast(I32), scales[0].bitcast(I32))

        dual_rows = dual.rearrange("(p j) m -> p j m", j=PACK)
        dual_lo = keep.tile([P, PACK // 2, N], F32, name="dual_lo", align_bytes=DMA_ALIGN)
        dual_hi = keep.tile([P, PACK // 2, N], F32, name="dual_hi", tag="dual_hi", align_bytes=DMA_ALIGN)
        nc.sync.dma_start(wgt_sb[:], wgt.rearrange("(p j) o -> p (j o)", j=PACK))
        nc.sync.dma_start(qry_sb[:], qry)
        nc.scalar.dma_start(hw[P - 1 :, :], half[:1, :])
        nc.sync.dma_start(dual_lo[:], dual_rows[:, : PACK // 2, :])
        nc.sync.dma_start(offs_sb[:], offs)
        load_scales(xs, x_scales)
        load_scales(es, e_scales)
        nc.sync.dma_start(dual_hi[:], dual_rows[:, PACK // 2 :, :])
        nc.sync.dma_start(xw[:].bitcast(I32), x_words[0].rearrange("p n r -> p (n r)").bitcast(I32))
        nc.sync.dma_start(ew[:].bitcast(I32), e_words[0].rearrange("p n r -> p (n r)").bitcast(I32))
        own_sb = keep.tile([P, PACK], F32, name="own_sb")
        nc.sync.dma_start(own_sb[:], own.rearrange("(p j) o -> p (j o)", j=PACK))

        size = keep.tile([P, PACK], F32, name="size")
        nc.scalar.activation(size[:], wgt_sb[:], ACT.Abs, scale=1.0 / SHRINK)
        unit = keep.tile([P, PACK], F32, name="unit")
        nc.scalar.activation(unit[:], wgt_sb[:], ACT.Sign)

        bits = size[:].bitcast(U32)
        inverse0 = keep.tile([P, PACK], F32, name="inverse0")
        nc.scalar.activation(inverse0[:], bits, ACT.Exp, scale=-BIT_LN, bias=BIT_OFFSET)
        guess0 = keep.tile([P, PACK], F32, name="guess0")
        nc.scalar.activation(guess0[:], bits, ACT.Copy, scale=BIT_LN, bias=-BIT_OFFSET - 1.0)
        guess1 = keep.tile([P, PACK], F32, name="guess1")
        for j in range(PACK):
            slot = slice(j, j + 1)
            nc.scalar.activation(
                guess1[:, slot], inverse0[:, slot], ACT.Identity, scale=size[:, slot], bias=guess0[:, slot]
            )

        hg = keep.tile([P, V], F32, name="hg")
        nc.scalar.activation(hg[:], hw[:].indirect(qry_sb[:]), ACT.Copy)
        spread = keep.tile([P, S + V], U8, name="spread", align_bytes=DMA_ALIGN)
        nc.vector.tensor_copy(spread[:, :S].rearrange("k (j p) -> k p j", j=PACK), xs[:].indirect(offs_sb[:]))

        dual_r = keep.tile([P, PACK, N], BF16, name="dual_r", tag="dual_r")
        for j in range(PACK):
            rows = (dual_lo, dual_hi)[j // 2][:, j % 2, :]
            if j == PACK - 1:
                nc.scalar.activation(dual_r[:, j, :], rows, ACT.Copy, scale=unit[:, j : j + 1])
            else:
                nc.gpsimd.tensor_scalar(dual_r[:, j, :], rows, unit[:, j : j + 1], 0.0, ALU.mult, ALU.add)

        nc.vector.tensor_copy(spread[:, S:], es[:].indirect(qry_sb[:]))
        inverse1 = keep.tile([P, PACK], F32, name="inverse1")
        nc.scalar.activation(inverse1[:], guess1[:], ACT.Exp, scale=-1.0, bias=-1.0)
        head = keep.tile([P, PACK], F32, name="head")
        nc.gpsimd.tensor_scalar(head[:], guess1[:], 2.0, 2.0 * math.log(SHRINK) - 3.0, ALU.mult, ALU.add)
        ratio1 = keep.tile([P, PACK], F32, name="ratio1")
        nc.gpsimd.tensor_tensor(ratio1[:], size[:], inverse1[:], ALU.mult)
        rest = keep.tile([P, PACK], F32, name="rest")
        nc.gpsimd.tensor_scalar(rest[:], ratio1[:], -math.e * math.e, 4.0 * math.e, ALU.mult, ALU.add)
        series = keep.tile([P, PACK], F32, name="series")
        nc.gpsimd.tensor_tensor(series[:], rest[:], ratio1[:], ALU.mult)
        ln2x = keep.tile([P, PACK], F32, name="ln2x")
        nc.gpsimd.tensor_tensor(ln2x[:], series[:], head[:], ALU.add)
        placed = keep.tile([P, S + V], U8, name="placed", align_bytes=DMA_ALIGN)
        nc.vector.tensor_copy(placed[:].bitcast(I32), spread[:].bitcast(I32))
        for i in range(1, SCALE_ROWS):
            nc.sync.dma_start(placed[i::QUAD, :].bitcast(I32), spread[ROW_STEP * i :: QUAD, :].bitcast(I32))

        h_turned = ps_y.tile([P, V // P, P], F32, name="h_turned", tag="y_ps")
        for b in range(V // P):
            nc.tensor.transpose(h_turned[:, b, :], hg[:, b * P : (b + 1) * P], ident[:])
        h_col = keep.tile([P, V // P], F32, name="h_col")
        nc.scalar.copy(h_col[:], h_turned[:, :, P - 1])
        h_rows = ps_y.tile([P, V], F32, name="h_rows", tag="y_ps")
        for b in range(V // P):
            nc.tensor.transpose(h_rows[:, b * P : (b + 1) * P], h_col[:, b : b + 1].to_broadcast([P, P]), ident[:])

        d_codes = keep.tile([P, N], U32, name="d_codes", align_bytes=64)
        d_scales = keep.tile([P, N], U8, name="d_scales", align_bytes=64)
        dual_bf = keep.tile([P, PACK, P, PACK], BF16, name="dual_bf", align_bytes=64)
        for c0, c1, copy in ((0, BY_SCALAR, nc.scalar.copy), (BY_SCALAR, P, nc.vector.tensor_copy)):
            copy(
                dual_bf[:, :, c0:c1, :].rearrange("p r c j -> p c j r"),
                dual_r[:, :, PACK * c0 : PACK * c1].rearrange("p j (c r) -> p c j r", r=PACK),
            )
        xw_d = keep.tile([P, S], U32, name="xw_d", tag="dual_hi", align_bytes=DMA_ALIGN)
        nc.vector.tensor_copy(xw_d[:].rearrange("k (j p) -> k p j", j=PACK), xw[:].indirect(offs_sb[:]))
        nc.vector.quantize_mx(d_codes[:].bitcast(FP8X4), d_scales[:], dual_bf[:].rearrange("p r c j -> p (r c j)"))
        minus_half2 = keep.tile([P, V], F32, name="minus_half2", tag="dual_r")
        nc.scalar.activation(minus_half2[:], h_rows[:], ACT.Copy, scale=-2.0)

        bias2 = keep.tile([P, PACK], F32, name="bias2")
        for j in range(PACK):
            slot = slice(j, j + 1)
            nc.scalar.activation(bias2[:, slot], own_sb[:, slot], ACT.Identity, scale=2.0, bias=ln2x[:, slot])

        ew_g = keep.tile([P, V], U32, name="ew_g", align_bytes=64)

        def gather(c):
            first, width = PIECES[c]
            entries = qry_sb[:, first // LIST_ROWS : (first + width) // LIST_ROWS]
            nc.vector.tensor_copy(ew_g[:, first : first + width], ew[:].indirect(entries))

        y_codes = keep.tile([P, V], U32, name="y_codes", align_bytes=DMA_ALIGN)
        y_scales = keep.tile([P, V], U8, name="y_scales", align_bytes=DMA_ALIGN)
        out_rows = out_0.rearrange("(p r) v -> p r v", r=PACK)
        out_words = out_1[0].rearrange("p n r -> p (n r)").bitcast(I32)

        z2 = {}

        def exponents(c):
            s_lo = ps_s.tile([P, PACK, CHUNK], F32, name="s_ps")
            s_hi = ps_y.tile([P, PACK, CHUNK], F32, name="s_hi", tag="y_ps") if c == 0 else s_lo
            s_ps = (s_lo, s_lo, s_hi, s_hi)
            for j in range(PACK):
                nc.tensor.matmul_mx(
                    s_ps[j][:, j, :],
                    lhsT=xw_d[:, j * P : (j + 1) * P].bitcast(FP8X4),
                    lhsT_scale=placed[:, j * P : (j + 1) * P],
                    rhs=ew_g[:, c * CHUNK : (c + 1) * CHUNK].bitcast(FP8X4),
                    rhs_scale=placed[:, S + c * CHUNK : S + (c + 1) * CHUNK],
                    start=True,
                    stop=True,
                )
            for first in range(c * CHUNK, (c + 1) * CHUNK, RUN):
                part = slice(first % CHUNK, first % CHUNK + RUN)
                z = keep.tile([P, PACK, RUN], F32, name="z2_%d" % first)
                z2[first] = z
                for j in range(PACK):
                    nc.vector.scalar_tensor_tensor(
                        z[:, j, :],
                        s_ps[j][:, j, part],
                        bias2[:, j : j + 1],
                        minus_half2[:, first : first + RUN],
                        ALU.add,
                        ALU.add,
                    )

        stages = []

        def kernels(s):
            first, width = STAGES[s]
            cols = slice(first, first + width)
            a_bf = keep.tile([P, width, PACK], BF16, name="a_bf%d" % first, align_bytes=64)
            for n in range(0, width, RUN):
                nc.scalar.activation(
                    a_bf[:, n : n + RUN, :].rearrange("p (g i) j -> p g j i", i=PACK),
                    z2[first + n][:].rearrange("p j (g i) -> p g j i", i=PACK),
                    ACT.Exp,
                    scale=0.5,
                )
            a_codes = keep.tile([P, width], U32, name="a_codes%d" % first, align_bytes=64)
            a_scales = keep.tile([P, width], U8, name="a_scales%d" % first, align_bytes=64)
            nc.vector.quantize_mx(a_codes[:].bitcast(FP8X4), a_scales[:], a_bf[:].rearrange("p n j -> p (n j)"))

            y_ps = ps_y.tile([P, PACK, width], F32, name="y_ps")
            y_hi = ps_y.tile([P, PACK, width], F32, name="y_hi", tag="y_ps") if s == 0 else y_ps
            for r in range(PACK):
                nc.tensor.matmul_mx(
                    (y_ps, y_ps, y_hi, y_hi)[r][:, r, :],
                    lhsT=d_codes[:, r * P : (r + 1) * P].bitcast(FP8X4),
                    lhsT_scale=d_scales[:, r * P : (r + 1) * P],
                    rhs=a_codes[:].bitcast(FP8X4),
                    rhs_scale=a_scales[:],
                    start=True,
                    stop=True,
                )
            stages.append((cols, width, y_ps, y_hi))

        ys = []
        end_cols = slice(V - CHUNK, V)
        y_end = keep.tile([P, PACK, CHUNK], F32, name="y_end", align_bytes=DMA_ALIGN)
        y_bf = []
        y_groups = {}
        for s0, s1 in GROUPS:
            start, stop = STAGES[s0][0], sum(STAGES[s1])
            group = keep.tile([P, stop - start, PACK], BF16, name="y_bf%d" % s0, align_bytes=64)
            y_groups[s1] = (slice(start, stop), group)
            y_bf.extend(group[:, first - start : first - start + width, :] for first, width in STAGES[s0 : s1 + 1])

        def results(s):
            cols, width, y_ps, y_hi = stages[s]
            copy = nc.vector.tensor_copy if s in BY_VECTOR else nc.scalar.copy
            if cols.start < end_cols.start:
                y = keep.tile([P, PACK, width], F32, name="y%d" % s, align_bytes=DMA_ALIGN)
                for rows, bank in zip(HALVES, (y_ps, y_hi)) if s == 0 else ((slice(0, PACK), y_ps),):
                    copy(y[:, rows, :], bank[:, rows, :])
                    nc.sync.dma_start(out_rows[:, rows, cols], y[:, rows, :])
                ys.append(y[:])
            else:
                y_part = y_end[:, :, cols.start - end_cols.start : cols.stop - end_cols.start]
                copy(y_part, y_ps[:])
                ys.append(y_part)
                if s == LAST:
                    nc.scalar.dma_start(out_rows[:, :, end_cols], y_end[:])

        def rounded(s):
            if s == LAST:
                nc.scalar.copy(y_bf[s], stages[s][2][:].rearrange("p r n -> p n r"))
            else:
                nc.vector.tensor_copy(
                    y_bf[s].rearrange("p (g i) r -> p g r i", i=PACK),
                    ys[s].rearrange("p r (g i) -> p g r i", i=PACK),
                )

        def quantised(s):
            cols, group = y_groups[s]
            nc.vector.quantize_mx(
                y_codes[:, cols].bitcast(FP8X4), y_scales[:, cols], group[:].rearrange("p n r -> p (n r)")
            )

        gather(0)
        for c in range(CHUNKS):
            if c + 1 < CHUNKS:
                gather(c + 1)
            exponents(c)
            kernels(c)
        for s in range(CHUNKS, len(STAGES)):
            kernels(s)
        first_group, middle_group, last_group = (s1 for s0, s1 in GROUPS)
        early_words = y_groups[first_group][0]
        results(0)
        rounded(0)
        results(1)
        results(2)
        rounded(1)
        results(LAST - 1)
        quantised(first_group)
        nc.sync.dma_start(out_words[:, early_words], y_codes[:, early_words].bitcast(I32))
        rounded(2)
        rounded(LAST - 1)
        results(LAST)
        rounded(LAST)
        quantised(middle_group)
        quantised(last_group)

        nc.sync.dma_start(out_words[:, early_words.stop :], y_codes[:, early_words.stop :].bitcast(I32))
        for q in range(QUADS):
            queue = nc.scalar if q % 2 else nc.sync
            queue.dma_start(
                out_2[0, SCALE_ROWS * q : SCALE_ROWS * (q + 1), :].bitcast(I32),
                y_scales[QUAD * q : QUAD * q + SCALE_ROWS, :].bitcast(I32),
            )
